import numpy as np
import ml_dtypes


def mxq(x, axis, fmt="e4m3"):
    dtype, down = {"e4m3": (ml_dtypes.float8_e4m3fn, 7), "e5m2": (ml_dtypes.float8_e5m2, 14)}[fmt]
    v = np.moveaxis(np.asarray(x, np.float32).astype(ml_dtypes.bfloat16).astype(np.float64), axis, -1)
    blocks = v.reshape(v.shape[:-1] + (-1, 32))
    amax = np.abs(blocks).max(-1, keepdims=True)
    byte = np.maximum(np.where(amax > 0, np.frexp(amax)[1] - 1 + 127, 0) - down, 1)
    scale = np.exp2(byte - 127.0)
    codes = (blocks / scale).astype(np.float32).astype(dtype).astype(np.float64)
    return np.moveaxis((codes * scale).reshape(v.shape), -1, axis)


WIDE = False


def mx_kscale(k):
    if not WIDE:
        return np.ones(k)
    levels = np.array([10, -10, 5, -5, 0])
    if k % 512:
        return np.exp2(np.random.permutation(np.resize(levels, k // 32))).repeat(32)
    a = np.empty((k // 512, 16))
    for p in range(k // 512):
        a[p, :8] = np.random.permutation(np.resize(levels, 8))
        for g in range(8):
            far = levels[np.abs(levels - a[p, g]) >= 10]
            a[p, g + 8] = far[np.random.randint(len(far))]
    return np.exp2(a.ravel()).repeat(32)


def f64(x):
    return np.asarray(x).astype(np.float64)


def striped(idx):
    return np.tile(idx.reshape(-1, 16).T, (8, 1)).astype(np.uint16)


def unstriped(offs):
    return offs[:16].T.reshape(-1).astype(np.int64)


def striped8(idx):
    return np.concatenate([x.reshape(-1, 16).T for x in idx]).astype(np.uint16)


def runs(offs, k):
    lists = np.stack([offs[16 * r : 16 * r + 16].T.reshape(-1) for r in range(8)]).astype(np.int64)
    return lists[np.arange(k) % 512 // 64]


def pack_weight(w):
    k, n = w.shape
    w = f64(np.asarray(w, np.float32).astype(ml_dtypes.bfloat16)).reshape(k // 32, 32, n)
    amax = np.abs(w).max(1)
    byte = np.clip(np.where(amax > 0, np.frexp(amax)[1] - 1 + 127 - 7, 1), 1, 254)
    scaled = (w * np.exp2(127.0 - byte)[:, None, :]).reshape(k, n).astype(np.float32)
    words = np.ascontiguousarray(scaled.reshape(k // 512, 128, 4, n).transpose(0, 1, 3, 2)).astype(ml_dtypes.float8_e4m3fn).view(np.uint8)
    return words, np.ascontiguousarray(byte.astype(np.uint8).reshape(k // 512, 16, n))


def unpack_weight(words, scales):
    g, p, n, _ = words.shape
    vals = np.ascontiguousarray(words).view(ml_dtypes.float8_e4m3fn).astype(np.float64) * np.repeat(np.exp2(scales.astype(np.float64) - 127.0), 8, axis=1)[..., None]
    return vals.transpose(0, 1, 3, 2).reshape(g * 512, n)


K, T, S, V, N = 512, 2048, 512, 512, 512
P = 2 ** 7


def setup_inputs():
    n = np.random.standard_normal
    s = mx_kscale(K)[:, None]
    packed_xT = pack_weight(n((K, T)) * s)
    return {
        "x_words": packed_xT[0],
        "x_scales": packed_xT[1],
        "w1": (n((K, N)) / np.sqrt(K) / s).astype(np.float32),
        "w2": (n((K, N)) / np.sqrt(K) / s).astype(np.float32),
        "dn": np.tile(np.random.uniform(4.0, 9.0, S), (P, 1)).astype(np.float32),
        "qn": (0.5 * n((N, 1))).astype(np.float32),
        "offs": striped8(np.random.randint(0, T, (8, S))),
        "cent": striped(np.random.permutation(T)[:V]),
        "own": striped(np.random.randint(0, V, S)),
    }


def reference(x_words, x_scales, w1, w2, dn, qn, offs, cent, own):
    xq = unpack_weight(x_words, x_scales)[np.arange(K)[:, None], runs(offs, K)]
    x_cent = unpack_weight(x_words, x_scales)[:, unstriped(cent)]
    c = mxq(f64(w1), 0, "e4m3").T @ x_cent
    o = f64(dn)[:1] - (2.0 * ((mxq(f64(w2), 0, "e4m3").T @ xq) + c[:, unstriped(own)]))
    return o + f64(qn)

@@ -1,0 +1,151 @@
+from contextlib import ExitStack
+
+import concourse.mybir as mybir
+
+K, T, S, V, N = 512, 2048, 512, 512, 512
+FLOPS = 2 * K * N * (V + S)
+
+F32 = mybir.dt.float32
+BF16 = mybir.dt.bfloat16
+I32 = mybir.dt.int32
+U32 = mybir.dt.uint32
+U16 = mybir.dt.uint16
+U8 = mybir.dt.uint8
+FP8X4 = mybir.dt.float8_e4m3fn_x4
+ADD = mybir.AluOpType.add
+MULT = mybir.AluOpType.mult
+IDENTITY = mybir.ActivationFunctionType.Identity
+
+P = 128
+PACK = 4
+M_TILES = N // P
+SPARE = 16
+
+
+def tile_picked_ivfpq_none_p_kernel(tc, x_words, x_scales, w1, w2, dn, qn, offs, cent, own, out):
+    nc = tc.nc
+    with ExitStack() as ctx:
+        keep = ctx.enter_context(tc.tile_pool(name="keep", bufs=1))
+        psum = ctx.enter_context(tc.psum_pool(name="psum", bufs=1))
+
+        cent_list = keep.tile([P, V // 16], U16, name="cent_list")
+        offs_list = keep.tile([P, S // 16], U16, name="offs_list")
+        own_list = keep.tile([P, S // 16], U16, name="own_list")
+        nc.sync.dma_start(cent_list[:], cent)
+        nc.sync.dma_start(offs_list[:], offs)
+
+        scale_table = keep.tile([P, T], U8, name="scale_table", align_bytes=64)
+        scale_rows = x_scales[0].bitcast(I32)
+        for q in (0, 2, 1, 3):
+            nc.sync.dma_start(
+                out=scale_table[:].bitcast(I32)[32 * q : 32 * q + 32, :],
+                in_=scale_rows[4 * q : 4 * q + 4, :].unsqueeze(0).to_broadcast([8, 4, T // 4]),
+            )
+
+        def load_weight(w, m0, m1, name, tag):
+            raw = keep.tile([P, PACK, m1 - m0], F32, name=name, tag=tag, align_bytes=64)
+            nc.sync.dma_start(out=raw[:], in_=w[:, m0:m1].rearrange("(p j) m -> p j m", j=PACK))
+            return raw
+
+        def interleave(raw, name):
+            grouped = keep.tile([P, raw.shape[2], PACK], BF16, name=name, tag=name, align_bytes=64)
+            nc.scalar.copy(
+                out=grouped[:].rearrange("p (c i) j -> p c j i", i=4),
+                in_=raw[:].rearrange("p j (c i) -> p c j i", i=4),
+            )
+            return grouped
+
+        def quantize(grouped, name):
+            width = grouped.shape[1]
+            codes = keep.tile([P, width], U32, name=name + "_codes", align_bytes=64)
+            scales = keep.tile([P, width], U8, name=name + "_scales", align_bytes=64)
+            nc.vector.quantize_mx(out=codes[:].bitcast(FP8X4), scales=scales[:], in_=grouped[:].rearrange("p m j -> p (m j)"))
+            return codes, scales
+
+        w1_raw01 = load_weight(w1, 0, 2 * P, "w1_raw01", "w1_raw01")
+        word_table = keep.tile([P, T], I32, name="word_table", align_bytes=64)
+        nc.sync.dma_start(out=word_table[:], in_=x_words[0].rearrange("p n t -> p (n t)").bitcast(I32))
+        nc.sync.dma_start(own_list[:], own)
+        qn_cols = keep.tile([P, M_TILES], F32, name="qn_cols")
+        with nc.allow_non_contiguous_dma(reason="one query norm to a partition"):
+            nc.sync.dma_start(out=qn_cols[:], in_=qn.rearrange("(t p) o -> p (t o)", p=P))
+        w1_raw23 = load_weight(w1, 2 * P, N, "w1_raw23", "w1_raw23")
+        dn_rows = keep.tile([P, S], F32, name="dn_rows")
+        nc.sync.dma_start(out=dn_rows[:], in_=dn)
+        w2_raw01 = load_weight(w2, 0, 2 * P, "w2_raw01", "w2_raw01")
+        w2_raw23 = load_weight(w2, 2 * P, N, "w2_raw23", "w2_raw23")
+
+        warm = keep.tile([P, 8], F32, name="warm")
+        nc.gpsimd.memset(warm[:, 0:1], 0.0)
+        nc.scalar.activation(warm[:, 1:2], warm[:, 0:1], IDENTITY, bias=warm[:, 0:1], scale=-2.0)
+
+        offs_plane = keep.tile([P, S], U8, name="offs_plane", align_bytes=64)
+        nc.gpsimd.memset(offs_plane[:].bitcast(I32), 0)
+
+        cent_plane = keep.tile([P, V], U8, name="cent_plane", align_bytes=64)
+        offs_bytes = keep.tile([P, S], U8, name="offs_bytes", align_bytes=64)
+        nc.vector.tensor_copy(offs_bytes[:], scale_table[:].indirect(offs_list[:]))
+        nc.vector.tensor_copy(cent_plane[:], scale_table[:].indirect(cent_list[:]))
+        w1_grouped01 = interleave(w1_raw01, "w1_grouped01")
+        for i in range(4):
+            nc.scalar.dma_start(
+                out=offs_plane[:].bitcast(I32)[i:P:32, :],
+                in_=offs_bytes[:].bitcast(I32)[16 * (i // 2) + i : P : 32, :],
+            )
+        w1_q01 = quantize(w1_grouped01, "w1_q01")
+
+        cent_words = keep.tile([P, V], U32, name="cent_words", align_bytes=64)
+        offs_words = keep.tile([P, S], U32, name="offs_words", align_bytes=64)
+        nc.vector.tensor_copy(cent_words[:], word_table[:].bitcast(U32).indirect(cent_list[:]))
+        nc.vector.tensor_copy(offs_words[:], word_table[:].bitcast(U32).indirect(offs_list[:]))
+
+        def product(quantized, cols, words, plane, name):
+            codes, scales = quantized
+            bank = psum.tile([P, 512], F32, name=name)
+            nc.tensor.matmul_mx(
+                out=bank[:],
+                lhsT=codes[:, cols].bitcast(FP8X4),
+                lhsT_scale=scales[:, cols],
+                rhs=words[:].bitcast(FP8X4),
+                rhs_scale=plane[:],
+                start=True,
+                stop=True,
+            )
+            return bank
+
+        def centres(t, quantized, tag):
+            bank = product(quantized, slice(t % 2 * P, (t % 2 + 1) * P), cent_words, cent_plane, f"c_bank{t}")
+            rows = keep.tile([P, V + SPARE], F32, name=f"c_rows{t}", tag=tag, align_bytes=64)
+            nc.gpsimd.memset(rows[:, V:], 0.0)
+            nc.scalar.activation(rows[:, :V], bank[:], IDENTITY, bias=qn_cols[:, t : t + 1], scale=-2.0)
+            return rows
+
+        def look_up(t, rows, tag):
+            part = keep.tile([P, S], F32, name=f"part{t}", tag=tag, align_bytes=64)
+            nc.vector.tensor_tensor(part[:], rows[:].indirect(own_list[:]), dn_rows[:], ADD)
+            return part
+
+        def finish(t, quantized, part, pieces):
+            bank = product(quantized, slice(t % 2 * P, (t % 2 + 1) * P), offs_words, offs_plane, f"r_bank{t}")
+            step = S // pieces
+            for h in range(pieces):
+                cols = slice(h * step, (h + 1) * step)
+                result = keep.tile([P, step], F32, name=f"result{t}_{h}")
+                nc.vector.scalar_tensor_tensor(result[:], bank[:, cols], -2.0, part[:, cols], MULT, ADD)
+                nc.sync.dma_start(out=out[t * P : (t + 1) * P, cols], in_=result[:])
+
+        w1_q23 = quantize(interleave(w1_raw23, "w1_grouped23"), "w1_q23")
+        c_rows0 = centres(0, w1_q01, "w1_raw23")
+        c_rows1 = centres(1, w1_q01, "w1_grouped23")
+        part0 = look_up(0, c_rows0, "part0")
+        part1 = look_up(1, c_rows1, "part1")
+        w2_q01 = quantize(interleave(w2_raw01, "w2_grouped01"), "w2_q01")
+        c_rows2 = centres(2, w1_q23, "c_rows2")
+        c_rows3 = centres(3, w1_q23, "c_rows3")
+        part2 = look_up(2, c_rows2, "part2")
+        finish(0, w2_q01, part0, 1)
+        finish(1, w2_q01, part1, 1)
+        w2_q23 = quantize(interleave(w2_raw23, "w2_grouped23"), "w2_q23")
+        part3 = look_up(3, c_rows3, "w2_grouped23")
+        finish(2, w2_q23, part2, 1)
+        finish(3, w2_q23, part3, 2)

@@ -1,6 +1,7 @@
 from contextlib import ExitStack
 
 import concourse.mybir as mybir
+from concourse.masks import make_identity
 
 K, T, S, V, N = 512, 2048, 512, 512, 512
 FLOPS = 2 * K * N * (V + S)
@@ -31,7 +32,6 @@ def tile_picked_ivfpq_none_p_kernel(tc, x_words, x_scales, w1, w2, dn, qn, offs,
         cent_list = keep.tile([P, V // 16], U16, name="cent_list")
         offs_list = keep.tile([P, S // 16], U16, name="offs_list")
         own_list = keep.tile([P, S // 16], U16, name="own_list")
-        nc.sync.dma_start(cent_list[:], cent)
         nc.sync.dma_start(offs_list[:], offs)
 
         scale_table = keep.tile([P, T], U8, name="scale_table", align_bytes=64)
@@ -41,6 +41,8 @@ def tile_picked_ivfpq_none_p_kernel(tc, x_words, x_scales, w1, w2, dn, qn, offs,
                 out=scale_table[:].bitcast(I32)[32 * q : 32 * q + 32, :],
                 in_=scale_rows[4 * q : 4 * q + 4, :].unsqueeze(0).to_broadcast([8, 4, T // 4]),
             )
+
+        nc.sync.dma_start(cent_list[:], cent)
 
         def load_weight(w, m0, m1, name, tag):
             raw = keep.tile([P, PACK, m1 - m0], F32, name=name, tag=tag, align_bytes=64)
@@ -62,13 +64,14 @@ def tile_picked_ivfpq_none_p_kernel(tc, x_words, x_scales, w1, w2, dn, qn, offs,
             nc.vector.quantize_mx(out=codes[:].bitcast(FP8X4), scales=scales[:], in_=grouped[:].rearrange("p m j -> p (m j)"))
             return codes, scales
 
-        w1_raw01 = load_weight(w1, 0, 2 * P, "w1_raw01", "w1_raw01")
+        w1_raw0 = load_weight(w1, 0, P, "w1_raw0", "w1_raw0")
         word_table = keep.tile([P, T], I32, name="word_table", align_bytes=64)
         nc.sync.dma_start(out=word_table[:], in_=x_words[0].rearrange("p n t -> p (n t)").bitcast(I32))
         nc.sync.dma_start(own_list[:], own)
-        qn_cols = keep.tile([P, M_TILES], F32, name="qn_cols")
-        with nc.allow_non_contiguous_dma(reason="one query norm to a partition"):
-            nc.sync.dma_start(out=qn_cols[:], in_=qn.rearrange("(t p) o -> p (t o)", p=P))
+        qn_rows = keep.tile([P, P], F32, name="qn_rows")
+        nc.gpsimd.memset(qn_rows[:], 0.0)
+        nc.sync.dma_start(out=qn_rows[:M_TILES, :], in_=qn.rearrange("(t p) o -> t (p o)", p=P))
+        w1_raw1 = load_weight(w1, P, 2 * P, "w1_raw1", "w1_raw1")
         w1_raw23 = load_weight(w1, 2 * P, N, "w1_raw23", "w1_raw23")
         dn_rows = keep.tile([P, S], F32, name="dn_rows")
         nc.sync.dma_start(out=dn_rows[:], in_=dn)
@@ -79,6 +82,11 @@ def tile_picked_ivfpq_none_p_kernel(tc, x_words, x_scales, w1, w2, dn, qn, offs,
         nc.gpsimd.memset(warm[:, 0:1], 0.0)
         nc.scalar.activation(warm[:, 1:2], warm[:, 0:1], IDENTITY, bias=warm[:, 0:1], scale=-2.0)
 
+        identity = keep.tile([P, P], F32, name="identity")
+        make_identity(nc, identity[:])
+        qn_bank = psum.tile([P, P], F32, name="qn_bank", tag="r_bank3")
+        nc.tensor.transpose(qn_bank[:], qn_rows[:], identity[:])
+
         offs_plane = keep.tile([P, S], U8, name="offs_plane", align_bytes=64)
         nc.gpsimd.memset(offs_plane[:].bitcast(I32), 0)
 
@@ -86,22 +94,22 @@ def tile_picked_ivfpq_none_p_kernel(tc, x_words, x_scales, w1, w2, dn, qn, offs,
         offs_bytes = keep.tile([P, S], U8, name="offs_bytes", align_bytes=64)
         nc.vector.tensor_copy(offs_bytes[:], scale_table[:].indirect(offs_list[:]))
         nc.vector.tensor_copy(cent_plane[:], scale_table[:].indirect(cent_list[:]))
-        w1_grouped01 = interleave(w1_raw01, "w1_grouped01")
         for i in range(4):
-            nc.scalar.dma_start(
+            nc.sync.dma_start(
                 out=offs_plane[:].bitcast(I32)[i:P:32, :],
                 in_=offs_bytes[:].bitcast(I32)[16 * (i // 2) + i : P : 32, :],
             )
-        w1_q01 = quantize(w1_grouped01, "w1_q01")
 
+        w1_q0 = quantize(interleave(w1_raw0, "w1_grouped0"), "w1_q0")
         cent_words = keep.tile([P, V], U32, name="cent_words", align_bytes=64)
-        offs_words = keep.tile([P, S], U32, name="offs_words", align_bytes=64)
         nc.vector.tensor_copy(cent_words[:], word_table[:].bitcast(U32).indirect(cent_list[:]))
+        w1_q1 = quantize(interleave(w1_raw1, "w1_grouped1"), "w1_q1")
+        offs_words = keep.tile([P, S], U32, name="offs_words", tag="w1_grouped1", align_bytes=64)
         nc.vector.tensor_copy(offs_words[:], word_table[:].bitcast(U32).indirect(offs_list[:]))
 
         def product(quantized, cols, words, plane, name):
             codes, scales = quantized
-            bank = psum.tile([P, 512], F32, name=name)
+            bank = psum.tile([P, 512], F32, name=name, tag=name)
             nc.tensor.matmul_mx(
                 out=bank[:],
                 lhsT=codes[:, cols].bitcast(FP8X4),
@@ -113,8 +121,8 @@ def tile_picked_ivfpq_none_p_kernel(tc, x_words, x_scales, w1, w2, dn, qn, offs,
             )
             return bank
 
-        def centres(t, quantized, tag):
-            bank = product(quantized, slice(t % 2 * P, (t % 2 + 1) * P), cent_words, cent_plane, f"c_bank{t}")
+        def centres(t, quantized, cols, tag):
+            bank = product(quantized, cols, cent_words, cent_plane, f"c_bank{t}")
             rows = keep.tile([P, V + SPARE], F32, name=f"c_rows{t}", tag=tag, align_bytes=64)
             nc.gpsimd.memset(rows[:, V:], 0.0)
             nc.scalar.activation(rows[:, :V], bank[:], IDENTITY, bias=qn_cols[:, t : t + 1], scale=-2.0)
@@ -125,27 +133,29 @@ def tile_picked_ivfpq_none_p_kernel(tc, x_words, x_scales, w1, w2, dn, qn, offs,
             nc.vector.tensor_tensor(part[:], rows[:].indirect(own_list[:]), dn_rows[:], ADD)
             return part
 
-        def finish(t, quantized, part, pieces):
+        def finish(t, quantized, part, pieces, tag):
             bank = product(quantized, slice(t % 2 * P, (t % 2 + 1) * P), offs_words, offs_plane, f"r_bank{t}")
             step = S // pieces
             for h in range(pieces):
                 cols = slice(h * step, (h + 1) * step)
-                result = keep.tile([P, step], F32, name=f"result{t}_{h}")
+                result = keep.tile([P, step], F32, name=f"result{t}_{h}", tag=f"{tag}{h}", align_bytes=64)
                 nc.vector.scalar_tensor_tensor(result[:], bank[:, cols], -2.0, part[:, cols], MULT, ADD)
                 nc.sync.dma_start(out=out[t * P : (t + 1) * P, cols], in_=result[:])
 
         w1_q23 = quantize(interleave(w1_raw23, "w1_grouped23"), "w1_q23")
-        c_rows0 = centres(0, w1_q01, "w1_raw23")
-        c_rows1 = centres(1, w1_q01, "w1_grouped23")
+        qn_cols = keep.tile([P, M_TILES], F32, name="qn_cols", tag="w1_raw23", align_bytes=64)
+        nc.scalar.copy(qn_cols[:], qn_bank[:, :M_TILES])
+        c_rows0 = centres(0, w1_q0, slice(0, P), "c_rows0")
+        c_rows1 = centres(1, w1_q1, slice(0, P), "c_rows1")
         part0 = look_up(0, c_rows0, "part0")
         part1 = look_up(1, c_rows1, "part1")
         w2_q01 = quantize(interleave(w2_raw01, "w2_grouped01"), "w2_q01")
-        c_rows2 = centres(2, w1_q23, "c_rows2")
-        c_rows3 = centres(3, w1_q23, "c_rows3")
+        c_rows2 = centres(2, w1_q23, slice(0, P), "c_rows2")
+        c_rows3 = centres(3, w1_q23, slice(P, 2 * P), "c_rows3")
         part2 = look_up(2, c_rows2, "part2")
-        finish(0, w2_q01, part0, 1)
-        finish(1, w2_q01, part1, 1)
+        finish(0, w2_q01, part0, 1, "first")
+        finish(1, w2_q01, part1, 1, "second")
         w2_q23 = quantize(interleave(w2_raw23, "w2_grouped23"), "w2_q23")
         part3 = look_up(3, c_rows3, "w2_grouped23")
-        finish(2, w2_q23, part2, 1)
-        finish(3, w2_q23, part3, 2)
+        finish(2, w2_q23, part2, 1, "third")
+        finish(3, w2_q23, part3, 2, "fourth")

@@ -14,7 +14,6 @@ U16 = mybir.dt.uint16
 U8 = mybir.dt.uint8
 FP8X4 = mybir.dt.float8_e4m3fn_x4
 ADD = mybir.AluOpType.add
-MULT = mybir.AluOpType.mult
 IDENTITY = mybir.ActivationFunctionType.Identity
 
 P = 128
@@ -27,13 +26,14 @@ def tile_picked_ivfpq_none_p_kernel(tc, x_words, x_scales, w1, w2, dn, qn, offs,
     nc = tc.nc
     with ExitStack() as ctx:
         keep = ctx.enter_context(tc.tile_pool(name="keep", bufs=1))
+        reused = ctx.enter_context(tc.tile_pool(name="reused", bufs=1))
         psum = ctx.enter_context(tc.psum_pool(name="psum", bufs=1))
 
         cent_list = keep.tile([P, V // 16], U16, name="cent_list")
         offs_list = keep.tile([P, S // 16], U16, name="offs_list")
         own_list = keep.tile([P, S // 16], U16, name="own_list")
-        nc.sync.dma_start(offs_list[:], offs)
 
+        nc.sync.dma_start(cent_list[:], cent)
         scale_table = keep.tile([P, T], U8, name="scale_table", align_bytes=64)
         scale_rows = x_scales[0].bitcast(I32)
         for q in (0, 2, 1, 3):
@@ -41,46 +41,45 @@ def tile_picked_ivfpq_none_p_kernel(tc, x_words, x_scales, w1, w2, dn, qn, offs,
                 out=scale_table[:].bitcast(I32)[32 * q : 32 * q + 32, :],
                 in_=scale_rows[4 * q : 4 * q + 4, :].unsqueeze(0).to_broadcast([8, 4, T // 4]),
             )
+        nc.sync.dma_start(offs_list[:], offs)
 
-        nc.sync.dma_start(cent_list[:], cent)
-
-        def load_weight(w, m0, m1, name, tag):
-            raw = keep.tile([P, PACK, m1 - m0], F32, name=name, tag=tag, align_bytes=64)
+        def load_weight(w, m0, m1, name):
+            raw = keep.tile([P, PACK, m1 - m0], F32, name=name, tag=name, align_bytes=64)
             nc.sync.dma_start(out=raw[:], in_=w[:, m0:m1].rearrange("(p j) m -> p j m", j=PACK))
             return raw
 
-        def interleave(raw, name):
-            grouped = keep.tile([P, raw.shape[2], PACK], BF16, name=name, tag=name, align_bytes=64)
-            nc.scalar.copy(
-                out=grouped[:].rearrange("p (c i) j -> p c j i", i=4),
-                in_=raw[:].rearrange("p j (c i) -> p c j i", i=4),
+        def interleave(raw, m0, m1, name, tag):
+            grouped = keep.tile([P, m1 - m0, PACK], BF16, name=name, tag=tag, align_bytes=64)
+            nc.scalar.activation(
+                grouped[:].rearrange("p (c i) j -> p c j i", i=4),
+                raw[:, :, m0:m1].rearrange("p j (c i) -> p c j i", i=4),
+                IDENTITY,
+                scale=-2.0,
             )
             return grouped
 
-        def quantize(grouped, name):
+        def quantize(grouped, name, tag=None):
             width = grouped.shape[1]
-            codes = keep.tile([P, width], U32, name=name + "_codes", align_bytes=64)
-            scales = keep.tile([P, width], U8, name=name + "_scales", align_bytes=64)
+            codes = keep.tile([P, width], U32, name=name + "_codes", tag=tag or name + "_codes", align_bytes=64)
+            scales = keep.tile([P, width], U8, name=name + "_scales", tag=name + "_scales", align_bytes=64)
             nc.vector.quantize_mx(out=codes[:].bitcast(FP8X4), scales=scales[:], in_=grouped[:].rearrange("p m j -> p (m j)"))
             return codes, scales
 
-        w1_raw0 = load_weight(w1, 0, P, "w1_raw0", "w1_raw0")
         word_table = keep.tile([P, T], I32, name="word_table", align_bytes=64)
         nc.sync.dma_start(out=word_table[:], in_=x_words[0].rearrange("p n t -> p (n t)").bitcast(I32))
-        nc.sync.dma_start(own_list[:], own)
+        w1_raw0 = load_weight(w1, 0, P, "w1_raw0")
         qn_rows = keep.tile([P, P], F32, name="qn_rows")
         nc.gpsimd.memset(qn_rows[:], 0.0)
         nc.sync.dma_start(out=qn_rows[:M_TILES, :], in_=qn.rearrange("(t p) o -> t (p o)", p=P))
-        w1_raw1 = load_weight(w1, P, 2 * P, "w1_raw1", "w1_raw1")
-        w1_raw23 = load_weight(w1, 2 * P, N, "w1_raw23", "w1_raw23")
+        w1_raw1 = load_weight(w1, P, 2 * P, "w1_raw1")
+        w1_raw2 = load_weight(w1, 2 * P, 3 * P, "w1_raw2")
+        w1_raw3 = load_weight(w1, 3 * P, N, "w1_raw3")
+        nc.sync.dma_start(own_list[:], own)
         dn_rows = keep.tile([P, S], F32, name="dn_rows")
         nc.sync.dma_start(out=dn_rows[:], in_=dn)
-        w2_raw01 = load_weight(w2, 0, 2 * P, "w2_raw01", "w2_raw01")
-        w2_raw23 = load_weight(w2, 2 * P, N, "w2_raw23", "w2_raw23")
-
-        warm = keep.tile([P, 8], F32, name="warm")
-        nc.gpsimd.memset(warm[:, 0:1], 0.0)
-        nc.scalar.activation(warm[:, 1:2], warm[:, 0:1], IDENTITY, bias=warm[:, 0:1], scale=-2.0)
+        w2_raw01 = load_weight(w2, 0, 2 * P, "w2_raw01")
+        w2_raw23 = reused.tile([P, PACK, 2 * P], F32, name="w2_raw23", offset=0)
+        nc.sync.dma_start(out=w2_raw23[:], in_=w2[:, 2 * P :].rearrange("(p j) m -> p j m", j=PACK))
 
         identity = keep.tile([P, P], F32, name="identity")
         make_identity(nc, identity[:])
@@ -92,24 +91,27 @@ def tile_picked_ivfpq_none_p_kernel(tc, x_words, x_scales, w1, w2, dn, qn, offs,
 
         cent_plane = keep.tile([P, V], U8, name="cent_plane", align_bytes=64)
         offs_bytes = keep.tile([P, S], U8, name="offs_bytes", align_bytes=64)
-        nc.vector.tensor_copy(offs_bytes[:], scale_table[:].indirect(offs_list[:]))
         nc.vector.tensor_copy(cent_plane[:], scale_table[:].indirect(cent_list[:]))
+        nc.vector.tensor_copy(offs_bytes[:], scale_table[:].indirect(offs_list[:]))
         for i in range(4):
             nc.sync.dma_start(
                 out=offs_plane[:].bitcast(I32)[i:P:32, :],
                 in_=offs_bytes[:].bitcast(I32)[16 * (i // 2) + i : P : 32, :],
             )
 
-        w1_q0 = quantize(interleave(w1_raw0, "w1_grouped0"), "w1_q0")
         cent_words = keep.tile([P, V], U32, name="cent_words", align_bytes=64)
         nc.vector.tensor_copy(cent_words[:], word_table[:].bitcast(U32).indirect(cent_list[:]))
-        w1_q1 = quantize(interleave(w1_raw1, "w1_grouped1"), "w1_q1")
-        offs_words = keep.tile([P, S], U32, name="offs_words", tag="w1_grouped1", align_bytes=64)
+        w1_q0 = quantize(interleave(w1_raw0, 0, P, "w1_grouped0", "w1_grouped0"), "w1_q0")
+        offs_words = keep.tile([P, S], U32, name="offs_words", tag="w1_raw0", align_bytes=64)
         nc.vector.tensor_copy(offs_words[:], word_table[:].bitcast(U32).indirect(offs_list[:]))
+        w1_q1 = quantize(interleave(w1_raw1, 0, P, "w1_grouped1", "w1_grouped1"), "w1_q1")
+        w1_q2 = quantize(interleave(w1_raw2, 0, P, "w1_grouped2", "w1_grouped2"), "w1_q2")
+        qn_cols = keep.tile([P, M_TILES], F32, name="qn_cols", align_bytes=64)
+        nc.scalar.copy(qn_cols[:], qn_bank[:, :M_TILES])
 
-        def product(quantized, cols, words, plane, name):
+        def product(quantized, cols, words, plane, name, tag):
             codes, scales = quantized
-            bank = psum.tile([P, 512], F32, name=name, tag=name)
+            bank = psum.tile([P, 512], F32, name=name, tag=tag)
             nc.tensor.matmul_mx(
                 out=bank[:],
                 lhsT=codes[:, cols].bitcast(FP8X4),
@@ -122,40 +124,57 @@ def tile_picked_ivfpq_none_p_kernel(tc, x_words, x_scales, w1, w2, dn, qn, offs,
             return bank
 
         def centres(t, quantized, cols, tag):
-            bank = product(quantized, cols, cent_words, cent_plane, f"c_bank{t}")
+            bank = product(quantized, cols, cent_words, cent_plane, f"c_bank{t}", f"c_bank{t}")
             rows = keep.tile([P, V + SPARE], F32, name=f"c_rows{t}", tag=tag, align_bytes=64)
             nc.gpsimd.memset(rows[:, V:], 0.0)
-            nc.scalar.activation(rows[:, :V], bank[:], IDENTITY, bias=qn_cols[:, t : t + 1], scale=-2.0)
+            nc.scalar.copy(rows[:, :V], bank[:])
             return rows
 
-        def look_up(t, rows, tag):
-            part = keep.tile([P, S], F32, name=f"part{t}", tag=tag, align_bytes=64)
-            nc.vector.tensor_tensor(part[:], rows[:].indirect(own_list[:]), dn_rows[:], ADD)
+        def look_up(rows, j0, j1, name, tag):
+            part = keep.tile([P, j1 - j0], F32, name=name, tag=tag, align_bytes=64)
+            nc.vector.tensor_tensor(part[:], rows[:].indirect(own_list[:, j0 // 16 : j1 // 16]), dn_rows[:, j0:j1], ADD)
             return part
 
-        def finish(t, quantized, part, pieces, tag):
-            bank = product(quantized, slice(t % 2 * P, (t % 2 + 1) * P), offs_words, offs_plane, f"r_bank{t}")
-            step = S // pieces
-            for h in range(pieces):
-                cols = slice(h * step, (h + 1) * step)
-                result = keep.tile([P, step], F32, name=f"result{t}_{h}", tag=f"{tag}{h}", align_bytes=64)
-                nc.vector.scalar_tensor_tensor(result[:], bank[:, cols], -2.0, part[:, cols], MULT, ADD)
-                nc.sync.dma_start(out=out[t * P : (t + 1) * P, cols], in_=result[:])
+        def finish(t, bank, part, j0, j1):
+            if t < 2:
+                result = reused.tile([P, j1 - j0], F32, name=f"result{t}", offset=t * S * 4)
+            else:
+                result = keep.tile([P, j1 - j0], F32, name=f"result{t}_{j0}", align_bytes=64)
+            nc.vector.scalar_tensor_tensor(result[:], bank[:, j0:j1], qn_cols[:, t : t + 1], part[:], ADD, ADD)
+            nc.sync.dma_start(out=out[t * P : (t + 1) * P, j0:j1], in_=result[:])
 
-        w1_q23 = quantize(interleave(w1_raw23, "w1_grouped23"), "w1_q23")
-        qn_cols = keep.tile([P, M_TILES], F32, name="qn_cols", tag="w1_raw23", align_bytes=64)
-        nc.scalar.copy(qn_cols[:], qn_bank[:, :M_TILES])
-        c_rows0 = centres(0, w1_q0, slice(0, P), "c_rows0")
+        def rests(t, quantized):
+            return product(quantized, slice(t % 2 * P, (t % 2 + 1) * P), offs_words, offs_plane, f"r_bank{t}", f"r_bank{t}")
+
+        c_rows0 = keep.tile([P, V + SPARE], F32, name="c_rows0", align_bytes=64)
+        nc.gpsimd.memset(c_rows0[:, V:], 0.0)
+        for h, tag in enumerate(("c_bank0", "r_bank2")):
+            cols = slice(h * V // 2, (h + 1) * V // 2)
+            bank = psum.tile([P, V // 2], F32, name=f"c_half{h}", tag=tag)
+            nc.tensor.matmul_mx(
+                out=bank[:],
+                lhsT=w1_q0[0][:].bitcast(FP8X4),
+                lhsT_scale=w1_q0[1][:],
+                rhs=cent_words[:, cols].bitcast(FP8X4),
+                rhs_scale=cent_plane[:, cols],
+                start=True,
+                stop=True,
+            )
+            nc.scalar.copy(c_rows0[:, cols], bank[:])
+        part0 = look_up(c_rows0, 0, S, "part0", "part0")
+        w1_q3 = quantize(interleave(w1_raw3, 0, P, "w1_grouped3", "w1_q0_codes"), "w1_q3")
         c_rows1 = centres(1, w1_q1, slice(0, P), "c_rows1")
-        part0 = look_up(0, c_rows0, "part0")
-        part1 = look_up(1, c_rows1, "part1")
-        w2_q01 = quantize(interleave(w2_raw01, "w2_grouped01"), "w2_q01")
-        c_rows2 = centres(2, w1_q23, slice(0, P), "c_rows2")
-        c_rows3 = centres(3, w1_q23, slice(P, 2 * P), "c_rows3")
-        part2 = look_up(2, c_rows2, "part2")
-        finish(0, w2_q01, part0, 1, "first")
-        finish(1, w2_q01, part1, 1, "second")
-        w2_q23 = quantize(interleave(w2_raw23, "w2_grouped23"), "w2_q23")
-        part3 = look_up(3, c_rows3, "w2_grouped23")
-        finish(2, w2_q23, part2, 1, "third")
-        finish(3, w2_q23, part3, 2, "fourth")
+        part1 = look_up(c_rows1, 0, S, "part1", "part1")
+        c_rows2 = centres(2, w1_q2, slice(0, P), "c_rows2")
+        part2 = look_up(c_rows2, 0, S, "part2", "part2")
+        w2_q01 = quantize(interleave(w2_raw01, 0, 2 * P, "w2_grouped01", "w1_q2_codes"), "w2_q01")
+        c_rows3 = centres(3, w1_q3, slice(0, P), "c_rows3")
+        part3a = look_up(c_rows3, 0, S // 2, "part3a", "w2_raw01")
+        w2_q23 = quantize(interleave(w2_raw23, 0, 2 * P, "w2_grouped23", "w1_q3_codes"), "w2_q23")
+        finish(0, rests(0, w2_q01), part0, 0, S)
+        finish(1, rests(1, w2_q01), part1, 0, S)
+        finish(2, rests(2, w2_q23), part2, 0, S)
+        r_bank3 = rests(3, w2_q23)
+        part3b = look_up(c_rows3, S // 2, S, "part3b", "w2_q23_scales")
+        finish(3, r_bank3, part3a, 0, S // 2)
+        finish(3, r_bank3, part3b, S // 2, S)

@@ -77,9 +77,9 @@ def tile_picked_ivfpq_none_p_kernel(tc, x_words, x_scales, w1, w2, dn, qn, offs,
         nc.sync.dma_start(own_list[:], own)
         dn_rows = keep.tile([P, S], F32, name="dn_rows")
         nc.sync.dma_start(out=dn_rows[:], in_=dn)
-        w2_raw01 = load_weight(w2, 0, 2 * P, "w2_raw01")
-        w2_raw23 = reused.tile([P, PACK, 2 * P], F32, name="w2_raw23", offset=0)
-        nc.sync.dma_start(out=w2_raw23[:], in_=w2[:, 2 * P :].rearrange("(p j) m -> p j m", j=PACK))
+        w2_raw23 = load_weight(w2, 2 * P, N, "w2_raw23")
+        w2_raw01 = reused.tile([P, PACK, 2 * P], F32, name="w2_raw01", offset=0, align_bytes=64)
+        nc.sync.dma_start(out=w2_raw01[:], in_=w2[:, : 2 * P].rearrange("(p j) m -> p j m", j=PACK))
 
         identity = keep.tile([P, P], F32, name="identity")
         make_identity(nc, identity[:])
@@ -105,7 +105,7 @@ def tile_picked_ivfpq_none_p_kernel(tc, x_words, x_scales, w1, w2, dn, qn, offs,
         offs_words = keep.tile([P, S], U32, name="offs_words", tag="w1_raw0", align_bytes=64)
         nc.vector.tensor_copy(offs_words[:], word_table[:].bitcast(U32).indirect(offs_list[:]))
         w1_q1 = quantize(interleave(w1_raw1, 0, P, "w1_grouped1", "w1_grouped1"), "w1_q1")
-        w1_q2 = quantize(interleave(w1_raw2, 0, P, "w1_grouped2", "w1_grouped2"), "w1_q2")
+        w1_grouped2 = interleave(w1_raw2, 0, P, "w1_grouped2", "w1_grouped2")
         qn_cols = keep.tile([P, M_TILES], F32, name="qn_cols", align_bytes=64)
         nc.scalar.copy(qn_cols[:], qn_bank[:, :M_TILES])
 
@@ -124,22 +124,22 @@ def tile_picked_ivfpq_none_p_kernel(tc, x_words, x_scales, w1, w2, dn, qn, offs,
             return bank
 
         def centres(t, quantized, cols, tag):
-            bank = product(quantized, cols, cent_words, cent_plane, f"c_bank{t}", f"c_bank{t}")
+            bank = product(quantized, cols, cent_words, cent_plane, f"c_bank{t}", "c_bank1")
             rows = keep.tile([P, V + SPARE], F32, name=f"c_rows{t}", tag=tag, align_bytes=64)
             nc.gpsimd.memset(rows[:, V:], 0.0)
             nc.scalar.copy(rows[:, :V], bank[:])
             return rows
 
-        def look_up(rows, j0, j1, name, tag):
+        def look_up(rows, added, j0, j1, name, tag):
             part = keep.tile([P, j1 - j0], F32, name=name, tag=tag, align_bytes=64)
-            nc.vector.tensor_tensor(part[:], rows[:].indirect(own_list[:, j0 // 16 : j1 // 16]), dn_rows[:, j0:j1], ADD)
+            nc.vector.tensor_tensor(part[:], rows[:].indirect(own_list[:, j0 // 16 : j1 // 16]), added[:, j0:j1], ADD)
             return part
 
-        def finish(t, bank, part, j0, j1):
-            if t < 2:
-                result = reused.tile([P, j1 - j0], F32, name=f"result{t}", offset=t * S * 4)
+        def finish(t, bank, part, j0, j1, tag):
+            if t == 2:
+                result = reused.tile([P, S], F32, name="result2", offset=S * 4, align_bytes=64)
             else:
-                result = keep.tile([P, j1 - j0], F32, name=f"result{t}_{j0}", align_bytes=64)
+                result = keep.tile([P, j1 - j0], F32, name=f"result{t}_{j0}", tag=tag, align_bytes=64)
             nc.vector.scalar_tensor_tensor(result[:], bank[:, j0:j1], qn_cols[:, t : t + 1], part[:], ADD, ADD)
             nc.sync.dma_start(out=out[t * P : (t + 1) * P, j0:j1], in_=result[:])
 
@@ -160,21 +160,30 @@ def tile_picked_ivfpq_none_p_kernel(tc, x_words, x_scales, w1, w2, dn, qn, offs,
                 start=True,
                 stop=True,
             )
-            nc.scalar.copy(c_rows0[:, cols], bank[:])
-        part0 = look_up(c_rows0, 0, S, "part0", "part0")
+            if h == 0:
+                nc.scalar.copy(c_rows0[:, cols], bank[:])
+            else:
+                nc.vector.tensor_copy(c_rows0[:, cols], bank[:])
+        w1_q2 = quantize(w1_grouped2, "w1_q2", "w1_grouped1")
+        part0 = look_up(c_rows0, dn_rows, 0, S, "part0", "part0")
         w1_q3 = quantize(interleave(w1_raw3, 0, P, "w1_grouped3", "w1_q0_codes"), "w1_q3")
         c_rows1 = centres(1, w1_q1, slice(0, P), "c_rows1")
-        part1 = look_up(c_rows1, 0, S, "part1", "part1")
+        part1 = look_up(c_rows1, dn_rows, 0, S, "part1", "part1")
+        w2_q23 = quantize(interleave(w2_raw23, 0, 2 * P, "w2_grouped23", "w1_q1_codes"), "w2_q23")
         c_rows2 = centres(2, w1_q2, slice(0, P), "c_rows2")
-        part2 = look_up(c_rows2, 0, S, "part2", "part2")
-        w2_q01 = quantize(interleave(w2_raw01, 0, 2 * P, "w2_grouped01", "w1_q2_codes"), "w2_q01")
-        c_rows3 = centres(3, w1_q3, slice(0, P), "c_rows3")
-        part3a = look_up(c_rows3, 0, S // 2, "part3a", "w2_raw01")
-        w2_q23 = quantize(interleave(w2_raw23, 0, 2 * P, "w2_grouped23", "w1_q3_codes"), "w2_q23")
-        finish(0, rests(0, w2_q01), part0, 0, S)
-        finish(1, rests(1, w2_q01), part1, 0, S)
-        finish(2, rests(2, w2_q23), part2, 0, S)
+        part2 = look_up(c_rows2, dn_rows, 0, S, "part2", "part2")
         r_bank3 = rests(3, w2_q23)
-        part3b = look_up(c_rows3, S // 2, S, "part3b", "w2_q23_scales")
-        finish(3, r_bank3, part3a, 0, S // 2)
-        finish(3, r_bank3, part3b, S // 2, S)
+        w2_grouped01 = interleave(w2_raw01, 0, 2 * P, "w2_grouped01", "w1_q2_codes")
+        w2_q01 = quantize(w2_grouped01, "w2_q01")
+        r_rows3 = keep.tile([P, S], F32, name="r_rows3", align_bytes=64)
+        nc.scalar.activation(r_rows3[:], r_bank3[:], IDENTITY, bias=qn_cols[:, 3:4])
+        r_dn3 = keep.tile([P, S], F32, name="r_dn3", tag="w1_q2_codes", align_bytes=64)
+        nc.gpsimd.tensor_tensor(r_dn3[:], r_rows3[:], dn_rows[:], ADD)
+        c_rows3 = centres(3, w1_q3, slice(0, P), "c_rows3")
+        finish(2, rests(2, w2_q23), part2, 0, S, "w2_raw01")
+        finish(0, rests(0, w2_q01), part0, 0, S, "result0")
+        finish(1, rests(1, w2_q01), part1, 0, S, "result1")
+        for h, tag in enumerate(("w2_q01_codes", "w2_q01_scales")):
+            j0, j1 = h * S // 2, (h + 1) * S // 2
+            result = look_up(c_rows3, r_dn3, j0, j1, f"result3_{h}", tag)
+            nc.sync.dma_start(out=out[3 * P :, j0:j1], in_=result[:])

@@ -73,13 +73,15 @@ def tile_picked_ivfpq_none_p_kernel(tc, x_words, x_scales, w1, w2, dn, qn, offs,
         nc.sync.dma_start(out=qn_rows[:M_TILES, :], in_=qn.rearrange("(t p) o -> t (p o)", p=P))
         w1_raw1 = load_weight(w1, P, 2 * P, "w1_raw1")
         w1_raw2 = load_weight(w1, 2 * P, 3 * P, "w1_raw2")
-        w1_raw3 = load_weight(w1, 3 * P, N, "w1_raw3")
         nc.sync.dma_start(own_list[:], own)
+        w2_raw3 = load_weight(w2, 3 * P, N, "w2_raw3")
         dn_rows = keep.tile([P, S], F32, name="dn_rows")
         nc.sync.dma_start(out=dn_rows[:], in_=dn)
-        w2_raw23 = load_weight(w2, 2 * P, N, "w2_raw23")
-        w2_raw01 = reused.tile([P, PACK, 2 * P], F32, name="w2_raw01", offset=0, align_bytes=64)
-        nc.sync.dma_start(out=w2_raw01[:], in_=w2[:, : 2 * P].rearrange("(p j) m -> p j m", j=PACK))
+        w2_raw2 = load_weight(w2, 2 * P, 3 * P, "w2_raw2")
+        w1_raw3 = load_weight(w1, 3 * P, N, "w1_raw3")
+        w2_raw0 = load_weight(w2, 0, P, "w2_raw0")
+        w2_raw1 = reused.tile([P, PACK, P], F32, name="w2_raw1", offset=0, align_bytes=64)
+        nc.sync.dma_start(out=w2_raw1[:], in_=w2[:, P : 2 * P].rearrange("(p j) m -> p j m", j=PACK))
 
         identity = keep.tile([P, P], F32, name="identity")
         make_identity(nc, identity[:])
@@ -106,8 +108,10 @@ def tile_picked_ivfpq_none_p_kernel(tc, x_words, x_scales, w1, w2, dn, qn, offs,
         nc.vector.tensor_copy(offs_words[:], word_table[:].bitcast(U32).indirect(offs_list[:]))
         w1_q1 = quantize(interleave(w1_raw1, 0, P, "w1_grouped1", "w1_grouped1"), "w1_q1")
         w1_grouped2 = interleave(w1_raw2, 0, P, "w1_grouped2", "w1_grouped2")
-        qn_cols = keep.tile([P, M_TILES], F32, name="qn_cols", align_bytes=64)
-        nc.scalar.copy(qn_cols[:], qn_bank[:, :M_TILES])
+        qn_cols = keep.tile([P, M_TILES - 1], F32, name="qn_cols", align_bytes=64)
+        nc.scalar.copy(qn_cols[:], qn_bank[:, : M_TILES - 1])
+        qn_last = keep.tile([P, 1], F32, name="qn_last", tag="qn_last", align_bytes=64)
+        nc.scalar.copy(qn_last[:], qn_bank[:, M_TILES - 1 : M_TILES])
 
         def product(quantized, cols, words, plane, name, tag):
             codes, scales = quantized
@@ -124,7 +128,7 @@ def tile_picked_ivfpq_none_p_kernel(tc, x_words, x_scales, w1, w2, dn, qn, offs,
             return bank
 
         def centres(t, quantized, cols, tag):
-            bank = product(quantized, cols, cent_words, cent_plane, f"c_bank{t}", "c_bank1")
+            bank = product(quantized, cols, cent_words, cent_plane, f"c_bank{t}", f"c_bank{t}")
             rows = keep.tile([P, V + SPARE], F32, name=f"c_rows{t}", tag=tag, align_bytes=64)
             nc.gpsimd.memset(rows[:, V:], 0.0)
             nc.scalar.copy(rows[:, :V], bank[:])
@@ -137,14 +141,14 @@ def tile_picked_ivfpq_none_p_kernel(tc, x_words, x_scales, w1, w2, dn, qn, offs,
 
         def finish(t, bank, part, j0, j1, tag):
             if t == 2:
-                result = reused.tile([P, S], F32, name="result2", offset=S * 4, align_bytes=64)
+                result = reused.tile([P, j1 - j0], F32, name=f"result2_{j0}", offset=j0 * 4, align_bytes=64)
             else:
                 result = keep.tile([P, j1 - j0], F32, name=f"result{t}_{j0}", tag=tag, align_bytes=64)
             nc.vector.scalar_tensor_tensor(result[:], bank[:, j0:j1], qn_cols[:, t : t + 1], part[:], ADD, ADD)
             nc.sync.dma_start(out=out[t * P : (t + 1) * P, j0:j1], in_=result[:])
 
-        def rests(t, quantized):
-            return product(quantized, slice(t % 2 * P, (t % 2 + 1) * P), offs_words, offs_plane, f"r_bank{t}", f"r_bank{t}")
+        def rests(t, quantized, m0):
+            return product(quantized, slice(m0, m0 + P), offs_words, offs_plane, f"r_bank{t}", f"r_bank{t}")
 
         c_rows0 = keep.tile([P, V + SPARE], F32, name="c_rows0", align_bytes=64)
         nc.gpsimd.memset(c_rows0[:, V:], 0.0)
@@ -166,24 +170,29 @@ def tile_picked_ivfpq_none_p_kernel(tc, x_words, x_scales, w1, w2, dn, qn, offs,
                 nc.vector.tensor_copy(c_rows0[:, cols], bank[:])
         w1_q2 = quantize(w1_grouped2, "w1_q2", "w1_grouped1")
         part0 = look_up(c_rows0, dn_rows, 0, S, "part0", "part0")
-        w1_q3 = quantize(interleave(w1_raw3, 0, P, "w1_grouped3", "w1_q0_codes"), "w1_q3")
+        w2_q3 = quantize(interleave(w2_raw3, 0, P, "w2_grouped3", "w1_q0_codes"), "w2_q3")
         c_rows1 = centres(1, w1_q1, slice(0, P), "c_rows1")
         part1 = look_up(c_rows1, dn_rows, 0, S, "part1", "part1")
-        w2_q23 = quantize(interleave(w2_raw23, 0, 2 * P, "w2_grouped23", "w1_q1_codes"), "w2_q23")
+        w2_q2 = quantize(interleave(w2_raw2, 0, P, "w2_grouped2", "w1_q1_codes"), "w2_q2")
         c_rows2 = centres(2, w1_q2, slice(0, P), "c_rows2")
-        part2 = look_up(c_rows2, dn_rows, 0, S, "part2", "part2")
-        r_bank3 = rests(3, w2_q23)
-        w2_grouped01 = interleave(w2_raw01, 0, 2 * P, "w2_grouped01", "w1_q2_codes")
-        w2_q01 = quantize(w2_grouped01, "w2_q01")
+        r_bank3 = rests(3, w2_q3, 0)
+        r_bank2 = rests(2, w2_q2, 0)
+        part2a = look_up(c_rows2, dn_rows, 0, S // 2, "part2a", "part2a")
+        w1_q3 = quantize(interleave(w1_raw3, 0, P, "w1_grouped3", "w1_q2_codes"), "w1_q3", "w2_q3_codes")
+        w2_q0 = quantize(interleave(w2_raw0, 0, P, "w2_grouped0", "w1_q2_scales"), "w2_q0")
+        part2b = look_up(c_rows2, dn_rows, S // 2, S, "part2b", "w2_raw0")
+        w2_q1 = quantize(interleave(w2_raw1, 0, P, "w2_grouped1", "w1_q1_scales"), "w2_q1")
         r_rows3 = keep.tile([P, S], F32, name="r_rows3", align_bytes=64)
-        nc.scalar.activation(r_rows3[:], r_bank3[:], IDENTITY, bias=qn_cols[:, 3:4])
-        r_dn3 = keep.tile([P, S], F32, name="r_dn3", tag="w1_q2_codes", align_bytes=64)
+        nc.scalar.activation(r_rows3[:], r_bank3[:], IDENTITY, bias=qn_last[:])
+        r_dn3 = keep.tile([P, S], F32, name="r_dn3", tag="c_rows2", align_bytes=64)
         nc.gpsimd.tensor_tensor(r_dn3[:], r_rows3[:], dn_rows[:], ADD)
-        c_rows3 = centres(3, w1_q3, slice(0, P), "c_rows3")
-        finish(2, rests(2, w2_q23), part2, 0, S, "w2_raw01")
-        finish(0, rests(0, w2_q01), part0, 0, S, "result0")
-        finish(1, rests(1, w2_q01), part1, 0, S, "result1")
-        for h, tag in enumerate(("w2_q01_codes", "w2_q01_scales")):
+        c_rows3 = keep.tile([P, V], F32, name="c_rows3", tag="qn_last", align_bytes=64)
+        nc.scalar.copy(c_rows3[:], product(w1_q3, slice(0, P), cent_words, cent_plane, "c_bank3", "c_bank3")[:])
+        finish(2, r_bank2, part2a, 0, S // 2, None)
+        finish(2, r_bank2, part2b, S // 2, S, None)
+        finish(0, rests(0, w2_q0, 0), part0, 0, S, "result0")
+        finish(1, rests(1, w2_q1, 0), part1, 0, S, "result1")
+        for h, tag in enumerate(("w2_q1_codes", "w2_q1_scales")):
             j0, j1 = h * S // 2, (h + 1) * S // 2
             result = look_up(c_rows3, r_dn3, j0, j1, f"result3_{h}", tag)
             nc.sync.dma_start(out=out[3 * P :, j0:j1], in_=result[:])

@@ -37,7 +37,8 @@ def tile_picked_ivfpq_none_p_kernel(tc, x_words, x_scales, w1, w2, dn, qn, offs,
         scale_table = keep.tile([P, T], U8, name="scale_table", align_bytes=64)
         scale_rows = x_scales[0].bitcast(I32)
         for q in (0, 2, 1, 3):
-            nc.sync.dma_start(
+            queue = nc.sync if q % 2 == 0 else nc.scalar
+            queue.dma_start(
                 out=scale_table[:].bitcast(I32)[32 * q : 32 * q + 32, :],
                 in_=scale_rows[4 * q : 4 * q + 4, :].unsqueeze(0).to_broadcast([8, 4, T // 4]),
             )
@@ -152,9 +153,9 @@ def tile_picked_ivfpq_none_p_kernel(tc, x_words, x_scales, w1, w2, dn, qn, offs,
 
         c_rows0 = keep.tile([P, V + SPARE], F32, name="c_rows0", align_bytes=64)
         nc.gpsimd.memset(c_rows0[:, V:], 0.0)
-        for h, tag in enumerate(("c_bank0", "r_bank2")):
-            cols = slice(h * V // 2, (h + 1) * V // 2)
-            bank = psum.tile([P, V // 2], F32, name=f"c_half{h}", tag=tag)
+        for v0, v1, tag in ((0, 256, "c_bank0"), (256, 384, "r_bank2"), (384, 512, "r_bank0")):
+            cols = slice(v0, v1)
+            bank = psum.tile([P, v1 - v0], F32, name=f"c_piece{v0}", tag=tag)
             nc.tensor.matmul_mx(
                 out=bank[:],
                 lhsT=w1_q0[0][:].bitcast(FP8X4),
@@ -164,7 +165,7 @@ def tile_picked_ivfpq_none_p_kernel(tc, x_words, x_scales, w1, w2, dn, qn, offs,
                 start=True,
                 stop=True,
             )
-            if h == 0:
+            if v1 < V:
                 nc.scalar.copy(c_rows0[:, cols], bank[:])
             else:
                 nc.vector.tensor_copy(c_rows0[:, cols], bank[:])
@@ -174,11 +175,11 @@ def tile_picked_ivfpq_none_p_kernel(tc, x_words, x_scales, w1, w2, dn, qn, offs,
         c_rows1 = centres(1, w1_q1, slice(0, P), "c_rows1")
         part1 = look_up(c_rows1, dn_rows, 0, S, "part1", "part1")
         w2_q2 = quantize(interleave(w2_raw2, 0, P, "w2_grouped2", "w1_q1_codes"), "w2_q2")
+        w1_q3 = quantize(interleave(w1_raw3, 0, P, "w1_grouped3", "w1_q2_codes"), "w1_q3")
         c_rows2 = centres(2, w1_q2, slice(0, P), "c_rows2")
         r_bank3 = rests(3, w2_q3, 0)
         r_bank2 = rests(2, w2_q2, 0)
         part2a = look_up(c_rows2, dn_rows, 0, S // 2, "part2a", "part2a")
-        w1_q3 = quantize(interleave(w1_raw3, 0, P, "w1_grouped3", "w1_q2_codes"), "w1_q3", "w2_q3_codes")
         w2_q0 = quantize(interleave(w2_raw0, 0, P, "w2_grouped0", "w1_q2_scales"), "w2_q0")
         part2b = look_up(c_rows2, dn_rows, S // 2, S, "part2b", "w2_raw0")
         w2_q1 = quantize(interleave(w2_raw1, 0, P, "w2_grouped1", "w1_q1_scales"), "w2_q1")
@@ -192,7 +193,6 @@ def tile_picked_ivfpq_none_p_kernel(tc, x_words, x_scales, w1, w2, dn, qn, offs,
         finish(2, r_bank2, part2b, S // 2, S, None)
         finish(0, rests(0, w2_q0, 0), part0, 0, S, "result0")
         finish(1, rests(1, w2_q1, 0), part1, 0, S, "result1")
-        for h, tag in enumerate(("w2_q1_codes", "w2_q1_scales")):
-            j0, j1 = h * S // 2, (h + 1) * S // 2
-            result = look_up(c_rows3, r_dn3, j0, j1, f"result3_{h}", tag)
+        for j0, j1, tag in ((0, 256, "w2_q1_codes"), (256, 384, "w2_q1_scales"), (384, 512, "w2_q0_scales")):
+            result = look_up(c_rows3, r_dn3, j0, j1, f"result3_{j0}", tag)
             nc.sync.dma_start(out=out[3 * P :, j0:j1], in_=result[:])

@@ -37,8 +37,7 @@ def tile_picked_ivfpq_none_p_kernel(tc, x_words, x_scales, w1, w2, dn, qn, offs,
         scale_table = keep.tile([P, T], U8, name="scale_table", align_bytes=64)
         scale_rows = x_scales[0].bitcast(I32)
         for q in (0, 2, 1, 3):
-            queue = nc.sync if q % 2 == 0 else nc.scalar
-            queue.dma_start(
+            nc.sync.dma_start(
                 out=scale_table[:].bitcast(I32)[32 * q : 32 * q + 32, :],
                 in_=scale_rows[4 * q : 4 * q + 4, :].unsqueeze(0).to_broadcast([8, 4, T // 4]),
             )
@@ -75,11 +74,11 @@ def tile_picked_ivfpq_none_p_kernel(tc, x_words, x_scales, w1, w2, dn, qn, offs,
         w1_raw1 = load_weight(w1, P, 2 * P, "w1_raw1")
         w1_raw2 = load_weight(w1, 2 * P, 3 * P, "w1_raw2")
         nc.sync.dma_start(own_list[:], own)
-        w2_raw3 = load_weight(w2, 3 * P, N, "w2_raw3")
+        w1_raw3 = load_weight(w1, 3 * P, N, "w1_raw3")
         dn_rows = keep.tile([P, S], F32, name="dn_rows")
         nc.sync.dma_start(out=dn_rows[:], in_=dn)
+        w2_raw3 = load_weight(w2, 3 * P, N, "w2_raw3")
         w2_raw2 = load_weight(w2, 2 * P, 3 * P, "w2_raw2")
-        w1_raw3 = load_weight(w1, 3 * P, N, "w1_raw3")
         w2_raw0 = load_weight(w2, 0, P, "w2_raw0")
         w2_raw1 = reused.tile([P, PACK, P], F32, name="w2_raw1", offset=0, align_bytes=64)
         nc.sync.dma_start(out=w2_raw1[:], in_=w2[:, P : 2 * P].rearrange("(p j) m -> p j m", j=PACK))
@@ -171,11 +170,11 @@ def tile_picked_ivfpq_none_p_kernel(tc, x_words, x_scales, w1, w2, dn, qn, offs,
                 nc.vector.tensor_copy(c_rows0[:, cols], bank[:])
         w1_q2 = quantize(w1_grouped2, "w1_q2", "w1_grouped1")
         part0 = look_up(c_rows0, dn_rows, 0, S, "part0", "part0")
-        w2_q3 = quantize(interleave(w2_raw3, 0, P, "w2_grouped3", "w1_q0_codes"), "w2_q3")
+        w1_q3 = quantize(interleave(w1_raw3, 0, P, "w1_grouped3", "w1_q0_codes"), "w1_q3")
         c_rows1 = centres(1, w1_q1, slice(0, P), "c_rows1")
         part1 = look_up(c_rows1, dn_rows, 0, S, "part1", "part1")
-        w2_q2 = quantize(interleave(w2_raw2, 0, P, "w2_grouped2", "w1_q1_codes"), "w2_q2")
-        w1_q3 = quantize(interleave(w1_raw3, 0, P, "w1_grouped3", "w1_q2_codes"), "w1_q3")
+        w2_q3 = quantize(interleave(w2_raw3, 0, P, "w2_grouped3", "w1_q1_codes"), "w2_q3")
+        w2_q2 = quantize(interleave(w2_raw2, 0, P, "w2_grouped2", "w1_q2_codes"), "w2_q2")
         c_rows2 = centres(2, w1_q2, slice(0, P), "c_rows2")
         r_bank3 = rests(3, w2_q3, 0)
         r_bank2 = rests(2, w2_q2, 0)

@@ -18,8 +18,14 @@ IDENTITY = mybir.ActivationFunctionType.Identity
 
 P = 128
 PACK = 4
+GROUP = 16
+QUADRANT = 32
+LINE = 4
 M_TILES = N // P
+LAST = M_TILES - 1
 SPARE = 16
+HALF = S // 2
+QUARTER = S // 4
 
 
 def tile_picked_ivfpq_none_p_kernel(tc, x_words, x_scales, w1, w2, dn, qn, offs, cent, own, out):
@@ -29,59 +35,73 @@ def tile_picked_ivfpq_none_p_kernel(tc, x_words, x_scales, w1, w2, dn, qn, offs,
         reused = ctx.enter_context(tc.tile_pool(name="reused", bufs=1))
         psum = ctx.enter_context(tc.psum_pool(name="psum", bufs=1))
 
-        cent_list = keep.tile([P, V // 16], U16, name="cent_list")
-        offs_list = keep.tile([P, S // 16], U16, name="offs_list")
-        own_list = keep.tile([P, S // 16], U16, name="own_list")
-
-        nc.sync.dma_start(cent_list[:], cent)
-        scale_table = keep.tile([P, T], U8, name="scale_table", align_bytes=64)
-        scale_rows = x_scales[0].bitcast(I32)
-        for q in (0, 2, 1, 3):
-            nc.sync.dma_start(
-                out=scale_table[:].bitcast(I32)[32 * q : 32 * q + 32, :],
-                in_=scale_rows[4 * q : 4 * q + 4, :].unsqueeze(0).to_broadcast([8, 4, T // 4]),
-            )
-        nc.sync.dma_start(offs_list[:], offs)
-
-        def load_weight(w, m0, m1, name):
-            raw = keep.tile([P, PACK, m1 - m0], F32, name=name, tag=name, align_bytes=64)
-            nc.sync.dma_start(out=raw[:], in_=w[:, m0:m1].rearrange("(p j) m -> p j m", j=PACK))
+        def load_weight(raw, w, t):
+            nc.sync.dma_start(out=raw[:], in_=w[:, t * P : (t + 1) * P].rearrange("(p j) m -> p j m", j=PACK))
             return raw
 
-        def interleave(raw, m0, m1, name, tag):
-            grouped = keep.tile([P, m1 - m0, PACK], BF16, name=name, tag=tag, align_bytes=64)
+        def raw_tile(name):
+            return keep.tile([P, PACK, P], F32, name=name, tag=name, align_bytes=64)
+
+        def interleave(raw, name, slot):
+            grouped = keep.tile([P, P, PACK], BF16, name=name, tag=slot, align_bytes=64)
             nc.scalar.activation(
-                grouped[:].rearrange("p (c i) j -> p c j i", i=4),
-                raw[:, :, m0:m1].rearrange("p j (c i) -> p c j i", i=4),
+                grouped[:].rearrange("p (c i) j -> p c j i", i=LINE),
+                raw[:].rearrange("p j (c i) -> p c j i", i=LINE),
                 IDENTITY,
                 scale=-2.0,
             )
             return grouped
 
-        def quantize(grouped, name, tag=None):
-            width = grouped.shape[1]
-            codes = keep.tile([P, width], U32, name=name + "_codes", tag=tag or name + "_codes", align_bytes=64)
-            scales = keep.tile([P, width], U8, name=name + "_scales", tag=name + "_scales", align_bytes=64)
+        def quantize(grouped, name, codes_slot):
+            codes = keep.tile([P, P], U32, name=name + "_codes", tag=codes_slot, align_bytes=64)
+            scales = keep.tile([P, P], U8, name=name + "_scales", tag=name + "_scales", align_bytes=64)
             nc.vector.quantize_mx(out=codes[:].bitcast(FP8X4), scales=scales[:], in_=grouped[:].rearrange("p m j -> p (m j)"))
             return codes, scales
 
+        def product(quantized, words, plane, c0, c1, name, bank_slot):
+            codes, scales = quantized
+            bank = psum.tile([P, c1 - c0], F32, name=name, tag=bank_slot)
+            nc.tensor.matmul_mx(
+                out=bank[:],
+                lhsT=codes[:].bitcast(FP8X4),
+                lhsT_scale=scales[:],
+                rhs=words[:, c0:c1].bitcast(FP8X4),
+                rhs_scale=plane[:, c0:c1],
+                start=True,
+                stop=True,
+            )
+            return bank
+
+        cent_list = keep.tile([P, V // GROUP], U16, name="cent_list")
+        offs_list = keep.tile([P, S // GROUP], U16, name="offs_list")
+        own_list = keep.tile([P, S // GROUP], U16, name="own_list")
+        nc.sync.dma_start(cent_list[:], cent)
+
+        scale_table = keep.tile([P, T], U8, name="scale_table", align_bytes=64)
+        scale_rows = x_scales[0].bitcast(I32)
+        for q in (0, 2, 1, 3):
+            nc.sync.dma_start(
+                out=scale_table[:].bitcast(I32)[QUADRANT * q : QUADRANT * (q + 1), :],
+                in_=scale_rows[4 * q : 4 * q + 4, :].unsqueeze(0).to_broadcast([QUADRANT // 4, 4, T // 4]),
+            )
+        nc.sync.dma_start(offs_list[:], offs)
         word_table = keep.tile([P, T], I32, name="word_table", align_bytes=64)
         nc.sync.dma_start(out=word_table[:], in_=x_words[0].rearrange("p n t -> p (n t)").bitcast(I32))
-        w1_raw0 = load_weight(w1, 0, P, "w1_raw0")
+        w1_raw0 = load_weight(raw_tile("w1_raw0"), w1, 0)
         qn_rows = keep.tile([P, P], F32, name="qn_rows")
         nc.gpsimd.memset(qn_rows[:], 0.0)
         nc.sync.dma_start(out=qn_rows[:M_TILES, :], in_=qn.rearrange("(t p) o -> t (p o)", p=P))
-        w1_raw1 = load_weight(w1, P, 2 * P, "w1_raw1")
-        w1_raw2 = load_weight(w1, 2 * P, 3 * P, "w1_raw2")
+        w1_raw1 = load_weight(raw_tile("w1_raw1"), w1, 1)
+        w1_raw2 = load_weight(raw_tile("w1_raw2"), w1, 2)
         nc.sync.dma_start(own_list[:], own)
-        w1_raw3 = load_weight(w1, 3 * P, N, "w1_raw3")
+        w1_raw3 = load_weight(raw_tile("w1_raw3"), w1, 3)
         dn_rows = keep.tile([P, S], F32, name="dn_rows")
         nc.sync.dma_start(out=dn_rows[:], in_=dn)
-        w2_raw3 = load_weight(w2, 3 * P, N, "w2_raw3")
-        w2_raw2 = load_weight(w2, 2 * P, 3 * P, "w2_raw2")
-        w2_raw0 = load_weight(w2, 0, P, "w2_raw0")
+        w2_raw3 = load_weight(raw_tile("w2_raw3"), w2, 3)
+        w2_raw2 = load_weight(raw_tile("w2_raw2"), w2, 2)
+        w2_raw0 = load_weight(raw_tile("w2_raw0"), w2, 0)
         w2_raw1 = reused.tile([P, PACK, P], F32, name="w2_raw1", offset=0, align_bytes=64)
-        nc.sync.dma_start(out=w2_raw1[:], in_=w2[:, P : 2 * P].rearrange("(p j) m -> p j m", j=PACK))
+        load_weight(w2_raw1, w2, 1)
 
         identity = keep.tile([P, P], F32, name="identity")
         make_identity(nc, identity[:])
@@ -90,108 +110,88 @@ def tile_picked_ivfpq_none_p_kernel(tc, x_words, x_scales, w1, w2, dn, qn, offs,
 
         offs_plane = keep.tile([P, S], U8, name="offs_plane", align_bytes=64)
         nc.gpsimd.memset(offs_plane[:].bitcast(I32), 0)
-
         cent_plane = keep.tile([P, V], U8, name="cent_plane", align_bytes=64)
         offs_bytes = keep.tile([P, S], U8, name="offs_bytes", align_bytes=64)
         nc.vector.tensor_copy(cent_plane[:], scale_table[:].indirect(cent_list[:]))
         nc.vector.tensor_copy(offs_bytes[:], scale_table[:].indirect(offs_list[:]))
         for i in range(4):
             nc.sync.dma_start(
-                out=offs_plane[:].bitcast(I32)[i:P:32, :],
-                in_=offs_bytes[:].bitcast(I32)[16 * (i // 2) + i : P : 32, :],
+                out=offs_plane[:].bitcast(I32)[i:P:QUADRANT, :],
+                in_=offs_bytes[:].bitcast(I32)[GROUP * (i // 2) + i : P : QUADRANT, :],
             )
 
         cent_words = keep.tile([P, V], U32, name="cent_words", align_bytes=64)
         nc.vector.tensor_copy(cent_words[:], word_table[:].bitcast(U32).indirect(cent_list[:]))
-        w1_q0 = quantize(interleave(w1_raw0, 0, P, "w1_grouped0", "w1_grouped0"), "w1_q0")
+        w1_q0 = quantize(interleave(w1_raw0, "w1_grouped0", "w1_grouped0"), "w1_q0", "w1_q0_codes")
         offs_words = keep.tile([P, S], U32, name="offs_words", tag="w1_raw0", align_bytes=64)
         nc.vector.tensor_copy(offs_words[:], word_table[:].bitcast(U32).indirect(offs_list[:]))
-        w1_q1 = quantize(interleave(w1_raw1, 0, P, "w1_grouped1", "w1_grouped1"), "w1_q1")
-        w1_grouped2 = interleave(w1_raw2, 0, P, "w1_grouped2", "w1_grouped2")
-        qn_cols = keep.tile([P, M_TILES - 1], F32, name="qn_cols", align_bytes=64)
-        nc.scalar.copy(qn_cols[:], qn_bank[:, : M_TILES - 1])
+        w1_q1 = quantize(interleave(w1_raw1, "w1_grouped1", "w1_grouped1"), "w1_q1", "w1_q1_codes")
+        w1_grouped2 = interleave(w1_raw2, "w1_grouped2", "w1_grouped2")
+        qn_cols = keep.tile([P, LAST], F32, name="qn_cols", align_bytes=64)
+        nc.scalar.copy(qn_cols[:], qn_bank[:, :LAST])
         qn_last = keep.tile([P, 1], F32, name="qn_last", tag="qn_last", align_bytes=64)
-        nc.scalar.copy(qn_last[:], qn_bank[:, M_TILES - 1 : M_TILES])
+        nc.scalar.copy(qn_last[:], qn_bank[:, LAST:M_TILES])
 
-        def product(quantized, cols, words, plane, name, tag):
-            codes, scales = quantized
-            bank = psum.tile([P, 512], F32, name=name, tag=tag)
-            nc.tensor.matmul_mx(
-                out=bank[:],
-                lhsT=codes[:, cols].bitcast(FP8X4),
-                lhsT_scale=scales[:, cols],
-                rhs=words[:].bitcast(FP8X4),
-                rhs_scale=plane[:],
-                start=True,
-                stop=True,
-            )
-            return bank
+        def centres(t, quantized):
+            return product(quantized, cent_words, cent_plane, 0, V, f"c_bank{t}", f"c_bank{t}")
 
-        def centres(t, quantized, cols, tag):
-            bank = product(quantized, cols, cent_words, cent_plane, f"c_bank{t}", f"c_bank{t}")
-            rows = keep.tile([P, V + SPARE], F32, name=f"c_rows{t}", tag=tag, align_bytes=64)
-            nc.gpsimd.memset(rows[:, V:], 0.0)
-            nc.scalar.copy(rows[:, :V], bank[:])
-            return rows
+        def rests(t, quantized):
+            return product(quantized, offs_words, offs_plane, 0, S, f"r_bank{t}", f"r_bank{t}")
 
-        def look_up(rows, added, j0, j1, name, tag):
-            part = keep.tile([P, j1 - j0], F32, name=name, tag=tag, align_bytes=64)
-            nc.vector.tensor_tensor(part[:], rows[:].indirect(own_list[:, j0 // 16 : j1 // 16]), added[:, j0:j1], ADD)
+        def look_up(c_rows, added, j0, j1, name, slot):
+            part = keep.tile([P, j1 - j0], F32, name=name, tag=slot, align_bytes=64)
+            offsets = own_list[:, j0 // GROUP : j1 // GROUP]
+            nc.vector.tensor_tensor(part[:], c_rows[:].indirect(offsets), added[:, j0:j1], ADD)
             return part
 
-        def finish(t, bank, part, j0, j1, tag):
-            if t == 2:
-                result = reused.tile([P, j1 - j0], F32, name=f"result2_{j0}", offset=j0 * 4, align_bytes=64)
-            else:
-                result = keep.tile([P, j1 - j0], F32, name=f"result{t}_{j0}", tag=tag, align_bytes=64)
-            nc.vector.scalar_tensor_tensor(result[:], bank[:, j0:j1], qn_cols[:, t : t + 1], part[:], ADD, ADD)
+        def finish(t, result, r_bank, part, j0, j1):
+            nc.vector.scalar_tensor_tensor(result[:], r_bank[:, j0:j1], qn_cols[:, t : t + 1], part[:], ADD, ADD)
             nc.sync.dma_start(out=out[t * P : (t + 1) * P, j0:j1], in_=result[:])
-
-        def rests(t, quantized, m0):
-            return product(quantized, slice(m0, m0 + P), offs_words, offs_plane, f"r_bank{t}", f"r_bank{t}")
 
         c_rows0 = keep.tile([P, V + SPARE], F32, name="c_rows0", align_bytes=64)
         nc.gpsimd.memset(c_rows0[:, V:], 0.0)
-        for v0, v1, tag in ((0, 256, "c_bank0"), (256, 384, "r_bank2"), (384, 512, "r_bank0")):
-            cols = slice(v0, v1)
-            bank = psum.tile([P, v1 - v0], F32, name=f"c_piece{v0}", tag=tag)
-            nc.tensor.matmul_mx(
-                out=bank[:],
-                lhsT=w1_q0[0][:].bitcast(FP8X4),
-                lhsT_scale=w1_q0[1][:],
-                rhs=cent_words[:, cols].bitcast(FP8X4),
-                rhs_scale=cent_plane[:, cols],
-                start=True,
-                stop=True,
-            )
-            if v1 < V:
-                nc.scalar.copy(c_rows0[:, cols], bank[:])
-            else:
-                nc.vector.tensor_copy(c_rows0[:, cols], bank[:])
+        for v0, v1, bank_slot in ((0, HALF, "c_bank0"), (HALF, V - QUARTER, "r_bank2")):
+            piece = product(w1_q0, cent_words, cent_plane, v0, v1, f"c_piece{v0}", bank_slot)
+            nc.scalar.copy(c_rows0[:, v0:v1], piece[:])
+        last_piece = product(w1_q0, cent_words, cent_plane, V - QUARTER, V, "c_last_piece", "r_bank0")
+        nc.vector.tensor_copy(c_rows0[:, V - QUARTER : V], last_piece[:])
         w1_q2 = quantize(w1_grouped2, "w1_q2", "w1_grouped1")
         part0 = look_up(c_rows0, dn_rows, 0, S, "part0", "part0")
-        w1_q3 = quantize(interleave(w1_raw3, 0, P, "w1_grouped3", "w1_q0_codes"), "w1_q3")
-        c_rows1 = centres(1, w1_q1, slice(0, P), "c_rows1")
+
+        w1_q3 = quantize(interleave(w1_raw3, "w1_grouped3", "w1_q0_codes"), "w1_q3", "w1_q3_codes")
+        c_bank1 = centres(1, w1_q1)
+        c_rows1 = keep.tile([P, V + SPARE], F32, name="c_rows1", align_bytes=64)
+        nc.gpsimd.memset(c_rows1[:, V:], 0.0)
+        nc.scalar.copy(c_rows1[:, :V], c_bank1[:])
         part1 = look_up(c_rows1, dn_rows, 0, S, "part1", "part1")
-        w2_q3 = quantize(interleave(w2_raw3, 0, P, "w2_grouped3", "w1_q1_codes"), "w2_q3")
-        w2_q2 = quantize(interleave(w2_raw2, 0, P, "w2_grouped2", "w1_q2_codes"), "w2_q2")
-        c_rows2 = centres(2, w1_q2, slice(0, P), "c_rows2")
-        r_bank3 = rests(3, w2_q3, 0)
-        r_bank2 = rests(2, w2_q2, 0)
-        part2a = look_up(c_rows2, dn_rows, 0, S // 2, "part2a", "part2a")
-        w2_q0 = quantize(interleave(w2_raw0, 0, P, "w2_grouped0", "w1_q2_scales"), "w2_q0")
-        part2b = look_up(c_rows2, dn_rows, S // 2, S, "part2b", "w2_raw0")
-        w2_q1 = quantize(interleave(w2_raw1, 0, P, "w2_grouped1", "w1_q1_scales"), "w2_q1")
+        w2_q3 = quantize(interleave(w2_raw3, "w2_grouped3", "w1_q1_codes"), "w2_q3", "w2_q3_codes")
+        w2_q2 = quantize(interleave(w2_raw2, "w2_grouped2", "w2_grouped2"), "w2_q2", "w2_q2_codes")
+        c_bank2 = centres(2, w1_q2)
+        c_rows2 = keep.tile([P, V], F32, name="c_rows2", tag="c_rows2", align_bytes=64)
+        nc.scalar.copy(c_rows2[:], c_bank2[:])
+        r_bank3 = rests(3, w2_q3)
+        r_bank2 = rests(2, w2_q2)
+
+        part2a = look_up(c_rows2, dn_rows, 0, HALF, "part2a", "part2a")
+        w2_q0 = quantize(interleave(w2_raw0, "w2_grouped0", "w1_q2_scales"), "w2_q0", "w2_q0_codes")
+        part2b = look_up(c_rows2, dn_rows, HALF, S, "part2b", "w2_raw0")
+        w2_q1 = quantize(interleave(w2_raw1, "w2_grouped1", "w1_q1_scales"), "w2_q1", "w2_q1_codes")
+
         r_rows3 = keep.tile([P, S], F32, name="r_rows3", align_bytes=64)
         nc.scalar.activation(r_rows3[:], r_bank3[:], IDENTITY, bias=qn_last[:])
         r_dn3 = keep.tile([P, S], F32, name="r_dn3", tag="c_rows2", align_bytes=64)
         nc.gpsimd.tensor_tensor(r_dn3[:], r_rows3[:], dn_rows[:], ADD)
         c_rows3 = keep.tile([P, V], F32, name="c_rows3", tag="qn_last", align_bytes=64)
-        nc.scalar.copy(c_rows3[:], product(w1_q3, slice(0, P), cent_words, cent_plane, "c_bank3", "c_bank3")[:])
-        finish(2, r_bank2, part2a, 0, S // 2, None)
-        finish(2, r_bank2, part2b, S // 2, S, None)
-        finish(0, rests(0, w2_q0, 0), part0, 0, S, "result0")
-        finish(1, rests(1, w2_q1, 0), part1, 0, S, "result1")
-        for j0, j1, tag in ((0, 256, "w2_q1_codes"), (256, 384, "w2_q1_scales"), (384, 512, "w2_q0_scales")):
-            result = look_up(c_rows3, r_dn3, j0, j1, f"result3_{j0}", tag)
-            nc.sync.dma_start(out=out[3 * P :, j0:j1], in_=result[:])
+        nc.scalar.copy(c_rows3[:], centres(3, w1_q3)[:])
+
+        for part, j0 in ((part2a, 0), (part2b, HALF)):
+            result2 = reused.tile([P, HALF], F32, name=f"result2_{j0}", offset=j0 * 4, align_bytes=64)
+            finish(2, result2, r_bank2, part, j0, j0 + HALF)
+        for t, quantized, part in ((0, w2_q0, part0), (1, w2_q1, part1)):
+            r_bank = rests(t, quantized)
+            result = keep.tile([P, S], F32, name=f"result{t}", align_bytes=64)
+            finish(t, result, r_bank, part, 0, S)
+
+        for j0, j1, slot in ((0, HALF, "w2_q1_codes"), (HALF, S - QUARTER, "w2_q1_scales"), (S - QUARTER, S, "w2_q0_scales")):
+            result3 = look_up(c_rows3, r_dn3, j0, j1, f"result3_{j0}", slot)
+            nc.sync.dma_start(out=out[LAST * P :, j0:j1], in_=result3[:])

@@ -19,6 +19,9 @@ IDENTITY = mybir.ActivationFunctionType.Identity
 P = 128
 PACK = 4
 GROUP = 16
+BLOCK = 8
+RAW = PACK * P * 4
+PAD = 16
 QUADRANT = 32
 LINE = 4
 M_TILES = N // P
@@ -35,15 +38,20 @@ def tile_picked_ivfpq_none_p_kernel(tc, x_words, x_scales, w1, w2, dn, qn, offs,
         reused = ctx.enter_context(tc.tile_pool(name="reused", bufs=1))
         psum = ctx.enter_context(tc.psum_pool(name="psum", bufs=1))
 
+        def place(shape, dtype, name, slot):
+            if isinstance(slot, str):
+                return keep.tile(shape, dtype, name=name, tag=slot, align_bytes=64)
+            return reused.tile(shape, dtype, name=name, offset=slot, align_bytes=64)
+
         def load_weight(raw, w, t):
             nc.sync.dma_start(out=raw[:], in_=w[:, t * P : (t + 1) * P].rearrange("(p j) m -> p j m", j=PACK))
             return raw
 
-        def raw_tile(name):
-            return keep.tile([P, PACK, P], F32, name=name, tag=name, align_bytes=64)
+        def raw_tile(name, offset):
+            return place([P, PACK, P], F32, name, offset)
 
         def interleave(raw, name, slot):
-            grouped = keep.tile([P, P, PACK], BF16, name=name, tag=slot, align_bytes=64)
+            grouped = place([P, P, PACK], BF16, name, slot)
             nc.scalar.activation(
                 grouped[:].rearrange("p (c i) j -> p c j i", i=LINE),
                 raw[:].rearrange("p j (c i) -> p c j i", i=LINE),
@@ -52,9 +60,9 @@ def tile_picked_ivfpq_none_p_kernel(tc, x_words, x_scales, w1, w2, dn, qn, offs,
             )
             return grouped
 
-        def quantize(grouped, name, codes_slot):
-            codes = keep.tile([P, P], U32, name=name + "_codes", tag=codes_slot, align_bytes=64)
-            scales = keep.tile([P, P], U8, name=name + "_scales", tag=name + "_scales", align_bytes=64)
+        def quantize(grouped, name, codes_slot, scales_slot=None):
+            codes = place([P, P], U32, name + "_codes", codes_slot)
+            scales = keep.tile([P, P], U8, name=name + "_scales", tag=scales_slot or name + "_scales", align_bytes=64)
             nc.vector.quantize_mx(out=codes[:].bitcast(FP8X4), scales=scales[:], in_=grouped[:].rearrange("p m j -> p (m j)"))
             return codes, scales
 
@@ -77,60 +85,72 @@ def tile_picked_ivfpq_none_p_kernel(tc, x_words, x_scales, w1, w2, dn, qn, offs,
         own_list = keep.tile([P, S // GROUP], U16, name="own_list")
         nc.sync.dma_start(cent_list[:], cent)
 
-        scale_table = keep.tile([P, T], U8, name="scale_table", align_bytes=64)
-        scale_rows = x_scales[0].bitcast(I32)
-        for q in (0, 2, 1, 3):
-            nc.sync.dma_start(
-                out=scale_table[:].bitcast(I32)[QUADRANT * q : QUADRANT * (q + 1), :],
-                in_=scale_rows[4 * q : 4 * q + 4, :].unsqueeze(0).to_broadcast([QUADRANT // 4, 4, T // 4]),
-            )
+        scale_table = place([P, T], U8, "scale_table", 3 * RAW)
+        nc.sync.dma_start(
+            out=scale_table[:].bitcast(I32),
+            in_=x_scales[0].bitcast(I32).unsqueeze(1).to_broadcast([K // 32, BLOCK, T // 4]),
+        )
         nc.sync.dma_start(offs_list[:], offs)
+        nc.sync.dma_start(own_list[:], own)
+        norm_rows = keep.tile([P, P], F32, name="norm_rows", align_bytes=64)
+        nc.gpsimd.memset(norm_rows[:], 0.0)
+        nc.sync.dma_start(out=norm_rows[:M_TILES, :], in_=qn.rearrange("(t p) o -> t (p o)", p=P))
+        nc.sync.dma_start(out=norm_rows[M_TILES : 2 * M_TILES, :], in_=dn[0].rearrange("(t p) -> t p", p=P))
+        w1_raw0 = load_weight(raw_tile("w1_raw0", RAW // 2), w1, 0)
         word_table = keep.tile([P, T], I32, name="word_table", align_bytes=64)
         nc.sync.dma_start(out=word_table[:], in_=x_words[0].rearrange("p n t -> p (n t)").bitcast(I32))
-        w1_raw0 = load_weight(raw_tile("w1_raw0"), w1, 0)
-        qn_rows = keep.tile([P, P], F32, name="qn_rows")
-        nc.gpsimd.memset(qn_rows[:], 0.0)
-        nc.sync.dma_start(out=qn_rows[:M_TILES, :], in_=qn.rearrange("(t p) o -> t (p o)", p=P))
-        w1_raw1 = load_weight(raw_tile("w1_raw1"), w1, 1)
-        w1_raw2 = load_weight(raw_tile("w1_raw2"), w1, 2)
-        nc.sync.dma_start(own_list[:], own)
-        w1_raw3 = load_weight(raw_tile("w1_raw3"), w1, 3)
-        dn_rows = keep.tile([P, S], F32, name="dn_rows")
-        nc.sync.dma_start(out=dn_rows[:], in_=dn)
-        w2_raw3 = load_weight(raw_tile("w2_raw3"), w2, 3)
-        w2_raw2 = load_weight(raw_tile("w2_raw2"), w2, 2)
-        w2_raw0 = load_weight(raw_tile("w2_raw0"), w2, 0)
-        w2_raw1 = reused.tile([P, PACK, P], F32, name="w2_raw1", offset=0, align_bytes=64)
-        load_weight(w2_raw1, w2, 1)
+        w1_raw1 = load_weight(raw_tile("w1_raw1", 8 * RAW - RAW // 4), w1, 1)
 
-        identity = keep.tile([P, P], F32, name="identity")
+        w1_raw2 = load_weight(raw_tile("w1_raw2", "w1_raw2"), w1, 2)
+        w1_grouped0 = interleave(w1_raw0, "w1_grouped0", "w1_grouped0")
+        identity = reused.tile([P, P], F32, name="identity", offset=5 * RAW - 2 * P, align_bytes=64)
         make_identity(nc, identity[:])
         qn_bank = psum.tile([P, P], F32, name="qn_bank", tag="r_bank3")
-        nc.tensor.transpose(qn_bank[:], qn_rows[:], identity[:])
-
-        offs_plane = keep.tile([P, S], U8, name="offs_plane", align_bytes=64)
-        nc.gpsimd.memset(offs_plane[:].bitcast(I32), 0)
-        cent_plane = keep.tile([P, V], U8, name="cent_plane", align_bytes=64)
-        offs_bytes = keep.tile([P, S], U8, name="offs_bytes", align_bytes=64)
-        nc.vector.tensor_copy(cent_plane[:], scale_table[:].indirect(cent_list[:]))
-        nc.vector.tensor_copy(offs_bytes[:], scale_table[:].indirect(offs_list[:]))
-        for i in range(4):
-            nc.sync.dma_start(
-                out=offs_plane[:].bitcast(I32)[i:P:QUADRANT, :],
-                in_=offs_bytes[:].bitcast(I32)[GROUP * (i // 2) + i : P : QUADRANT, :],
-            )
-
-        cent_words = keep.tile([P, V], U32, name="cent_words", align_bytes=64)
-        nc.vector.tensor_copy(cent_words[:], word_table[:].bitcast(U32).indirect(cent_list[:]))
-        w1_q0 = quantize(interleave(w1_raw0, "w1_grouped0", "w1_grouped0"), "w1_q0", "w1_q0_codes")
-        offs_words = keep.tile([P, S], U32, name="offs_words", tag="w1_raw0", align_bytes=64)
-        nc.vector.tensor_copy(offs_words[:], word_table[:].bitcast(U32).indirect(offs_list[:]))
-        w1_q1 = quantize(interleave(w1_raw1, "w1_grouped1", "w1_grouped1"), "w1_q1", "w1_q1_codes")
-        w1_grouped2 = interleave(w1_raw2, "w1_grouped2", "w1_grouped2")
+        nc.tensor.transpose(qn_bank[:], norm_rows[:], identity[:])
+        dn_rows = keep.tile([P, S], F32, name="dn_rows", align_bytes=64)
+        for half, bank_slot in enumerate(("r_bank1", "c_bank1")):
+            dn_bank = psum.tile([P, HALF], F32, name=f"dn_bank{half}", tag=bank_slot)
+            dn_cols = place([P, 2 * PAD], F32, f"dn_cols{half}", f"dn_cols{half}")
+            for i in range(2):
+                jt = 2 * half + i
+                nc.scalar.copy(dn_cols[:, PAD * i : PAD * i + 1], qn_bank[:, M_TILES + jt : M_TILES + jt + 1])
+                nc.tensor.transpose(dn_bank[:, i * P : (i + 1) * P], dn_cols[:, PAD * i : PAD * i + 1].to_broadcast([P, P]), identity[:])
+            nc.scalar.copy(dn_rows[:, half * HALF : (half + 1) * HALF], dn_bank[:])
         qn_cols = keep.tile([P, LAST], F32, name="qn_cols", align_bytes=64)
         nc.scalar.copy(qn_cols[:], qn_bank[:, :LAST])
         qn_last = keep.tile([P, 1], F32, name="qn_last", tag="qn_last", align_bytes=64)
         nc.scalar.copy(qn_last[:], qn_bank[:, LAST:M_TILES])
+
+        def move_rows(plane, gathered):
+            nc.gpsimd.memset(plane[:].bitcast(I32), 0)
+            for i in range(4):
+                nc.sync.dma_start(
+                    out=plane[:].bitcast(I32)[i:P:QUADRANT, :],
+                    in_=gathered[:].bitcast(I32)[BLOCK * i : P : QUADRANT, :],
+                )
+
+        cent_bytes = keep.tile([P, V], U8, name="cent_bytes", align_bytes=64)
+        nc.vector.tensor_copy(cent_bytes[:], scale_table[:].indirect(cent_list[:]))
+        cent_plane = keep.tile([P, V], U8, name="cent_plane", align_bytes=64)
+        move_rows(cent_plane, cent_bytes)
+        w1_q0 = quantize(w1_grouped0, "w1_q0", "w1_q0_codes")
+        offs_bytes = place([P, S], U8, "offs_bytes", "offs_bytes")
+        nc.vector.tensor_copy(offs_bytes[:], scale_table[:].indirect(offs_list[:]))
+
+        w1_raw3 = load_weight(raw_tile("w1_raw3", 0), w1, 3)
+        w2_raw3 = load_weight(raw_tile("w2_raw3", RAW), w2, 3)
+        w2_raw2 = load_weight(raw_tile("w2_raw2", 5 * RAW // 2), w2, 2)
+        w2_raw0 = load_weight(raw_tile("w2_raw0", 7 * RAW // 2), w2, 0)
+
+        cent_words = keep.tile([P, V], U32, name="cent_words", align_bytes=64)
+        nc.vector.tensor_copy(cent_words[:], word_table[:].bitcast(U32).indirect(cent_list[:]))
+        offs_words = keep.tile([P, S], U32, name="offs_words", align_bytes=64)
+        nc.vector.tensor_copy(offs_words[:], word_table[:].bitcast(U32).indirect(offs_list[:]))
+        w1_grouped1 = interleave(w1_raw1, "w1_grouped1", 5 * RAW)
+        w2_raw1 = load_weight(raw_tile("w2_raw1", 8 * RAW + RAW // 2), w2, 1)
+        offs_plane = place([P, S], U8, "offs_plane", 8 * RAW)
+        move_rows(offs_plane, offs_bytes)
+        w1_grouped2 = interleave(w1_raw2, "w1_grouped2", 9 * RAW // 2)
 
         def centres(t, quantized):
             return product(quantized, cent_words, cent_plane, 0, V, f"c_bank{t}", f"c_bank{t}")
@@ -139,7 +159,7 @@ def tile_picked_ivfpq_none_p_kernel(tc, x_words, x_scales, w1, w2, dn, qn, offs,
             return product(quantized, offs_words, offs_plane, 0, S, f"r_bank{t}", f"r_bank{t}")
 
         def look_up(c_rows, added, j0, j1, name, slot):
-            part = keep.tile([P, j1 - j0], F32, name=name, tag=slot, align_bytes=64)
+            part = place([P, j1 - j0], F32, name, slot)
             offsets = own_list[:, j0 // GROUP : j1 // GROUP]
             nc.vector.tensor_tensor(part[:], c_rows[:].indirect(offsets), added[:, j0:j1], ADD)
             return part
@@ -154,18 +174,19 @@ def tile_picked_ivfpq_none_p_kernel(tc, x_words, x_scales, w1, w2, dn, qn, offs,
             piece = product(w1_q0, cent_words, cent_plane, v0, v1, f"c_piece{v0}", bank_slot)
             nc.scalar.copy(c_rows0[:, v0:v1], piece[:])
         last_piece = product(w1_q0, cent_words, cent_plane, V - QUARTER, V, "c_last_piece", "r_bank0")
+        w1_q1 = quantize(w1_grouped1, "w1_q1", "w1_q1_codes")
         nc.vector.tensor_copy(c_rows0[:, V - QUARTER : V], last_piece[:])
-        w1_q2 = quantize(w1_grouped2, "w1_q2", "w1_grouped1")
+        w1_q2 = quantize(w1_grouped2, "w1_q2", 5 * RAW)
         part0 = look_up(c_rows0, dn_rows, 0, S, "part0", "part0")
 
-        w1_q3 = quantize(interleave(w1_raw3, "w1_grouped3", "w1_q0_codes"), "w1_q3", "w1_q3_codes")
         c_bank1 = centres(1, w1_q1)
+        w1_q3 = quantize(interleave(w1_raw3, "w1_grouped3", 5 * RAW + RAW // 4), "w1_q3", "w1_q3_codes")
         c_rows1 = keep.tile([P, V + SPARE], F32, name="c_rows1", align_bytes=64)
         nc.gpsimd.memset(c_rows1[:, V:], 0.0)
         nc.scalar.copy(c_rows1[:, :V], c_bank1[:])
         part1 = look_up(c_rows1, dn_rows, 0, S, "part1", "part1")
-        w2_q3 = quantize(interleave(w2_raw3, "w2_grouped3", "w1_q1_codes"), "w2_q3", "w2_q3_codes")
-        w2_q2 = quantize(interleave(w2_raw2, "w2_grouped2", "w2_grouped2"), "w2_q2", "w2_q2_codes")
+        w2_q3 = quantize(interleave(w2_raw3, "w2_grouped3", RAW // 2), "w2_q3", "w2_q3_codes")
+        w2_q2 = quantize(interleave(w2_raw2, "w2_grouped2", 0), "w2_q2", "w2_q2_codes")
         c_bank2 = centres(2, w1_q2)
         c_rows2 = keep.tile([P, V], F32, name="c_rows2", tag="c_rows2", align_bytes=64)
         nc.scalar.copy(c_rows2[:], c_bank2[:])
@@ -174,8 +195,8 @@ def tile_picked_ivfpq_none_p_kernel(tc, x_words, x_scales, w1, w2, dn, qn, offs,
 
         part2a = look_up(c_rows2, dn_rows, 0, HALF, "part2a", "part2a")
         w2_q0 = quantize(interleave(w2_raw0, "w2_grouped0", "w1_q2_scales"), "w2_q0", "w2_q0_codes")
-        part2b = look_up(c_rows2, dn_rows, HALF, S, "part2b", "w2_raw0")
-        w2_q1 = quantize(interleave(w2_raw1, "w2_grouped1", "w1_q1_scales"), "w2_q1", "w2_q1_codes")
+        part2b = look_up(c_rows2, dn_rows, HALF, S, "part2b", 7 * RAW // 2)
+        w2_q1 = quantize(interleave(w2_raw1, "w2_grouped1", 5 * RAW // 2), "w2_q1", "w2_q1_codes")
 
         r_rows3 = keep.tile([P, S], F32, name="r_rows3", align_bytes=64)
         nc.scalar.activation(r_rows3[:], r_bank3[:], IDENTITY, bias=qn_last[:])
@@ -185,7 +206,7 @@ def tile_picked_ivfpq_none_p_kernel(tc, x_words, x_scales, w1, w2, dn, qn, offs,
         nc.scalar.copy(c_rows3[:], centres(3, w1_q3)[:])
 
         for part, j0 in ((part2a, 0), (part2b, HALF)):
-            result2 = reused.tile([P, HALF], F32, name=f"result2_{j0}", offset=j0 * 4, align_bytes=64)
+            result2 = reused.tile([P, HALF], F32, name=f"result2_{j0}", offset=8 * RAW + RAW // 2 + j0 * 4, align_bytes=64)
             finish(2, result2, r_bank2, part, j0, j0 + HALF)
         for t, quantized, part in ((0, w2_q0, part0), (1, w2_q1, part1)):
             r_bank = rests(t, quantized)

@@ -85,24 +85,22 @@ def tile_picked_ivfpq_none_p_kernel(tc, x_words, x_scales, w1, w2, dn, qn, offs,
         own_list = keep.tile([P, S // GROUP], U16, name="own_list")
         nc.sync.dma_start(cent_list[:], cent)
 
-        scale_table = place([P, T], U8, "scale_table", 3 * RAW)
+        scale_table = place([P, T], U8, "scale_table", "scale_table")
         nc.sync.dma_start(
             out=scale_table[:].bitcast(I32),
             in_=x_scales[0].bitcast(I32).unsqueeze(1).to_broadcast([K // 32, BLOCK, T // 4]),
         )
         nc.sync.dma_start(offs_list[:], offs)
         nc.sync.dma_start(own_list[:], own)
-        norm_rows = keep.tile([P, P], F32, name="norm_rows", align_bytes=64)
+        norm_rows = place([P, P], F32, "norm_rows", 12 * RAW - 2 * P)
         nc.gpsimd.memset(norm_rows[:], 0.0)
         nc.sync.dma_start(out=norm_rows[:M_TILES, :], in_=qn.rearrange("(t p) o -> t (p o)", p=P))
         nc.sync.dma_start(out=norm_rows[M_TILES : 2 * M_TILES, :], in_=dn[0].rearrange("(t p) -> t p", p=P))
-        w1_raw0 = load_weight(raw_tile("w1_raw0", RAW // 2), w1, 0)
         word_table = keep.tile([P, T], I32, name="word_table", align_bytes=64)
         nc.sync.dma_start(out=word_table[:], in_=x_words[0].rearrange("p n t -> p (n t)").bitcast(I32))
-        w1_raw1 = load_weight(raw_tile("w1_raw1", 8 * RAW - RAW // 4), w1, 1)
+        w1_raw0 = load_weight(raw_tile("w1_raw0", "w1_raw0"), w1, 0)
+        w1_raw1 = load_weight(raw_tile("w1_raw1", 15 * RAW // 2), w1, 1)
 
-        w1_raw2 = load_weight(raw_tile("w1_raw2", "w1_raw2"), w1, 2)
-        w1_grouped0 = interleave(w1_raw0, "w1_grouped0", "w1_grouped0")
         identity = reused.tile([P, P], F32, name="identity", offset=5 * RAW - 2 * P, align_bytes=64)
         make_identity(nc, identity[:])
         qn_bank = psum.tile([P, P], F32, name="qn_bank", tag="r_bank3")
@@ -110,7 +108,7 @@ def tile_picked_ivfpq_none_p_kernel(tc, x_words, x_scales, w1, w2, dn, qn, offs,
         dn_rows = keep.tile([P, S], F32, name="dn_rows", align_bytes=64)
         for half, bank_slot in enumerate(("r_bank1", "c_bank1")):
             dn_bank = psum.tile([P, HALF], F32, name=f"dn_bank{half}", tag=bank_slot)
-            dn_cols = place([P, 2 * PAD], F32, f"dn_cols{half}", f"dn_cols{half}")
+            dn_cols = place([P, 2 * PAD], F32, f"dn_cols{half}", 7 * RAW // 2 - 4 * PAD if half else "dn_cols0")
             for i in range(2):
                 jt = 2 * half + i
                 nc.scalar.copy(dn_cols[:, PAD * i : PAD * i + 1], qn_bank[:, M_TILES + jt : M_TILES + jt + 1])
@@ -133,24 +131,25 @@ def tile_picked_ivfpq_none_p_kernel(tc, x_words, x_scales, w1, w2, dn, qn, offs,
         nc.vector.tensor_copy(cent_bytes[:], scale_table[:].indirect(cent_list[:]))
         cent_plane = keep.tile([P, V], U8, name="cent_plane", align_bytes=64)
         move_rows(cent_plane, cent_bytes)
-        w1_q0 = quantize(w1_grouped0, "w1_q0", "w1_q0_codes")
         offs_bytes = place([P, S], U8, "offs_bytes", "offs_bytes")
         nc.vector.tensor_copy(offs_bytes[:], scale_table[:].indirect(offs_list[:]))
 
-        w1_raw3 = load_weight(raw_tile("w1_raw3", 0), w1, 3)
-        w2_raw3 = load_weight(raw_tile("w2_raw3", RAW), w2, 3)
-        w2_raw2 = load_weight(raw_tile("w2_raw2", 5 * RAW // 2), w2, 2)
-        w2_raw0 = load_weight(raw_tile("w2_raw0", 7 * RAW // 2), w2, 0)
+        w1_raw2 = load_weight(raw_tile("w1_raw2", 12 * RAW), w1, 2)
+        w1_raw3 = load_weight(raw_tile("w1_raw3", 11 * RAW), w1, 3)
+        w2_raw3 = load_weight(raw_tile("w2_raw3", 5 * RAW // 2), w2, 3)
+        w2_raw2 = load_weight(raw_tile("w2_raw2", 7 * RAW // 2), w2, 2)
 
         cent_words = keep.tile([P, V], U32, name="cent_words", align_bytes=64)
         nc.vector.tensor_copy(cent_words[:], word_table[:].bitcast(U32).indirect(cent_list[:]))
-        offs_words = keep.tile([P, S], U32, name="offs_words", align_bytes=64)
+        w1_q0 = quantize(interleave(w1_raw0, "w1_grouped0", 5 * RAW), "w1_q0", "w1_q0_codes")
+        offs_words = keep.tile([P, S], U32, name="offs_words", tag="w1_raw0", align_bytes=64)
         nc.vector.tensor_copy(offs_words[:], word_table[:].bitcast(U32).indirect(offs_list[:]))
-        w1_grouped1 = interleave(w1_raw1, "w1_grouped1", 5 * RAW)
-        w2_raw1 = load_weight(raw_tile("w2_raw1", 8 * RAW + RAW // 2), w2, 1)
-        offs_plane = place([P, S], U8, "offs_plane", 8 * RAW)
+        w1_grouped1 = interleave(w1_raw1, "w1_grouped1", 9 * RAW // 2)
+        w2_raw0 = load_weight(raw_tile("w2_raw0", 27 * RAW // 4), w2, 0)
+        w2_raw1 = load_weight(raw_tile("w2_raw1", 33 * RAW // 4), w2, 1)
+        offs_plane = place([P, S], U8, "offs_plane", 31 * RAW // 4)
         move_rows(offs_plane, offs_bytes)
-        w1_grouped2 = interleave(w1_raw2, "w1_grouped2", 9 * RAW // 2)
+        w1_grouped2 = interleave(w1_raw2, "w1_grouped2", 21 * RAW // 4)
 
         def centres(t, quantized):
             return product(quantized, cent_words, cent_plane, 0, V, f"c_bank{t}", f"c_bank{t}")
@@ -176,37 +175,37 @@ def tile_picked_ivfpq_none_p_kernel(tc, x_words, x_scales, w1, w2, dn, qn, offs,
         last_piece = product(w1_q0, cent_words, cent_plane, V - QUARTER, V, "c_last_piece", "r_bank0")
         w1_q1 = quantize(w1_grouped1, "w1_q1", "w1_q1_codes")
         nc.vector.tensor_copy(c_rows0[:, V - QUARTER : V], last_piece[:])
-        w1_q2 = quantize(w1_grouped2, "w1_q2", 5 * RAW)
+        w1_q2 = quantize(w1_grouped2, "w1_q2", 9 * RAW // 2)
         part0 = look_up(c_rows0, dn_rows, 0, S, "part0", "part0")
 
         c_bank1 = centres(1, w1_q1)
-        w1_q3 = quantize(interleave(w1_raw3, "w1_grouped3", 5 * RAW + RAW // 4), "w1_q3", "w1_q3_codes")
-        c_rows1 = keep.tile([P, V + SPARE], F32, name="c_rows1", align_bytes=64)
+        w1_q3 = quantize(interleave(w1_raw3, "w1_grouped3", "w1_q0_codes"), "w1_q3", "w1_q3_codes")
+        c_rows1 = place([P, V + SPARE], F32, "c_rows1", 10 * RAW)
         nc.gpsimd.memset(c_rows1[:, V:], 0.0)
         nc.scalar.copy(c_rows1[:, :V], c_bank1[:])
         part1 = look_up(c_rows1, dn_rows, 0, S, "part1", "part1")
-        w2_q3 = quantize(interleave(w2_raw3, "w2_grouped3", RAW // 2), "w2_q3", "w2_q3_codes")
-        w2_q2 = quantize(interleave(w2_raw2, "w2_grouped2", 0), "w2_q2", "w2_q2_codes")
+        w2_q3 = quantize(interleave(w2_raw3, "w2_grouped3", 11 * RAW + RAW // 8), "w2_q3", "w2_q3_codes")
+        w2_q2 = quantize(interleave(w2_raw2, "w2_grouped2", 11 * RAW + 5 * RAW // 8), "w2_q2", "w2_q2_codes")
         c_bank2 = centres(2, w1_q2)
-        c_rows2 = keep.tile([P, V], F32, name="c_rows2", tag="c_rows2", align_bytes=64)
+        c_rows2 = place([P, V], F32, "c_rows2", 2 * RAW)
         nc.scalar.copy(c_rows2[:], c_bank2[:])
         r_bank3 = rests(3, w2_q3)
         r_bank2 = rests(2, w2_q2)
 
         part2a = look_up(c_rows2, dn_rows, 0, HALF, "part2a", "part2a")
-        w2_q0 = quantize(interleave(w2_raw0, "w2_grouped0", "w1_q2_scales"), "w2_q0", "w2_q0_codes")
-        part2b = look_up(c_rows2, dn_rows, HALF, S, "part2b", 7 * RAW // 2)
-        w2_q1 = quantize(interleave(w2_raw1, "w2_grouped1", 5 * RAW // 2), "w2_q1", "w2_q1_codes")
+        w2_q0 = quantize(interleave(w2_raw0, "w2_grouped0", 4 * RAW), "w2_q0", "w2_q0_codes")
+        part2b = look_up(c_rows2, dn_rows, HALF, S, "part2b", 7 * RAW)
+        w2_q1 = quantize(interleave(w2_raw1, "w2_grouped1", 7 * RAW // 2), "w2_q1", "w2_q1_codes")
 
-        r_rows3 = keep.tile([P, S], F32, name="r_rows3", align_bytes=64)
+        r_rows3 = place([P, S], F32, "r_rows3", 6 * RAW)
         nc.scalar.activation(r_rows3[:], r_bank3[:], IDENTITY, bias=qn_last[:])
-        r_dn3 = keep.tile([P, S], F32, name="r_dn3", tag="c_rows2", align_bytes=64)
+        r_dn3 = place([P, S], F32, "r_dn3", 2 * RAW)
         nc.gpsimd.tensor_tensor(r_dn3[:], r_rows3[:], dn_rows[:], ADD)
         c_rows3 = keep.tile([P, V], F32, name="c_rows3", tag="qn_last", align_bytes=64)
         nc.scalar.copy(c_rows3[:], centres(3, w1_q3)[:])
 
         for part, j0 in ((part2a, 0), (part2b, HALF)):
-            result2 = reused.tile([P, HALF], F32, name=f"result2_{j0}", offset=8 * RAW + RAW // 2 + j0 * 4, align_bytes=64)
+            result2 = reused.tile([P, HALF], F32, name=f"result2_{j0}", offset=33 * RAW // 4 + j0 * 4, align_bytes=64)
             finish(2, result2, r_bank2, part, j0, j0 + HALF)
         for t, quantized, part in ((0, w2_q0, part0), (1, w2_q1, part1)):
             r_bank = rests(t, quantized)

@@ -101,6 +101,7 @@ def tile_picked_ivfpq_none_p_kernel(tc, x_words, x_scales, w1, w2, dn, qn, offs,
         w1_raw0 = load_weight(raw_tile("w1_raw0", "w1_raw0"), w1, 0)
         w1_raw1 = load_weight(raw_tile("w1_raw1", 15 * RAW // 2), w1, 1)
 
+        w1_raw2 = load_weight(raw_tile("w1_raw2", "w1_raw2"), w1, 2)
         identity = reused.tile([P, P], F32, name="identity", offset=5 * RAW - 2 * P, align_bytes=64)
         make_identity(nc, identity[:])
         qn_bank = psum.tile([P, P], F32, name="qn_bank", tag="r_bank3")
@@ -134,7 +135,6 @@ def tile_picked_ivfpq_none_p_kernel(tc, x_words, x_scales, w1, w2, dn, qn, offs,
         offs_bytes = place([P, S], U8, "offs_bytes", "offs_bytes")
         nc.vector.tensor_copy(offs_bytes[:], scale_table[:].indirect(offs_list[:]))
 
-        w1_raw2 = load_weight(raw_tile("w1_raw2", 12 * RAW), w1, 2)
         w1_raw3 = load_weight(raw_tile("w1_raw3", 11 * RAW), w1, 3)
         w2_raw3 = load_weight(raw_tile("w2_raw3", 5 * RAW // 2), w2, 3)
         w2_raw2 = load_weight(raw_tile("w2_raw2", 7 * RAW // 2), w2, 2)

@@ -99,9 +99,9 @@ def tile_picked_ivfpq_none_p_kernel(tc, x_words, x_scales, w1, w2, dn, qn, offs,
         word_table = keep.tile([P, T], I32, name="word_table", align_bytes=64)
         nc.sync.dma_start(out=word_table[:], in_=x_words[0].rearrange("p n t -> p (n t)").bitcast(I32))
         w1_raw0 = load_weight(raw_tile("w1_raw0", "w1_raw0"), w1, 0)
-        w1_raw1 = load_weight(raw_tile("w1_raw1", 15 * RAW // 2), w1, 1)
+        w1_raw1 = load_weight(raw_tile("w1_raw1", "w1_raw1"), w1, 1)
 
-        w1_raw2 = load_weight(raw_tile("w1_raw2", "w1_raw2"), w1, 2)
+        w1_raw2 = load_weight(raw_tile("w1_raw2", 15 * RAW // 2), w1, 2)
         identity = reused.tile([P, P], F32, name="identity", offset=5 * RAW - 2 * P, align_bytes=64)
         make_identity(nc, identity[:])
         qn_bank = psum.tile([P, P], F32, name="qn_bank", tag="r_bank3")
@@ -142,20 +142,39 @@ def tile_picked_ivfpq_none_p_kernel(tc, x_words, x_scales, w1, w2, dn, qn, offs,
         cent_words = keep.tile([P, V], U32, name="cent_words", align_bytes=64)
         nc.vector.tensor_copy(cent_words[:], word_table[:].bitcast(U32).indirect(cent_list[:]))
         w1_q0 = quantize(interleave(w1_raw0, "w1_grouped0", 5 * RAW), "w1_q0", "w1_q0_codes")
-        offs_words = keep.tile([P, S], U32, name="offs_words", tag="w1_raw0", align_bytes=64)
-        nc.vector.tensor_copy(offs_words[:], word_table[:].bitcast(U32).indirect(offs_list[:]))
-        w1_grouped1 = interleave(w1_raw1, "w1_grouped1", 9 * RAW // 2)
+
+        def gather_offs_words(j0, slot):
+            words = place([P, HALF], U32, f"offs_words{j0}", slot)
+            offsets = offs_list[:, j0 // GROUP : (j0 + HALF) // GROUP]
+            nc.vector.tensor_copy(words[:], word_table[:].bitcast(U32).indirect(offsets))
+            return words
+
+        offs_words_a = gather_offs_words(0, "w1_raw0")
+        w1_q1 = quantize(interleave(w1_raw1, "w1_grouped1", 9 * RAW // 2), "w1_q1", "w1_q1_codes")
+        offs_words_b = gather_offs_words(HALF, "w1_raw1")
+        w1_grouped2 = interleave(w1_raw2, "w1_grouped2", 21 * RAW // 4)
         w2_raw0 = load_weight(raw_tile("w2_raw0", 27 * RAW // 4), w2, 0)
         w2_raw1 = load_weight(raw_tile("w2_raw1", 33 * RAW // 4), w2, 1)
         offs_plane = place([P, S], U8, "offs_plane", 31 * RAW // 4)
         move_rows(offs_plane, offs_bytes)
-        w1_grouped2 = interleave(w1_raw2, "w1_grouped2", 21 * RAW // 4)
 
         def centres(t, quantized):
             return product(quantized, cent_words, cent_plane, 0, V, f"c_bank{t}", f"c_bank{t}")
 
         def rests(t, quantized):
-            return product(quantized, offs_words, offs_plane, 0, S, f"r_bank{t}", f"r_bank{t}")
+            codes, scales = quantized
+            bank = psum.tile([P, S], F32, name=f"r_bank{t}", tag=f"r_bank{t}")
+            for words, j0 in ((offs_words_a, 0), (offs_words_b, HALF)):
+                nc.tensor.matmul_mx(
+                    out=bank[:, j0 : j0 + HALF],
+                    lhsT=codes[:].bitcast(FP8X4),
+                    lhsT_scale=scales[:],
+                    rhs=words[:].bitcast(FP8X4),
+                    rhs_scale=offs_plane[:, j0 : j0 + HALF],
+                    start=True,
+                    stop=True,
+                )
+            return bank
 
         def look_up(c_rows, added, j0, j1, name, slot):
             part = place([P, j1 - j0], F32, name, slot)
@@ -173,9 +192,8 @@ def tile_picked_ivfpq_none_p_kernel(tc, x_words, x_scales, w1, w2, dn, qn, offs,
             piece = product(w1_q0, cent_words, cent_plane, v0, v1, f"c_piece{v0}", bank_slot)
             nc.scalar.copy(c_rows0[:, v0:v1], piece[:])
         last_piece = product(w1_q0, cent_words, cent_plane, V - QUARTER, V, "c_last_piece", "r_bank0")
-        w1_q1 = quantize(w1_grouped1, "w1_q1", "w1_q1_codes")
         nc.vector.tensor_copy(c_rows0[:, V - QUARTER : V], last_piece[:])
-        w1_q2 = quantize(w1_grouped2, "w1_q2", 9 * RAW // 2)
+        w1_q2 = quantize(w1_grouped2, "w1_q2", "w1_q0_scales")
         part0 = look_up(c_rows0, dn_rows, 0, S, "part0", "part0")
 
         c_bank1 = centres(1, w1_q1)

@@ -103,7 +103,8 @@ def tile_picked_ivfpq_none_p_kernel(tc, x_words, x_scales, w1, w2, dn, qn, offs,
 
         w1_raw2 = load_weight(raw_tile("w1_raw2", 15 * RAW // 2), w1, 2)
         identity = reused.tile([P, P], F32, name="identity", offset=5 * RAW - 2 * P, align_bytes=64)
-        make_identity(nc, identity[:])
+        nc.vector.memset(identity[:], 0.0)
+        make_identity(nc, identity[:], nomemset=True)
         qn_bank = psum.tile([P, P], F32, name="qn_bank", tag="r_bank3")
         nc.tensor.transpose(qn_bank[:], norm_rows[:], identity[:])
         dn_rows = keep.tile([P, S], F32, name="dn_rows", align_bytes=64)
@@ -120,8 +121,8 @@ def tile_picked_ivfpq_none_p_kernel(tc, x_words, x_scales, w1, w2, dn, qn, offs,
         qn_last = keep.tile([P, 1], F32, name="qn_last", tag="qn_last", align_bytes=64)
         nc.scalar.copy(qn_last[:], qn_bank[:, LAST:M_TILES])
 
-        def move_rows(plane, gathered):
-            nc.gpsimd.memset(plane[:].bitcast(I32), 0)
+        def move_rows(plane, gathered, clearing_engine):
+            clearing_engine.memset(plane[:].bitcast(I32), 0)
             for i in range(4):
                 nc.sync.dma_start(
                     out=plane[:].bitcast(I32)[i:P:QUADRANT, :],
@@ -131,7 +132,7 @@ def tile_picked_ivfpq_none_p_kernel(tc, x_words, x_scales, w1, w2, dn, qn, offs,
         cent_bytes = keep.tile([P, V], U8, name="cent_bytes", align_bytes=64)
         nc.vector.tensor_copy(cent_bytes[:], scale_table[:].indirect(cent_list[:]))
         cent_plane = keep.tile([P, V], U8, name="cent_plane", align_bytes=64)
-        move_rows(cent_plane, cent_bytes)
+        move_rows(cent_plane, cent_bytes, nc.vector)
         offs_bytes = place([P, S], U8, "offs_bytes", "offs_bytes")
         nc.vector.tensor_copy(offs_bytes[:], scale_table[:].indirect(offs_list[:]))
 
@@ -156,7 +157,7 @@ def tile_picked_ivfpq_none_p_kernel(tc, x_words, x_scales, w1, w2, dn, qn, offs,
         w2_raw0 = load_weight(raw_tile("w2_raw0", 27 * RAW // 4), w2, 0)
         w2_raw1 = load_weight(raw_tile("w2_raw1", 33 * RAW // 4), w2, 1)
         offs_plane = place([P, S], U8, "offs_plane", 31 * RAW // 4)
-        move_rows(offs_plane, offs_bytes)
+        move_rows(offs_plane, offs_bytes, nc.gpsimd)
 
         def centres(t, quantized):
             return product(quantized, cent_words, cent_plane, 0, V, f"c_bank{t}", f"c_bank{t}")
@@ -187,7 +188,7 @@ def tile_picked_ivfpq_none_p_kernel(tc, x_words, x_scales, w1, w2, dn, qn, offs,
             nc.sync.dma_start(out=out[t * P : (t + 1) * P, j0:j1], in_=result[:])
 
         c_rows0 = keep.tile([P, V + SPARE], F32, name="c_rows0", align_bytes=64)
-        nc.gpsimd.memset(c_rows0[:, V:], 0.0)
+        nc.vector.memset(c_rows0[:, V:], 0.0)
         for v0, v1, bank_slot in ((0, HALF, "c_bank0"), (HALF, V - QUARTER, "r_bank2")):
             piece = product(w1_q0, cent_words, cent_plane, v0, v1, f"c_piece{v0}", bank_slot)
             nc.scalar.copy(c_rows0[:, v0:v1], piece[:])

@@ -14,223 +14,232 @@ U16 = mybir.dt.uint16
 U8 = mybir.dt.uint8
 FP8X4 = mybir.dt.float8_e4m3fn_x4
 ADD = mybir.AluOpType.add
+MULT = mybir.AluOpType.mult
 IDENTITY = mybir.ActivationFunctionType.Identity
+COPY = mybir.ActivationFunctionType.Copy
 
 P = 128
 PACK = 4
 GROUP = 16
 BLOCK = 8
-RAW = PACK * P * 4
-PAD = 16
 QUADRANT = 32
 LINE = 4
+PAD = 16
 M_TILES = N // P
-LAST = M_TILES - 1
 SPARE = 16
 HALF = S // 2
 QUARTER = S // 4
+OVERLAP = 64
+LEAD = 4096
+CHAIN = 16384
+BYTES_OF = {F32: 4, BF16: 2, U32: 4, U8: 1, I32: 4}
 
 
 def tile_picked_ivfpq_none_p_kernel(tc, x_words, x_scales, w1, w2, dn, qn, offs, cent, own, out):
     nc = tc.nc
     with ExitStack() as ctx:
         keep = ctx.enter_context(tc.tile_pool(name="keep", bufs=1))
-        reused = ctx.enter_context(tc.tile_pool(name="reused", bufs=1))
+        shared = ctx.enter_context(tc.tile_pool(name="shared", bufs=1))
         psum = ctx.enter_context(tc.psum_pool(name="psum", bufs=1))
+        spans = {}
+        chains = []
 
-        def place(shape, dtype, name, slot):
-            if isinstance(slot, str):
-                return keep.tile(shape, dtype, name=name, tag=slot, align_bytes=64)
-            return reused.tile(shape, dtype, name=name, offset=slot, align_bytes=64)
+        def place(shape, dtype, name, behind=None, ahead=None, inside=None, first=False):
+            size = BYTES_OF[dtype]
+            for extent in shape[1:]:
+                size = size * extent
+            if first:
+                offset = len(chains) * CHAIN + LEAD
+                chains.append(name)
+            elif behind:
+                offset = spans[behind][1] - OVERLAP
+            elif inside:
+                offset = spans[inside][0] + 16 * OVERLAP
+            elif ahead:
+                offset = spans[ahead][0] + OVERLAP - size
+            else:
+                return keep.tile(shape, dtype, name=name, align_bytes=64)
+            spans[name] = (offset, offset + size)
+            return shared.tile(shape, dtype, name=name, offset=offset, align_bytes=64)
 
-        def load_weight(raw, w, t):
-            nc.sync.dma_start(out=raw[:], in_=w[:, t * P : (t + 1) * P].rearrange("(p j) m -> p j m", j=PACK))
+        def load_weight(w, t, tiles, name, **where):
+            raw = place([P, PACK, tiles * P], F32, name, **where)
+            nc.sync.dma_start(out=raw[:], in_=w[:, t * P : (t + tiles) * P].rearrange("(p j) m -> p j m", j=PACK))
             return raw
 
-        def raw_tile(name, offset):
-            return place([P, PACK, P], F32, name, offset)
+        def grouped_tile(name, tiles=1, **where):
+            return place([P, tiles * P * PACK], BF16, name, **where)
 
-        def interleave(raw, name, slot):
-            grouped = place([P, P, PACK], BF16, name, slot)
-            nc.scalar.activation(
-                grouped[:].rearrange("p (c i) j -> p c j i", i=LINE),
-                raw[:].rearrange("p j (c i) -> p c j i", i=LINE),
-                IDENTITY,
-                scale=-2.0,
-            )
+        def interleave(engine, raw, grouped):
+            target = grouped[:].rearrange("p (c i j) -> p c j i", i=LINE, j=PACK)
+            source = raw[:].rearrange("p j (c i) -> p c j i", i=LINE)
+            if engine == "vector":
+                nc.vector.tensor_copy(target, source)
+            else:
+                nc.scalar.activation(target, source, COPY)
             return grouped
 
-        def quantize(grouped, name, codes_slot, scales_slot=None):
-            codes = place([P, P], U32, name + "_codes", codes_slot)
-            scales = keep.tile([P, P], U8, name=name + "_scales", tag=scales_slot or name + "_scales", align_bytes=64)
-            nc.vector.quantize_mx(out=codes[:].bitcast(FP8X4), scales=scales[:], in_=grouped[:].rearrange("p m j -> p (m j)"))
-            return codes, scales
+        def quantize(grouped, name, **where):
+            columns = grouped.shape[1] // PACK
+            codes = place([P, columns], U32, name + "_codes", **where)
+            scales = place([P, columns], U8, name + "_scales")
+            nc.vector.quantize_mx(out=codes[:].bitcast(FP8X4), scales=scales[:], in_=grouped[:])
+            return [(codes[:, c : c + P], scales[:, c : c + P]) for c in range(0, columns, P)]
 
-        def product(quantized, words, plane, c0, c1, name, bank_slot):
+        def multiply(bank, quantized, words, plane):
             codes, scales = quantized
-            bank = psum.tile([P, c1 - c0], F32, name=name, tag=bank_slot)
             nc.tensor.matmul_mx(
-                out=bank[:],
-                lhsT=codes[:].bitcast(FP8X4),
-                lhsT_scale=scales[:],
-                rhs=words[:, c0:c1].bitcast(FP8X4),
-                rhs_scale=plane[:, c0:c1],
+                out=bank,
+                lhsT=codes.bitcast(FP8X4),
+                lhsT_scale=scales,
+                rhs=words.bitcast(FP8X4),
+                rhs_scale=plane,
                 start=True,
                 stop=True,
             )
-            return bank
+
+        def offsets(tile, j0, j1):
+            return tile[:, j0 // GROUP : j1 // GROUP]
 
         cent_list = keep.tile([P, V // GROUP], U16, name="cent_list")
         offs_list = keep.tile([P, S // GROUP], U16, name="offs_list")
         own_list = keep.tile([P, S // GROUP], U16, name="own_list")
         nc.sync.dma_start(cent_list[:], cent)
-
-        scale_table = place([P, T], U8, "scale_table", "scale_table")
+        scale_table = place([P, T], U8, "scale_table")
         nc.sync.dma_start(
             out=scale_table[:].bitcast(I32),
             in_=x_scales[0].bitcast(I32).unsqueeze(1).to_broadcast([K // 32, BLOCK, T // 4]),
         )
         nc.sync.dma_start(offs_list[:], offs)
         nc.sync.dma_start(own_list[:], own)
-        norm_rows = place([P, P], F32, "norm_rows", 12 * RAW - 2 * P)
+        norm_rows = place([P, P], F32, "norm_rows", first=True)
         nc.gpsimd.memset(norm_rows[:], 0.0)
         nc.sync.dma_start(out=norm_rows[:M_TILES, :], in_=qn.rearrange("(t p) o -> t (p o)", p=P))
         nc.sync.dma_start(out=norm_rows[M_TILES : 2 * M_TILES, :], in_=dn[0].rearrange("(t p) -> t p", p=P))
-        word_table = keep.tile([P, T], I32, name="word_table", align_bytes=64)
+        word_table = place([P, T], I32, "word_table")
         nc.sync.dma_start(out=word_table[:], in_=x_words[0].rearrange("p n t -> p (n t)").bitcast(I32))
-        w1_raw0 = load_weight(raw_tile("w1_raw0", "w1_raw0"), w1, 0)
-        w1_raw1 = load_weight(raw_tile("w1_raw1", "w1_raw1"), w1, 1)
+        w1_raw0 = load_weight(w1, 0, 1, "w1_raw0", first=True)
+        w1_raw1 = load_weight(w1, 1, 1, "w1_raw1", first=True)
+        w1_raw2 = load_weight(w1, 2, 1, "w1_raw2")
 
-        w1_raw2 = load_weight(raw_tile("w1_raw2", 15 * RAW // 2), w1, 2)
-        identity = reused.tile([P, P], F32, name="identity", offset=5 * RAW - 2 * P, align_bytes=64)
+        identity = place([P, P], F32, "identity", first=True)
         nc.vector.memset(identity[:], 0.0)
         make_identity(nc, identity[:], nomemset=True)
         qn_bank = psum.tile([P, P], F32, name="qn_bank", tag="r_bank3")
         nc.tensor.transpose(qn_bank[:], norm_rows[:], identity[:])
-        dn_rows = keep.tile([P, S], F32, name="dn_rows", align_bytes=64)
-        for half, bank_slot in enumerate(("r_bank1", "c_bank1")):
+        dn_rows = place([P, S], F32, "dn_rows")
+        for half, bank_slot in enumerate(("r_bank1", "r_bank2")):
             dn_bank = psum.tile([P, HALF], F32, name=f"dn_bank{half}", tag=bank_slot)
-            dn_cols = place([P, 2 * PAD], F32, f"dn_cols{half}", 7 * RAW // 2 - 4 * PAD if half else "dn_cols0")
             for i in range(2):
                 jt = 2 * half + i
-                nc.scalar.copy(dn_cols[:, PAD * i : PAD * i + 1], qn_bank[:, M_TILES + jt : M_TILES + jt + 1])
-                nc.tensor.transpose(dn_bank[:, i * P : (i + 1) * P], dn_cols[:, PAD * i : PAD * i + 1].to_broadcast([P, P]), identity[:])
+                dn_col = place([P, 2 * PAD], F32, f"dn_col{jt}", first=jt < 2)
+                nc.scalar.copy(dn_col[:, :1], qn_bank[:, M_TILES + jt : M_TILES + jt + 1])
+                nc.tensor.transpose(dn_bank[:, i * P : (i + 1) * P], dn_col[:, :1].to_broadcast([P, P]), identity[:])
             nc.scalar.copy(dn_rows[:, half * HALF : (half + 1) * HALF], dn_bank[:])
-        qn_cols = keep.tile([P, LAST], F32, name="qn_cols", align_bytes=64)
-        nc.scalar.copy(qn_cols[:], qn_bank[:, :LAST])
-        qn_last = keep.tile([P, 1], F32, name="qn_last", tag="qn_last", align_bytes=64)
-        nc.scalar.copy(qn_last[:], qn_bank[:, LAST:M_TILES])
+        qn_first = place([P, 2 * PAD], F32, "qn_first", first=True)
+        nc.scalar.copy(qn_first[:, :1], qn_bank[:, :1])
+        qn_others = place([P, M_TILES - 1], F32, "qn_others")
+        nc.scalar.copy(qn_others[:], qn_bank[:, 1:M_TILES])
+        qn_cols = [qn_first[:, :1]] + [qn_others[:, i : i + 1] for i in range(M_TILES - 1)]
 
-        def move_rows(plane, gathered, clearing_engine):
-            clearing_engine.memset(plane[:].bitcast(I32), 0)
+        def move_rows(plane, gathered):
+            nc.vector.memset(plane[:].bitcast(I32), 0)
             for i in range(4):
                 nc.sync.dma_start(
                     out=plane[:].bitcast(I32)[i:P:QUADRANT, :],
                     in_=gathered[:].bitcast(I32)[BLOCK * i : P : QUADRANT, :],
                 )
 
-        cent_bytes = keep.tile([P, V], U8, name="cent_bytes", align_bytes=64)
+        c_rows0 = place([P, V + SPARE], F32, "c_rows0")
+        nc.vector.memset(c_rows0[:, V:], 0.0)
+
+        cent_bytes = place([P, V], U8, "cent_bytes")
         nc.vector.tensor_copy(cent_bytes[:], scale_table[:].indirect(cent_list[:]))
-        cent_plane = keep.tile([P, V], U8, name="cent_plane", align_bytes=64)
-        move_rows(cent_plane, cent_bytes, nc.vector)
-        offs_bytes = place([P, S], U8, "offs_bytes", "offs_bytes")
+        cent_plane = place([P, V], U8, "cent_plane")
+        move_rows(cent_plane, cent_bytes)
+        offs_bytes = place([P, S], U8, "offs_bytes")
         nc.vector.tensor_copy(offs_bytes[:], scale_table[:].indirect(offs_list[:]))
 
-        w1_raw3 = load_weight(raw_tile("w1_raw3", 11 * RAW), w1, 3)
-        w2_raw3 = load_weight(raw_tile("w2_raw3", 5 * RAW // 2), w2, 3)
-        w2_raw2 = load_weight(raw_tile("w2_raw2", 7 * RAW // 2), w2, 2)
+        w1_raw3 = load_weight(w1, 3, 1, "w1_raw3", ahead="norm_rows")
+        w2_raw01 = load_weight(w2, 0, 2, "w2_raw01", behind="norm_rows")
+        w2_raw23 = load_weight(w2, 2, 2, "w2_raw23", behind="dn_col0")
+        offs_plane = place([P, S], U8, "offs_plane", behind="dn_col1")
+        move_rows(offs_plane, offs_bytes)
 
-        cent_words = keep.tile([P, V], U32, name="cent_words", align_bytes=64)
-        nc.vector.tensor_copy(cent_words[:], word_table[:].bitcast(U32).indirect(cent_list[:]))
-        w1_q0 = quantize(interleave(w1_raw0, "w1_grouped0", 5 * RAW), "w1_q0", "w1_q0_codes")
-
-        def gather_offs_words(j0, slot):
-            words = place([P, HALF], U32, f"offs_words{j0}", slot)
-            offsets = offs_list[:, j0 // GROUP : (j0 + HALF) // GROUP]
-            nc.vector.tensor_copy(words[:], word_table[:].bitcast(U32).indirect(offsets))
+        def gather_words(index_list, j0, j1, name, **where):
+            words = place([P, j1 - j0], U32, name, **where)
+            nc.vector.tensor_copy(words[:], word_table[:].bitcast(U32).indirect(offsets(index_list, j0, j1)))
             return words
 
-        offs_words_a = gather_offs_words(0, "w1_raw0")
-        w1_q1 = quantize(interleave(w1_raw1, "w1_grouped1", 9 * RAW // 2), "w1_q1", "w1_q1_codes")
-        offs_words_b = gather_offs_words(HALF, "w1_raw1")
-        w1_grouped2 = interleave(w1_raw2, "w1_grouped2", 21 * RAW // 4)
-        w2_raw0 = load_weight(raw_tile("w2_raw0", 27 * RAW // 4), w2, 0)
-        w2_raw1 = load_weight(raw_tile("w2_raw1", 33 * RAW // 4), w2, 1)
-        offs_plane = place([P, S], U8, "offs_plane", 31 * RAW // 4)
-        move_rows(offs_plane, offs_bytes, nc.gpsimd)
-
-        def centres(t, quantized):
-            return product(quantized, cent_words, cent_plane, 0, V, f"c_bank{t}", f"c_bank{t}")
+        def centres(t, quantized, c_rows, v0, v1, bank_slot):
+            bank = psum.tile([P, v1 - v0], F32, name=f"c_bank{t}_{v0}", tag=bank_slot)
+            multiply(bank[:], quantized, cent_words[:, v0:v1], cent_plane[:, v0:v1])
+            nc.scalar.activation(c_rows[:, v0:v1], bank[:], IDENTITY, bias=qn_cols[t], scale=-2.0)
 
         def rests(t, quantized):
-            codes, scales = quantized
             bank = psum.tile([P, S], F32, name=f"r_bank{t}", tag=f"r_bank{t}")
             for words, j0 in ((offs_words_a, 0), (offs_words_b, HALF)):
-                nc.tensor.matmul_mx(
-                    out=bank[:, j0 : j0 + HALF],
-                    lhsT=codes[:].bitcast(FP8X4),
-                    lhsT_scale=scales[:],
-                    rhs=words[:].bitcast(FP8X4),
-                    rhs_scale=offs_plane[:, j0 : j0 + HALF],
-                    start=True,
-                    stop=True,
-                )
+                multiply(bank[:, j0 : j0 + HALF], quantized, words[:], offs_plane[:, j0 : j0 + HALF])
             return bank
 
-        def look_up(c_rows, added, j0, j1, name, slot):
-            part = place([P, j1 - j0], F32, name, slot)
-            offsets = own_list[:, j0 // GROUP : j1 // GROUP]
-            nc.vector.tensor_tensor(part[:], c_rows[:].indirect(offsets), added[:, j0:j1], ADD)
+        def look_up_add(c_rows, part, j0, j1):
+            nc.vector.tensor_tensor(part, c_rows[:].indirect(offsets(own_list, j0, j1)), dn_rows[:, j0:j1], ADD)
+
+        def look_up(c_rows, j0, name, **where):
+            part = place([P, HALF], F32, name, **where)
+            nc.scalar.activation(part[:], c_rows[:].indirect(offsets(own_list, j0, j0 + HALF)), COPY)
             return part
 
-        def finish(t, result, r_bank, part, j0, j1):
-            nc.vector.scalar_tensor_tensor(result[:], r_bank[:, j0:j1], qn_cols[:, t : t + 1], part[:], ADD, ADD)
-            nc.sync.dma_start(out=out[t * P : (t + 1) * P, j0:j1], in_=result[:])
+        def add_dn(total, part, j0):
+            nc.gpsimd.tensor_tensor(total, part[:], dn_rows[:, j0 : j0 + HALF], ADD)
 
-        c_rows0 = keep.tile([P, V + SPARE], F32, name="c_rows0", align_bytes=64)
-        nc.vector.memset(c_rows0[:, V:], 0.0)
-        for v0, v1, bank_slot in ((0, HALF, "c_bank0"), (HALF, V - QUARTER, "r_bank2")):
-            piece = product(w1_q0, cent_words, cent_plane, v0, v1, f"c_piece{v0}", bank_slot)
-            nc.scalar.copy(c_rows0[:, v0:v1], piece[:])
-        last_piece = product(w1_q0, cent_words, cent_plane, V - QUARTER, V, "c_last_piece", "r_bank0")
-        nc.vector.tensor_copy(c_rows0[:, V - QUARTER : V], last_piece[:])
-        w1_q2 = quantize(w1_grouped2, "w1_q2", "w1_q0_scales")
-        part0 = look_up(c_rows0, dn_rows, 0, S, "part0", "part0")
+        def finish(r_part, added, name, **where):
+            result = place([P, added.shape[1]], F32, name, **where)
+            nc.vector.scalar_tensor_tensor(result[:], r_part, -2.0, added, MULT, ADD)
+            return result
 
-        c_bank1 = centres(1, w1_q1)
-        w1_q3 = quantize(interleave(w1_raw3, "w1_grouped3", "w1_q0_codes"), "w1_q3", "w1_q3_codes")
-        c_rows1 = place([P, V + SPARE], F32, "c_rows1", 10 * RAW)
-        nc.gpsimd.memset(c_rows1[:, V:], 0.0)
-        nc.scalar.copy(c_rows1[:, :V], c_bank1[:])
-        part1 = look_up(c_rows1, dn_rows, 0, S, "part1", "part1")
-        w2_q3 = quantize(interleave(w2_raw3, "w2_grouped3", 11 * RAW + RAW // 8), "w2_q3", "w2_q3_codes")
-        w2_q2 = quantize(interleave(w2_raw2, "w2_grouped2", 11 * RAW + 5 * RAW // 8), "w2_q2", "w2_q2_codes")
-        c_bank2 = centres(2, w1_q2)
-        c_rows2 = place([P, V], F32, "c_rows2", 2 * RAW)
-        nc.scalar.copy(c_rows2[:], c_bank2[:])
-        r_bank3 = rests(3, w2_q3)
-        r_bank2 = rests(2, w2_q2)
+        def store(t, j0, j1, result):
+            nc.sync.dma_start(out=out[t * P : (t + 1) * P, j0:j1], in_=result)
 
-        part2a = look_up(c_rows2, dn_rows, 0, HALF, "part2a", "part2a")
-        w2_q0 = quantize(interleave(w2_raw0, "w2_grouped0", 4 * RAW), "w2_q0", "w2_q0_codes")
-        part2b = look_up(c_rows2, dn_rows, HALF, S, "part2b", 7 * RAW)
-        w2_q1 = quantize(interleave(w2_raw1, "w2_grouped1", 7 * RAW // 2), "w2_q1", "w2_q1_codes")
-
-        r_rows3 = place([P, S], F32, "r_rows3", 6 * RAW)
-        nc.scalar.activation(r_rows3[:], r_bank3[:], IDENTITY, bias=qn_last[:])
-        r_dn3 = place([P, S], F32, "r_dn3", 2 * RAW)
-        nc.gpsimd.tensor_tensor(r_dn3[:], r_rows3[:], dn_rows[:], ADD)
-        c_rows3 = keep.tile([P, V], F32, name="c_rows3", tag="qn_last", align_bytes=64)
-        nc.scalar.copy(c_rows3[:], centres(3, w1_q3)[:])
-
-        for part, j0 in ((part2a, 0), (part2b, HALF)):
-            result2 = reused.tile([P, HALF], F32, name=f"result2_{j0}", offset=33 * RAW // 4 + j0 * 4, align_bytes=64)
-            finish(2, result2, r_bank2, part, j0, j0 + HALF)
-        for t, quantized, part in ((0, w2_q0, part0), (1, w2_q1, part1)):
-            r_bank = rests(t, quantized)
-            result = keep.tile([P, S], F32, name=f"result{t}", align_bytes=64)
-            finish(t, result, r_bank, part, 0, S)
-
-        for j0, j1, slot in ((0, HALF, "w2_q1_codes"), (HALF, S - QUARTER, "w2_q1_scales"), (S - QUARTER, S, "w2_q0_scales")):
-            result3 = look_up(c_rows3, r_dn3, j0, j1, f"result3_{j0}", slot)
-            nc.sync.dma_start(out=out[LAST * P :, j0:j1], in_=result3[:])
+        cent_words = gather_words(cent_list, 0, V, "cent_words")
+        (w1_q0,) = quantize(interleave("scalar", w1_raw0, grouped_tile("w1_grouped0", behind="identity")), "w1_q0")
+        offs_words_a = gather_words(offs_list, 0, HALF, "offs_words_a", ahead="w1_raw0")
+        (w1_q1,) = quantize(interleave("scalar", w1_raw1, grouped_tile("w1_grouped1", ahead="identity")), "w1_q1")
+        offs_words_b = gather_words(offs_list, HALF, S, "offs_words_b", ahead="w1_raw1")
+        w1_grouped3 = interleave("vector", w1_raw3, grouped_tile("w1_grouped3", behind="w1_raw1"))
+        (w1_q2,) = quantize(interleave("scalar", w1_raw2, grouped_tile("w1_grouped2", behind="w1_grouped0")), "w1_q2")
+        (w1_q3,) = quantize(w1_grouped3, "w1_q3")
+        centres(0, w1_q0, c_rows0, 0, V, "c_bank0")
+        part0 = place([P, S], F32, "part0")
+        look_up_add(c_rows0, part0[:], 0, S)
+        c_rows1 = place([P, V], F32, "c_rows1")
+        centres(1, w1_q1, c_rows1, 0, V, "c_bank1")
+        w2_grouped01 = interleave("scalar", w2_raw01, grouped_tile("w2_grouped01", 2, ahead="qn_first"))
+        w2_grouped23 = interleave("vector", w2_raw23, grouped_tile("w2_grouped23", 2, behind="qn_first"))
+        c_rows2 = place([P, V], F32, "c_rows2")
+        centres(2, w1_q2, c_rows2, 0, V, "c_bank2")
+        c_rows3 = place([P, V], F32, "c_rows3")
+        centres(3, w1_q3, c_rows3, 0, V, "c_bank3")
+        w2_q0, w2_q1 = quantize(w2_grouped01, "w2_q01")
+        part1 = place([P, S], F32, "part1", behind="w2_raw01")
+        look_up_add(c_rows1, part1[:, :HALF], 0, HALF)
+        w2_q2, w2_q3 = quantize(w2_grouped23, "w2_q23", inside="w2_raw01")
+        look_up_add(c_rows1, part1[:, HALF:], HALF, S)
+        part2a = look_up(c_rows2, 0, "part2a")
+        part2b = look_up(c_rows2, HALF, "part2b")
+        part3a = look_up(c_rows3, 0, "part3a")
+        part3b = look_up(c_rows3, HALF, "part3b")
+        r_banks = [rests(t, quantized) for t, quantized in enumerate((w2_q0, w2_q1, w2_q2, w2_q3))]
+        sum2 = place([P, S], F32, "sum2", behind="w2_grouped23")
+        add_dn(sum2[:, :HALF], part2a, 0)
+        add_dn(sum2[:, HALF:], part2b, HALF)
+        sum3a = place([P, HALF], F32, "sum3a")
+        add_dn(sum3a[:], part3a, 0)
+        store(0, 0, S, finish(r_banks[0][:], part0[:], "result0", ahead="w2_grouped23")[:])
+        store(1, 0, S, finish(r_banks[1][:], part1[:], "result1")[:])
+        r_dn3b = finish(r_banks[3][:, HALF:], dn_rows[:, HALF:], "r_dn3b")
+        store(2, 0, S, finish(r_banks[2][:], sum2[:], "result2")[:])
+        store(3, 0, HALF, finish(r_banks[3][:, :HALF], sum3a[:], "result3a")[:])
+        result3b = place([P, HALF], F32, "result3b")
+        nc.vector.tensor_tensor(result3b[:], r_dn3b[:], part3b[:], ADD)
+        store(3, HALF, S, result3b[:])

@@ -31,7 +31,7 @@ HALF = S // 2
 QUARTER = S // 4
 OVERLAP = 64
 LEAD = 4096
-CHAIN = 16384
+CHAIN = 12288
 BYTES_OF = {F32: 4, BF16: 2, U32: 4, U8: 1, I32: 4}
 
 
@@ -120,7 +120,7 @@ def tile_picked_ivfpq_none_p_kernel(tc, x_words, x_scales, w1, w2, dn, qn, offs,
         nc.sync.dma_start(out=word_table[:], in_=x_words[0].rearrange("p n t -> p (n t)").bitcast(I32))
         w1_raw0 = load_weight(w1, 0, 1, "w1_raw0", first=True)
         w1_raw1 = load_weight(w1, 1, 1, "w1_raw1", first=True)
-        w1_raw2 = load_weight(w1, 2, 1, "w1_raw2")
+        w1_raw2 = load_weight(w1, 2, 1, "w1_raw2", first=True)
 
         identity = place([P, P], F32, "identity", first=True)
         nc.vector.memset(identity[:], 0.0)
@@ -136,11 +136,14 @@ def tile_picked_ivfpq_none_p_kernel(tc, x_words, x_scales, w1, w2, dn, qn, offs,
                 nc.scalar.copy(dn_col[:, :1], qn_bank[:, M_TILES + jt : M_TILES + jt + 1])
                 nc.tensor.transpose(dn_bank[:, i * P : (i + 1) * P], dn_col[:, :1].to_broadcast([P, P]), identity[:])
             nc.scalar.copy(dn_rows[:, half * HALF : (half + 1) * HALF], dn_bank[:])
-        qn_first = place([P, 2 * PAD], F32, "qn_first", first=True)
-        nc.scalar.copy(qn_first[:, :1], qn_bank[:, :1])
-        qn_others = place([P, M_TILES - 1], F32, "qn_others")
-        nc.scalar.copy(qn_others[:], qn_bank[:, 1:M_TILES])
-        qn_cols = [qn_first[:, :1]] + [qn_others[:, i : i + 1] for i in range(M_TILES - 1)]
+        qn_cols = []
+        for t in range(2):
+            qn_col = place([P, 2 * PAD], F32, f"qn_col{t}", first=True)
+            nc.scalar.copy(qn_col[:, :1], qn_bank[:, t : t + 1])
+            qn_cols.append(qn_col[:, :1])
+        qn_last = place([P, 2], F32, "qn_last")
+        nc.scalar.copy(qn_last[:], qn_bank[:, 2:M_TILES])
+        qn_cols.extend([qn_last[:, :1], qn_last[:, 1:]])
 
         def move_rows(plane, gathered):
             nc.vector.memset(plane[:].bitcast(I32), 0)
@@ -214,17 +217,18 @@ def tile_picked_ivfpq_none_p_kernel(tc, x_words, x_scales, w1, w2, dn, qn, offs,
         look_up_add(c_rows0, part0[:], 0, S)
         c_rows1 = place([P, V], F32, "c_rows1")
         centres(1, w1_q1, c_rows1, 0, V, "c_bank1")
-        w2_grouped01 = interleave("scalar", w2_raw01, grouped_tile("w2_grouped01", 2, ahead="qn_first"))
-        w2_grouped23 = interleave("vector", w2_raw23, grouped_tile("w2_grouped23", 2, behind="qn_first"))
+        part1a = place([P, HALF], F32, "part1a")
+        look_up_add(c_rows1, part1a[:], 0, HALF)
+        w2_grouped01 = interleave("scalar", w2_raw01, grouped_tile("w2_grouped01", 2, ahead="qn_col0"))
         c_rows2 = place([P, V], F32, "c_rows2")
         centres(2, w1_q2, c_rows2, 0, V, "c_bank2")
+        w2_grouped23 = interleave("vector", w2_raw23, grouped_tile("w2_grouped23", 2, behind="qn_col1"))
         c_rows3 = place([P, V], F32, "c_rows3")
         centres(3, w1_q3, c_rows3, 0, V, "c_bank3")
         w2_q0, w2_q1 = quantize(w2_grouped01, "w2_q01")
-        part1 = place([P, S], F32, "part1", behind="w2_raw01")
-        look_up_add(c_rows1, part1[:, :HALF], 0, HALF)
         w2_q2, w2_q3 = quantize(w2_grouped23, "w2_q23", inside="w2_raw01")
-        look_up_add(c_rows1, part1[:, HALF:], HALF, S)
+        part1b = place([P, HALF], F32, "part1b", behind="w2_raw01")
+        look_up_add(c_rows1, part1b[:], HALF, S)
         part2a = look_up(c_rows2, 0, "part2a")
         part2b = look_up(c_rows2, HALF, "part2b")
         part3a = look_up(c_rows3, 0, "part3a")
@@ -236,7 +240,8 @@ def tile_picked_ivfpq_none_p_kernel(tc, x_words, x_scales, w1, w2, dn, qn, offs,
         sum3a = place([P, HALF], F32, "sum3a")
         add_dn(sum3a[:], part3a, 0)
         store(0, 0, S, finish(r_banks[0][:], part0[:], "result0", ahead="w2_grouped23")[:])
-        store(1, 0, S, finish(r_banks[1][:], part1[:], "result1")[:])
+        store(1, 0, HALF, finish(r_banks[1][:, :HALF], part1a[:], "result1a")[:])
+        store(1, HALF, S, finish(r_banks[1][:, HALF:], part1b[:], "result1b")[:])
         r_dn3b = finish(r_banks[3][:, HALF:], dn_rows[:, HALF:], "r_dn3b")
         store(2, 0, S, finish(r_banks[2][:], sum2[:], "result2")[:])
         store(3, 0, HALF, finish(r_banks[3][:, :HALF], sum3a[:], "result3a")[:])

@@ -104,12 +104,12 @@ def tile_picked_ivfpq_none_p_kernel(tc, x_words, x_scales, w1, w2, dn, qn, offs,
         cent_list = keep.tile([P, V // GROUP], U16, name="cent_list")
         offs_list = keep.tile([P, S // GROUP], U16, name="offs_list")
         own_list = keep.tile([P, S // GROUP], U16, name="own_list")
-        nc.sync.dma_start(cent_list[:], cent)
         scale_table = place([P, T], U8, "scale_table")
         nc.sync.dma_start(
             out=scale_table[:].bitcast(I32),
             in_=x_scales[0].bitcast(I32).unsqueeze(1).to_broadcast([K // 32, BLOCK, T // 4]),
         )
+        nc.sync.dma_start(cent_list[:], cent)
         nc.sync.dma_start(offs_list[:], offs)
         nc.sync.dma_start(own_list[:], own)
         norm_rows = place([P, P], F32, "norm_rows", first=True)
@@ -154,7 +154,9 @@ def tile_picked_ivfpq_none_p_kernel(tc, x_words, x_scales, w1, w2, dn, qn, offs,
                 )
 
         c_rows0 = place([P, V + SPARE], F32, "c_rows0")
-        nc.vector.memset(c_rows0[:, V:], 0.0)
+        c_rows2 = place([P, V + SPARE], F32, "c_rows2")
+        for c_rows in (c_rows0, c_rows2):
+            nc.vector.memset(c_rows[:, V:], 0.0)
 
         cent_bytes = place([P, V], U8, "cent_bytes")
         nc.vector.tensor_copy(cent_bytes[:], scale_table[:].indirect(cent_list[:]))
@@ -188,13 +190,11 @@ def tile_picked_ivfpq_none_p_kernel(tc, x_words, x_scales, w1, w2, dn, qn, offs,
         def look_up_add(c_rows, part, j0, j1):
             nc.vector.tensor_tensor(part, c_rows[:].indirect(offsets(own_list, j0, j1)), dn_rows[:, j0:j1], ADD)
 
-        def look_up(c_rows, j0, name, **where):
-            part = place([P, HALF], F32, name, **where)
-            nc.scalar.activation(part[:], c_rows[:].indirect(offsets(own_list, j0, j0 + HALF)), COPY)
-            return part
+        def look_up(c_rows, part, j0, j1):
+            nc.scalar.activation(part, c_rows[:].indirect(offsets(own_list, j0, j1)), COPY)
 
-        def add_dn(total, part, j0):
-            nc.gpsimd.tensor_tensor(total, part[:], dn_rows[:, j0 : j0 + HALF], ADD)
+        def add_dn(total, part, j1):
+            nc.gpsimd.tensor_tensor(total[:], part[:], dn_rows[:, :j1], ADD)
 
         def finish(r_part, added, name, **where):
             result = place([P, added.shape[1]], F32, name, **where)
@@ -215,12 +215,11 @@ def tile_picked_ivfpq_none_p_kernel(tc, x_words, x_scales, w1, w2, dn, qn, offs,
         centres(0, w1_q0, c_rows0, 0, V, "c_bank0")
         part0 = place([P, S], F32, "part0")
         look_up_add(c_rows0, part0[:], 0, S)
-        c_rows1 = place([P, V], F32, "c_rows1")
+        c_rows1 = place([P, V], F32, "c_rows1", first=True)
         centres(1, w1_q1, c_rows1, 0, V, "c_bank1")
         part1a = place([P, HALF], F32, "part1a")
         look_up_add(c_rows1, part1a[:], 0, HALF)
         w2_grouped01 = interleave("scalar", w2_raw01, grouped_tile("w2_grouped01", 2, ahead="qn_col0"))
-        c_rows2 = place([P, V], F32, "c_rows2")
         centres(2, w1_q2, c_rows2, 0, V, "c_bank2")
         w2_grouped23 = interleave("vector", w2_raw23, grouped_tile("w2_grouped23", 2, behind="qn_col1"))
         c_rows3 = place([P, V], F32, "c_rows3")
@@ -229,16 +228,17 @@ def tile_picked_ivfpq_none_p_kernel(tc, x_words, x_scales, w1, w2, dn, qn, offs,
         w2_q2, w2_q3 = quantize(w2_grouped23, "w2_q23", inside="w2_raw01")
         part1b = place([P, HALF], F32, "part1b", behind="w2_raw01")
         look_up_add(c_rows1, part1b[:], HALF, S)
-        part2a = look_up(c_rows2, 0, "part2a")
-        part2b = look_up(c_rows2, HALF, "part2b")
-        part3a = look_up(c_rows3, 0, "part3a")
-        part3b = look_up(c_rows3, HALF, "part3b")
+        part2 = place([P, S], F32, "part2")
+        look_up(c_rows2, part2[:], 0, S)
+        part3a = place([P, HALF], F32, "part3a")
+        look_up(c_rows3, part3a[:], 0, HALF)
+        part3b = place([P, HALF], F32, "part3b")
+        look_up(c_rows3, part3b[:], HALF, S)
         r_banks = [rests(t, quantized) for t, quantized in enumerate((w2_q0, w2_q1, w2_q2, w2_q3))]
-        sum2 = place([P, S], F32, "sum2", behind="w2_grouped23")
-        add_dn(sum2[:, :HALF], part2a, 0)
-        add_dn(sum2[:, HALF:], part2b, HALF)
+        sum2 = place([P, S], F32, "sum2", behind="c_rows1")
+        add_dn(sum2, part2, S)
         sum3a = place([P, HALF], F32, "sum3a")
-        add_dn(sum3a[:], part3a, 0)
+        add_dn(sum3a, part3a, HALF)
         store(0, 0, S, finish(r_banks[0][:], part0[:], "result0", ahead="w2_grouped23")[:])
         store(1, 0, HALF, finish(r_banks[1][:, :HALF], part1a[:], "result1a")[:])
         store(1, HALF, S, finish(r_banks[1][:, HALF:], part1b[:], "result1b")[:])

@@ -70,9 +70,10 @@ def tile_picked_ivfpq_none_p_kernel(tc, x_words, x_scales, w1, w2, dn, qn, offs,
         def grouped_tile(name, tiles=1, **where):
             return place([P, tiles * P * PACK], BF16, name, **where)
 
-        def interleave(engine, raw, grouped):
-            target = grouped[:].rearrange("p (c i j) -> p c j i", i=LINE, j=PACK)
-            source = raw[:].rearrange("p j (c i) -> p c j i", i=LINE)
+        def interleave(engine, raw, grouped, m0=0, m1=None):
+            m1 = m1 or raw.shape[2]
+            target = grouped[:, m0 * PACK : m1 * PACK].rearrange("p (c i j) -> p c j i", i=LINE, j=PACK)
+            source = raw[:, :, m0:m1].rearrange("p j (c i) -> p c j i", i=LINE)
             if engine == "vector":
                 nc.vector.tensor_copy(target, source)
             else:
@@ -122,7 +123,7 @@ def tile_picked_ivfpq_none_p_kernel(tc, x_words, x_scales, w1, w2, dn, qn, offs,
         w1_raw1 = load_weight(w1, 1, 1, "w1_raw1", first=True)
         w1_raw2 = load_weight(w1, 2, 1, "w1_raw2", first=True)
 
-        identity = place([P, P], F32, "identity", first=True)
+        identity = place([P, P], F32, "identity")
         nc.vector.memset(identity[:], 0.0)
         make_identity(nc, identity[:], nomemset=True)
         qn_bank = psum.tile([P, P], F32, name="qn_bank", tag="r_bank3")
@@ -132,7 +133,7 @@ def tile_picked_ivfpq_none_p_kernel(tc, x_words, x_scales, w1, w2, dn, qn, offs,
             dn_bank = psum.tile([P, HALF], F32, name=f"dn_bank{half}", tag=bank_slot)
             for i in range(2):
                 jt = 2 * half + i
-                dn_col = place([P, 2 * PAD], F32, f"dn_col{jt}", first=jt < 2)
+                dn_col = place([P, 2 * PAD], F32, f"dn_col{jt}", first=jt != 2)
                 nc.scalar.copy(dn_col[:, :1], qn_bank[:, M_TILES + jt : M_TILES + jt + 1])
                 nc.tensor.transpose(dn_bank[:, i * P : (i + 1) * P], dn_col[:, :1].to_broadcast([P, P]), identity[:])
             nc.scalar.copy(dn_rows[:, half * HALF : (half + 1) * HALF], dn_bank[:])
@@ -141,9 +142,9 @@ def tile_picked_ivfpq_none_p_kernel(tc, x_words, x_scales, w1, w2, dn, qn, offs,
             qn_col = place([P, 2 * PAD], F32, f"qn_col{t}", first=True)
             nc.scalar.copy(qn_col[:, :1], qn_bank[:, t : t + 1])
             qn_cols.append(qn_col[:, :1])
-        qn_last = place([P, 2], F32, "qn_last")
-        nc.scalar.copy(qn_last[:], qn_bank[:, 2:M_TILES])
-        qn_cols.extend([qn_last[:, :1], qn_last[:, 1:]])
+        late_cols = place([P, 2 + M_TILES], F32, "late_cols")
+        nc.scalar.copy(late_cols[:], qn_bank[:, 2 : 2 * M_TILES])
+        qn_cols.extend([late_cols[:, :1], late_cols[:, 1:2]])
 
         def move_rows(plane, gathered):
             nc.vector.memset(plane[:].bitcast(I32), 0)
@@ -166,8 +167,8 @@ def tile_picked_ivfpq_none_p_kernel(tc, x_words, x_scales, w1, w2, dn, qn, offs,
         nc.vector.tensor_copy(offs_bytes[:], scale_table[:].indirect(offs_list[:]))
 
         w1_raw3 = load_weight(w1, 3, 1, "w1_raw3", ahead="norm_rows")
-        w2_raw01 = load_weight(w2, 0, 2, "w2_raw01", behind="norm_rows")
-        w2_raw23 = load_weight(w2, 2, 2, "w2_raw23", behind="dn_col0")
+        w2_raw23 = load_weight(w2, 2, 2, "w2_raw23", behind="norm_rows")
+        w2_raw01 = load_weight(w2, 0, 2, "w2_raw01", behind="dn_col0")
         offs_plane = place([P, S], U8, "offs_plane", behind="dn_col1")
         move_rows(offs_plane, offs_bytes)
 
@@ -205,9 +206,9 @@ def tile_picked_ivfpq_none_p_kernel(tc, x_words, x_scales, w1, w2, dn, qn, offs,
             nc.sync.dma_start(out=out[t * P : (t + 1) * P, j0:j1], in_=result)
 
         cent_words = gather_words(cent_list, 0, V, "cent_words")
-        (w1_q0,) = quantize(interleave("scalar", w1_raw0, grouped_tile("w1_grouped0", behind="identity")), "w1_q0")
+        (w1_q0,) = quantize(interleave("scalar", w1_raw0, grouped_tile("w1_grouped0", behind="dn_col3")), "w1_q0")
         offs_words_a = gather_words(offs_list, 0, HALF, "offs_words_a", ahead="w1_raw0")
-        (w1_q1,) = quantize(interleave("scalar", w1_raw1, grouped_tile("w1_grouped1", ahead="identity")), "w1_q1")
+        (w1_q1,) = quantize(interleave("scalar", w1_raw1, grouped_tile("w1_grouped1", ahead="dn_col3")), "w1_q1")
         offs_words_b = gather_words(offs_list, HALF, S, "offs_words_b", ahead="w1_raw1")
         w1_grouped3 = interleave("vector", w1_raw3, grouped_tile("w1_grouped3", behind="w1_raw1"))
         (w1_q2,) = quantize(interleave("scalar", w1_raw2, grouped_tile("w1_grouped2", behind="w1_grouped0")), "w1_q2")
@@ -215,36 +216,54 @@ def tile_picked_ivfpq_none_p_kernel(tc, x_words, x_scales, w1, w2, dn, qn, offs,
         centres(0, w1_q0, c_rows0, 0, V, "c_bank0")
         part0 = place([P, S], F32, "part0")
         look_up_add(c_rows0, part0[:], 0, S)
-        c_rows1 = place([P, V], F32, "c_rows1", first=True)
+        c_rows1 = place([P, V], F32, "c_rows1")
         centres(1, w1_q1, c_rows1, 0, V, "c_bank1")
         part1a = place([P, HALF], F32, "part1a")
         look_up_add(c_rows1, part1a[:], 0, HALF)
-        w2_grouped01 = interleave("scalar", w2_raw01, grouped_tile("w2_grouped01", 2, ahead="qn_col0"))
+        w2_grouped23 = interleave("scalar", w2_raw23, grouped_tile("w2_grouped23", 2, ahead="qn_col0"), 0, P)
         centres(2, w1_q2, c_rows2, 0, V, "c_bank2")
-        w2_grouped23 = interleave("vector", w2_raw23, grouped_tile("w2_grouped23", 2, behind="qn_col1"))
-        c_rows3 = place([P, V], F32, "c_rows3")
-        centres(3, w1_q3, c_rows3, 0, V, "c_bank3")
-        w2_q0, w2_q1 = quantize(w2_grouped01, "w2_q01")
-        w2_q2, w2_q3 = quantize(w2_grouped23, "w2_q23", inside="w2_raw01")
-        part1b = place([P, HALF], F32, "part1b", behind="w2_raw01")
-        look_up_add(c_rows1, part1b[:], HALF, S)
+        interleave("scalar", w2_raw23, w2_grouped23, P, 2 * P)
         part2 = place([P, S], F32, "part2")
         look_up(c_rows2, part2[:], 0, S)
-        part3a = place([P, HALF], F32, "part3a")
+        w2_grouped01 = interleave("vector", w2_raw01, grouped_tile("w2_grouped01", 2, behind="qn_col1"))
+        c_rows3 = place([P, V], F32, "c_rows3")
+        centres(3, w1_q3, c_rows3, 0, V, "c_bank3")
+        w2_q2, w2_q3 = quantize(w2_grouped23, "w2_q23")
+        w2_q0, w2_q1 = quantize(w2_grouped01, "w2_q01", inside="w2_raw23")
+        part1b = place([P, HALF], F32, "part1b", behind="w2_raw23")
+        look_up_add(c_rows1, part1b[:], HALF, S)
+        turned_bank = psum.tile([P, S], F32, name="turned_bank", tag="r_bank3")
+        for jt in range(M_TILES):
+            words = (offs_words_a, offs_words_b)[jt // 2][:, jt % 2 * P : (jt % 2 + 1) * P]
+            multiply(turned_bank[:, jt * P : (jt + 1) * P], (words, offs_plane[:, jt * P : (jt + 1) * P]), *w2_q3)
+        r_banks = [rests(t, quantized) for t, quantized in enumerate((w2_q0, w2_q1, w2_q2))]
+        turned = place([P, S], F32, "turned")
+        nc.scalar.activation(turned[:], turned_bank[:], IDENTITY, scale=-2.0)
+        sum_banks = []
+        for half in range(2):
+            sum_bank = psum.tile([P, HALF], F32, name=f"sum_bank{half}", tag=f"c_bank{half}")
+            for i in range(2):
+                dn_spread = late_cols[:, 2 + 2 * half + i : 3 + 2 * half + i].to_broadcast([P, P])
+                nc.tensor.matmul(sum_bank[:, i * P : (i + 1) * P], dn_spread, identity[:], start=i == 0, stop=False, is_transpose=True)
+            for i in range(2):
+                jt = 2 * half + i
+                nc.tensor.matmul(sum_bank[:, i * P : (i + 1) * P], turned[:, jt * P : (jt + 1) * P], identity[:], start=False, stop=i == 1, is_transpose=True)
+            sum_banks.append(sum_bank)
+        part3a = place([P, HALF], F32, "part3a", ahead="offs_words_b")
         look_up(c_rows3, part3a[:], 0, HALF)
-        part3b = place([P, HALF], F32, "part3b")
+        part3b = place([P, HALF], F32, "part3b", ahead="offs_words_a")
         look_up(c_rows3, part3b[:], HALF, S)
-        r_banks = [rests(t, quantized) for t, quantized in enumerate((w2_q0, w2_q1, w2_q2, w2_q3))]
-        sum2 = place([P, S], F32, "sum2", behind="c_rows1")
+        sum2 = place([P, S], F32, "sum2", behind="w2_grouped01")
         add_dn(sum2, part2, S)
-        sum3a = place([P, HALF], F32, "sum3a")
-        add_dn(sum3a, part3a, HALF)
-        store(0, 0, S, finish(r_banks[0][:], part0[:], "result0", ahead="w2_grouped23")[:])
+        store(0, 0, S, finish(r_banks[0][:], part0[:], "result0", ahead="w2_grouped01")[:])
         store(1, 0, HALF, finish(r_banks[1][:, :HALF], part1a[:], "result1a")[:])
         store(1, HALF, S, finish(r_banks[1][:, HALF:], part1b[:], "result1b")[:])
-        r_dn3b = finish(r_banks[3][:, HALF:], dn_rows[:, HALF:], "r_dn3b")
+
+        def finish_last(half, part):
+            result3 = place([P, HALF], F32, f"result3_{half}")
+            nc.vector.tensor_tensor(result3[:], sum_banks[half][:], part[:], ADD)
+            store(3, half * HALF, (half + 1) * HALF, result3[:])
+
         store(2, 0, S, finish(r_banks[2][:], sum2[:], "result2")[:])
-        store(3, 0, HALF, finish(r_banks[3][:, :HALF], sum3a[:], "result3a")[:])
-        result3b = place([P, HALF], F32, "result3b")
-        nc.vector.tensor_tensor(result3b[:], r_dn3b[:], part3b[:], ADD)
-        store(3, HALF, S, result3b[:])
+        finish_last(0, part3a)
+        finish_last(1, part3b)

@@ -30,8 +30,9 @@ SPARE = 16
 HALF = S // 2
 QUARTER = S // 4
 OVERLAP = 64
-LEAD = 4096
-CHAIN = 12288
+LEAD = 6144
+CHAIN = 14336
+TILE_OF = (0, 2, 1, 3)
 BYTES_OF = {F32: 4, BF16: 2, U32: 4, U8: 1, I32: 4}
 
 
@@ -120,8 +121,8 @@ def tile_picked_ivfpq_none_p_kernel(tc, x_words, x_scales, w1, w2, dn, qn, offs,
         word_table = place([P, T], I32, "word_table")
         nc.sync.dma_start(out=word_table[:], in_=x_words[0].rearrange("p n t -> p (n t)").bitcast(I32))
         w1_raw0 = load_weight(w1, 0, 1, "w1_raw0", first=True)
-        w1_raw1 = load_weight(w1, 1, 1, "w1_raw1", first=True)
-        w1_raw2 = load_weight(w1, 2, 1, "w1_raw2", first=True)
+        w1_raw1 = load_weight(w1, TILE_OF[1], 1, "w1_raw1", first=True)
+        w1_raw2 = load_weight(w1, TILE_OF[2], 1, "w1_raw2")
 
         identity = place([P, P], F32, "identity")
         nc.vector.memset(identity[:], 0.0)
@@ -137,14 +138,11 @@ def tile_picked_ivfpq_none_p_kernel(tc, x_words, x_scales, w1, w2, dn, qn, offs,
                 nc.scalar.copy(dn_col[:, :1], qn_bank[:, M_TILES + jt : M_TILES + jt + 1])
                 nc.tensor.transpose(dn_bank[:, i * P : (i + 1) * P], dn_col[:, :1].to_broadcast([P, P]), identity[:])
             nc.scalar.copy(dn_rows[:, half * HALF : (half + 1) * HALF], dn_bank[:])
-        qn_cols = []
-        for t in range(2):
-            qn_col = place([P, 2 * PAD], F32, f"qn_col{t}", first=True)
-            nc.scalar.copy(qn_col[:, :1], qn_bank[:, t : t + 1])
-            qn_cols.append(qn_col[:, :1])
-        late_cols = place([P, 2 + M_TILES], F32, "late_cols")
-        nc.scalar.copy(late_cols[:], qn_bank[:, 2 : 2 * M_TILES])
-        qn_cols.extend([late_cols[:, :1], late_cols[:, 1:2]])
+        qn_first = place([P, 2 * PAD], F32, "qn_first", first=True)
+        nc.scalar.copy(qn_first[:, :1], qn_bank[:, :1])
+        late_cols = place([P, 2 * M_TILES - 1], F32, "late_cols")
+        nc.scalar.copy(late_cols[:], qn_bank[:, 1 : 2 * M_TILES])
+        qn_cols = [qn_first[:, :1]] + [late_cols[:, TILE_OF[t] - 1 : TILE_OF[t]] for t in range(1, M_TILES)]
 
         def move_rows(plane, gathered):
             nc.vector.memset(plane[:].bitcast(I32), 0)
@@ -167,8 +165,9 @@ def tile_picked_ivfpq_none_p_kernel(tc, x_words, x_scales, w1, w2, dn, qn, offs,
         nc.vector.tensor_copy(offs_bytes[:], scale_table[:].indirect(offs_list[:]))
 
         w1_raw3 = load_weight(w1, 3, 1, "w1_raw3", ahead="norm_rows")
-        w2_raw23 = load_weight(w2, 2, 2, "w2_raw23", behind="norm_rows")
-        w2_raw01 = load_weight(w2, 0, 2, "w2_raw01", behind="dn_col0")
+        w2_raw0 = load_weight(w2, TILE_OF[0], 1, "w2_raw0", behind="norm_rows")
+        w2_raw2 = load_weight(w2, TILE_OF[2], 1, "w2_raw2", behind="dn_col0")
+        w2_raw13 = load_weight(w2, TILE_OF[1], 2, "w2_raw13", ahead="dn_col0")
         offs_plane = place([P, S], U8, "offs_plane", behind="dn_col1")
         move_rows(offs_plane, offs_bytes)
 
@@ -194,8 +193,10 @@ def tile_picked_ivfpq_none_p_kernel(tc, x_words, x_scales, w1, w2, dn, qn, offs,
         def look_up(c_rows, part, j0, j1):
             nc.scalar.activation(part, c_rows[:].indirect(offsets(own_list, j0, j1)), COPY)
 
-        def add_dn(total, part, j1):
-            nc.gpsimd.tensor_tensor(total[:], part[:], dn_rows[:, :j1], ADD)
+        def add_dn(part, j0, name, **where):
+            total = place([P, HALF], F32, name, **where)
+            nc.gpsimd.tensor_tensor(total[:], part[:, j0 : j0 + HALF], dn_rows[:, j0 : j0 + HALF], ADD)
+            return total
 
         def finish(r_part, added, name, **where):
             result = place([P, added.shape[1]], F32, name, **where)
@@ -203,7 +204,7 @@ def tile_picked_ivfpq_none_p_kernel(tc, x_words, x_scales, w1, w2, dn, qn, offs,
             return result
 
         def store(t, j0, j1, result):
-            nc.sync.dma_start(out=out[t * P : (t + 1) * P, j0:j1], in_=result)
+            nc.sync.dma_start(out=out[TILE_OF[t] * P : (TILE_OF[t] + 1) * P, j0:j1], in_=result)
 
         cent_words = gather_words(cent_list, 0, V, "cent_words")
         (w1_q0,) = quantize(interleave("scalar", w1_raw0, grouped_tile("w1_grouped0", behind="dn_col3")), "w1_q0")
@@ -214,36 +215,37 @@ def tile_picked_ivfpq_none_p_kernel(tc, x_words, x_scales, w1, w2, dn, qn, offs,
         (w1_q2,) = quantize(interleave("scalar", w1_raw2, grouped_tile("w1_grouped2", behind="w1_grouped0")), "w1_q2")
         (w1_q3,) = quantize(w1_grouped3, "w1_q3")
         centres(0, w1_q0, c_rows0, 0, V, "c_bank0")
-        part0 = place([P, S], F32, "part0")
+        part0 = place([P, S], F32, "part0", first=True)
         look_up_add(c_rows0, part0[:], 0, S)
         c_rows1 = place([P, V], F32, "c_rows1")
         centres(1, w1_q1, c_rows1, 0, V, "c_bank1")
-        part1a = place([P, HALF], F32, "part1a")
-        look_up_add(c_rows1, part1a[:], 0, HALF)
-        w2_grouped23 = interleave("scalar", w2_raw23, grouped_tile("w2_grouped23", 2, ahead="qn_col0"), 0, P)
+        w2_grouped0 = interleave("scalar", w2_raw0, grouped_tile("w2_grouped0", ahead="qn_first"))
         centres(2, w1_q2, c_rows2, 0, V, "c_bank2")
-        interleave("scalar", w2_raw23, w2_grouped23, P, 2 * P)
+        w2_grouped2 = interleave("scalar", w2_raw2, grouped_tile("w2_grouped2", behind="qn_first"))
         part2 = place([P, S], F32, "part2")
         look_up(c_rows2, part2[:], 0, S)
-        w2_grouped01 = interleave("vector", w2_raw01, grouped_tile("w2_grouped01", 2, behind="qn_col1"))
         c_rows3 = place([P, V], F32, "c_rows3")
         centres(3, w1_q3, c_rows3, 0, V, "c_bank3")
-        w2_q2, w2_q3 = quantize(w2_grouped23, "w2_q23")
-        w2_q0, w2_q1 = quantize(w2_grouped01, "w2_q01", inside="w2_raw23")
-        part1b = place([P, HALF], F32, "part1b", behind="w2_raw23")
-        look_up_add(c_rows1, part1b[:], HALF, S)
+        w2_grouped13 = interleave("vector", w2_raw13, grouped_tile("w2_grouped13", 2, behind="w2_raw0"))
+        (w2_q0,) = quantize(w2_grouped0, "w2_q0")
+        w2_q1, w2_q3 = quantize(w2_grouped13, "w2_q13")
+        (w2_q2,) = quantize(w2_grouped2, "w2_q2")
+        part1a = place([P, HALF], F32, "part1a", behind="w2_grouped13")
+        look_up_add(c_rows1, part1a[:], 0, HALF)
+        r_banks = [rests(t, quantized) for t, quantized in enumerate((w2_q0, w2_q1))]
         turned_bank = psum.tile([P, S], F32, name="turned_bank", tag="r_bank3")
         for jt in range(M_TILES):
             words = (offs_words_a, offs_words_b)[jt // 2][:, jt % 2 * P : (jt % 2 + 1) * P]
             multiply(turned_bank[:, jt * P : (jt + 1) * P], (words, offs_plane[:, jt * P : (jt + 1) * P]), *w2_q3)
-        r_banks = [rests(t, quantized) for t, quantized in enumerate((w2_q0, w2_q1, w2_q2))]
+        r_banks.append(rests(2, w2_q2))
         turned = place([P, S], F32, "turned")
         nc.scalar.activation(turned[:], turned_bank[:], IDENTITY, scale=-2.0)
         sum_banks = []
         for half in range(2):
             sum_bank = psum.tile([P, HALF], F32, name=f"sum_bank{half}", tag=f"c_bank{half}")
             for i in range(2):
-                dn_spread = late_cols[:, 2 + 2 * half + i : 3 + 2 * half + i].to_broadcast([P, P])
+                jt = 2 * half + i
+                dn_spread = late_cols[:, M_TILES - 1 + jt : M_TILES + jt].to_broadcast([P, P])
                 nc.tensor.matmul(sum_bank[:, i * P : (i + 1) * P], dn_spread, identity[:], start=i == 0, stop=False, is_transpose=True)
             for i in range(2):
                 jt = 2 * half + i
@@ -253,17 +255,24 @@ def tile_picked_ivfpq_none_p_kernel(tc, x_words, x_scales, w1, w2, dn, qn, offs,
         look_up(c_rows3, part3a[:], 0, HALF)
         part3b = place([P, HALF], F32, "part3b", ahead="offs_words_a")
         look_up(c_rows3, part3b[:], HALF, S)
-        sum2 = place([P, S], F32, "sum2", behind="w2_grouped01")
-        add_dn(sum2, part2, S)
-        store(0, 0, S, finish(r_banks[0][:], part0[:], "result0", ahead="w2_grouped01")[:])
-        store(1, 0, HALF, finish(r_banks[1][:, :HALF], part1a[:], "result1a")[:])
-        store(1, HALF, S, finish(r_banks[1][:, HALF:], part1b[:], "result1b")[:])
+
+        def finish_half(t, half, added):
+            columns = slice(half * HALF, (half + 1) * HALF)
+            store(t, columns.start, columns.stop, finish(r_banks[t][:, columns], added[:], f"result{t}_{half}")[:])
 
         def finish_last(half, part):
             result3 = place([P, HALF], F32, f"result3_{half}")
             nc.vector.tensor_tensor(result3[:], sum_banks[half][:], part[:], ADD)
             store(3, half * HALF, (half + 1) * HALF, result3[:])
 
-        store(2, 0, S, finish(r_banks[2][:], sum2[:], "result2")[:])
+        sum2a = add_dn(part2, 0, "sum2a", behind="w2_grouped2")
+        store(0, 0, S, finish(r_banks[0][:], part0[:], "result0", ahead="w2_grouped13")[:])
+        finish_half(1, 0, part1a)
+        part1b = place([P, HALF], F32, "part1b", behind="part0")
+        look_up_add(c_rows1, part1b[:], HALF, S)
+        sum2b = add_dn(part2, HALF, "sum2b", behind="part1a")
+        finish_half(1, 1, part1b)
+        finish_half(2, 0, sum2a)
         finish_last(0, part3a)
+        finish_half(2, 1, sum2b)
         finish_last(1, part3b)

@@ -30,9 +30,8 @@ SPARE = 16
 HALF = S // 2
 QUARTER = S // 4
 OVERLAP = 64
-LEAD = 6144
-CHAIN = 14336
-TILE_OF = (0, 2, 1, 3)
+LEAD = 4096
+CHAIN = 10240
 BYTES_OF = {F32: 4, BF16: 2, U32: 4, U8: 1, I32: 4}
 
 
@@ -121,8 +120,8 @@ def tile_picked_ivfpq_none_p_kernel(tc, x_words, x_scales, w1, w2, dn, qn, offs,
         word_table = place([P, T], I32, "word_table")
         nc.sync.dma_start(out=word_table[:], in_=x_words[0].rearrange("p n t -> p (n t)").bitcast(I32))
         w1_raw0 = load_weight(w1, 0, 1, "w1_raw0", first=True)
-        w1_raw1 = load_weight(w1, TILE_OF[1], 1, "w1_raw1", first=True)
-        w1_raw2 = load_weight(w1, TILE_OF[2], 1, "w1_raw2")
+        w1_raw1 = load_weight(w1, 1, 1, "w1_raw1", first=True)
+        w1_raw2 = load_weight(w1, 2, 1, "w1_raw2")
 
         identity = place([P, P], F32, "identity")
         nc.vector.memset(identity[:], 0.0)
@@ -142,7 +141,9 @@ def tile_picked_ivfpq_none_p_kernel(tc, x_words, x_scales, w1, w2, dn, qn, offs,
         nc.scalar.copy(qn_first[:, :1], qn_bank[:, :1])
         late_cols = place([P, 2 * M_TILES - 1], F32, "late_cols")
         nc.scalar.copy(late_cols[:], qn_bank[:, 1 : 2 * M_TILES])
-        qn_cols = [qn_first[:, :1]] + [late_cols[:, TILE_OF[t] - 1 : TILE_OF[t]] for t in range(1, M_TILES)]
+        qn_third = place([P, 2 * PAD], F32, "qn_third", first=True)
+        nc.scalar.copy(qn_third[:, :1], qn_bank[:, 2:3])
+        qn_cols = [qn_first[:, :1], late_cols[:, :1], qn_third[:, :1], late_cols[:, 2:3]]
 
         def move_rows(plane, gathered):
             nc.vector.memset(plane[:].bitcast(I32), 0)
@@ -153,9 +154,7 @@ def tile_picked_ivfpq_none_p_kernel(tc, x_words, x_scales, w1, w2, dn, qn, offs,
                 )
 
         c_rows0 = place([P, V + SPARE], F32, "c_rows0")
-        c_rows2 = place([P, V + SPARE], F32, "c_rows2")
-        for c_rows in (c_rows0, c_rows2):
-            nc.vector.memset(c_rows[:, V:], 0.0)
+        nc.vector.memset(c_rows0[:, V:], 0.0)
 
         cent_bytes = place([P, V], U8, "cent_bytes")
         nc.vector.tensor_copy(cent_bytes[:], scale_table[:].indirect(cent_list[:]))
@@ -165,9 +164,9 @@ def tile_picked_ivfpq_none_p_kernel(tc, x_words, x_scales, w1, w2, dn, qn, offs,
         nc.vector.tensor_copy(offs_bytes[:], scale_table[:].indirect(offs_list[:]))
 
         w1_raw3 = load_weight(w1, 3, 1, "w1_raw3", ahead="norm_rows")
-        w2_raw0 = load_weight(w2, TILE_OF[0], 1, "w2_raw0", behind="norm_rows")
-        w2_raw2 = load_weight(w2, TILE_OF[2], 1, "w2_raw2", behind="dn_col0")
-        w2_raw13 = load_weight(w2, TILE_OF[1], 2, "w2_raw13", ahead="dn_col0")
+        w2_raw3 = load_weight(w2, 3, 1, "w2_raw3", behind="norm_rows")
+        w2_raw0 = load_weight(w2, 0, 1, "w2_raw0", behind="dn_col0")
+        w2_raw12 = load_weight(w2, 1, 2, "w2_raw12", ahead="dn_col0")
         offs_plane = place([P, S], U8, "offs_plane", behind="dn_col1")
         move_rows(offs_plane, offs_bytes)
 
@@ -195,7 +194,7 @@ def tile_picked_ivfpq_none_p_kernel(tc, x_words, x_scales, w1, w2, dn, qn, offs,
 
         def add_dn(part, j0, name, **where):
             total = place([P, HALF], F32, name, **where)
-            nc.gpsimd.tensor_tensor(total[:], part[:, j0 : j0 + HALF], dn_rows[:, j0 : j0 + HALF], ADD)
+            nc.gpsimd.tensor_tensor(total[:], part[:], dn_rows[:, j0 : j0 + HALF], ADD)
             return total
 
         def finish(r_part, added, name, **where):
@@ -204,7 +203,7 @@ def tile_picked_ivfpq_none_p_kernel(tc, x_words, x_scales, w1, w2, dn, qn, offs,
             return result
 
         def store(t, j0, j1, result):
-            nc.sync.dma_start(out=out[TILE_OF[t] * P : (TILE_OF[t] + 1) * P, j0:j1], in_=result)
+            nc.sync.dma_start(out=out[t * P : (t + 1) * P, j0:j1], in_=result)
 
         cent_words = gather_words(cent_list, 0, V, "cent_words")
         (w1_q0,) = quantize(interleave("scalar", w1_raw0, grouped_tile("w1_grouped0", behind="dn_col3")), "w1_q0")
@@ -219,27 +218,29 @@ def tile_picked_ivfpq_none_p_kernel(tc, x_words, x_scales, w1, w2, dn, qn, offs,
         look_up_add(c_rows0, part0[:], 0, S)
         c_rows1 = place([P, V], F32, "c_rows1")
         centres(1, w1_q1, c_rows1, 0, V, "c_bank1")
-        w2_grouped0 = interleave("scalar", w2_raw0, grouped_tile("w2_grouped0", ahead="qn_first"))
+        w2_grouped3 = interleave("scalar", w2_raw3, grouped_tile("w2_grouped3", ahead="qn_first"))
+        c_rows2 = place([P, V], F32, "c_rows2")
         centres(2, w1_q2, c_rows2, 0, V, "c_bank2")
-        w2_grouped2 = interleave("scalar", w2_raw2, grouped_tile("w2_grouped2", behind="qn_first"))
-        part2 = place([P, S], F32, "part2")
-        look_up(c_rows2, part2[:], 0, S)
-        c_rows3 = place([P, V], F32, "c_rows3")
-        centres(3, w1_q3, c_rows3, 0, V, "c_bank3")
-        w2_grouped13 = interleave("vector", w2_raw13, grouped_tile("w2_grouped13", 2, behind="w2_raw0"))
-        (w2_q0,) = quantize(w2_grouped0, "w2_q0")
-        w2_q1, w2_q3 = quantize(w2_grouped13, "w2_q13")
-        (w2_q2,) = quantize(w2_grouped2, "w2_q2")
-        part1a = place([P, HALF], F32, "part1a", behind="w2_grouped13")
+        w2_grouped0 = interleave("scalar", w2_raw0, grouped_tile("w2_grouped0", behind="qn_first"))
+        part2a = place([P, HALF], F32, "part2a")
+        look_up(c_rows2, part2a[:], 0, HALF)
+        (w2_q3,) = quantize(w2_grouped3, "w2_q3")
+        w2_grouped12 = interleave("vector", w2_raw12, grouped_tile("w2_grouped12", 2, behind="qn_third"))
+        (w2_q0,) = quantize(w2_grouped0, "w2_q0", first=True)
+        w2_q1, w2_q2 = quantize(w2_grouped12, "w2_q12")
+        part1a = place([P, HALF], F32, "part1a", behind="w2_grouped0")
         look_up_add(c_rows1, part1a[:], 0, HALF)
-        r_banks = [rests(t, quantized) for t, quantized in enumerate((w2_q0, w2_q1))]
         turned_bank = psum.tile([P, S], F32, name="turned_bank", tag="r_bank3")
         for jt in range(M_TILES):
             words = (offs_words_a, offs_words_b)[jt // 2][:, jt % 2 * P : (jt % 2 + 1) * P]
             multiply(turned_bank[:, jt * P : (jt + 1) * P], (words, offs_plane[:, jt * P : (jt + 1) * P]), *w2_q3)
-        r_banks.append(rests(2, w2_q2))
+        r_banks = [rests(t, quantized) for t, quantized in enumerate((w2_q0, w2_q1, w2_q2))]
         turned = place([P, S], F32, "turned")
         nc.scalar.activation(turned[:], turned_bank[:], IDENTITY, scale=-2.0)
+        c_rows3 = place([P, V], F32, "c_rows3", behind="w2_q0_codes")
+        centres(3, w1_q3, c_rows3, 0, V, "c_bank3")
+        part2b = place([P, HALF], F32, "part2b", ahead="w2_q0_codes")
+        look_up(c_rows2, part2b[:], HALF, S)
         sum_banks = []
         for half in range(2):
             sum_bank = psum.tile([P, HALF], F32, name=f"sum_bank{half}", tag=f"c_bank{half}")
@@ -251,9 +252,9 @@ def tile_picked_ivfpq_none_p_kernel(tc, x_words, x_scales, w1, w2, dn, qn, offs,
                 jt = 2 * half + i
                 nc.tensor.matmul(sum_bank[:, i * P : (i + 1) * P], turned[:, jt * P : (jt + 1) * P], identity[:], start=False, stop=i == 1, is_transpose=True)
             sum_banks.append(sum_bank)
-        part3a = place([P, HALF], F32, "part3a", ahead="offs_words_b")
+        part3a = place([P, HALF], F32, "part3a")
         look_up(c_rows3, part3a[:], 0, HALF)
-        part3b = place([P, HALF], F32, "part3b", ahead="offs_words_a")
+        part3b = place([P, HALF], F32, "part3b")
         look_up(c_rows3, part3b[:], HALF, S)
 
         def finish_half(t, half, added):
@@ -265,12 +266,12 @@ def tile_picked_ivfpq_none_p_kernel(tc, x_words, x_scales, w1, w2, dn, qn, offs,
             nc.vector.tensor_tensor(result3[:], sum_banks[half][:], part[:], ADD)
             store(3, half * HALF, (half + 1) * HALF, result3[:])
 
-        sum2a = add_dn(part2, 0, "sum2a", behind="w2_grouped2")
-        store(0, 0, S, finish(r_banks[0][:], part0[:], "result0", ahead="w2_grouped13")[:])
+        sum2a = add_dn(part2a, 0, "sum2a", behind="w2_grouped12")
+        store(0, 0, S, finish(r_banks[0][:], part0[:], "result0", ahead="w2_grouped12")[:])
         finish_half(1, 0, part1a)
         part1b = place([P, HALF], F32, "part1b", behind="part0")
         look_up_add(c_rows1, part1b[:], HALF, S)
-        sum2b = add_dn(part2, HALF, "sum2b", behind="part1a")
+        sum2b = add_dn(part2b, HALF, "sum2b", behind="part1a")
         finish_half(1, 1, part1b)
         finish_half(2, 0, sum2a)
         finish_last(0, part3a)

@@ -54,7 +54,7 @@ def tile_picked_ivfpq_none_p_kernel(tc, x_words, x_scales, w1, w2, dn, qn, offs,
             elif behind:
                 offset = spans[behind][1] - OVERLAP
             elif inside:
-                offset = spans[inside][0] + 16 * OVERLAP
+                offset = spans[inside][0] + OVERLAP
             elif ahead:
                 offset = spans[ahead][0] + OVERLAP - size
             else:
@@ -121,7 +121,7 @@ def tile_picked_ivfpq_none_p_kernel(tc, x_words, x_scales, w1, w2, dn, qn, offs,
         nc.sync.dma_start(out=word_table[:], in_=x_words[0].rearrange("p n t -> p (n t)").bitcast(I32))
         w1_raw0 = load_weight(w1, 0, 1, "w1_raw0", first=True)
         w1_raw1 = load_weight(w1, 1, 1, "w1_raw1", first=True)
-        w1_raw2 = load_weight(w1, 2, 1, "w1_raw2")
+        w1_raw2 = load_weight(w1, 2, 1, "w1_raw2", first=True)
 
         identity = place([P, P], F32, "identity")
         nc.vector.memset(identity[:], 0.0)
@@ -137,13 +137,11 @@ def tile_picked_ivfpq_none_p_kernel(tc, x_words, x_scales, w1, w2, dn, qn, offs,
                 nc.scalar.copy(dn_col[:, :1], qn_bank[:, M_TILES + jt : M_TILES + jt + 1])
                 nc.tensor.transpose(dn_bank[:, i * P : (i + 1) * P], dn_col[:, :1].to_broadcast([P, P]), identity[:])
             nc.scalar.copy(dn_rows[:, half * HALF : (half + 1) * HALF], dn_bank[:])
-        qn_first = place([P, 2 * PAD], F32, "qn_first", first=True)
-        nc.scalar.copy(qn_first[:, :1], qn_bank[:, :1])
-        late_cols = place([P, 2 * M_TILES - 1], F32, "late_cols")
-        nc.scalar.copy(late_cols[:], qn_bank[:, 1 : 2 * M_TILES])
-        qn_third = place([P, 2 * PAD], F32, "qn_third", first=True)
-        nc.scalar.copy(qn_third[:, :1], qn_bank[:, 2:3])
-        qn_cols = [qn_first[:, :1], late_cols[:, :1], qn_third[:, :1], late_cols[:, 2:3]]
+        qn_second = place([P, 2 * PAD], F32, "qn_second", first=True)
+        nc.scalar.copy(qn_second[:, :1], qn_bank[:, 1:2])
+        norm_cols = place([P, 2 * M_TILES], F32, "norm_cols")
+        nc.scalar.copy(norm_cols[:], qn_bank[:, : 2 * M_TILES])
+        qn_cols = [norm_cols[:, :1], qn_second[:, :1], norm_cols[:, 2:3], norm_cols[:, 3:4]]
 
         def move_rows(plane, gathered):
             nc.vector.memset(plane[:].bitcast(I32), 0)
@@ -213,22 +211,24 @@ def tile_picked_ivfpq_none_p_kernel(tc, x_words, x_scales, w1, w2, dn, qn, offs,
         w1_grouped3 = interleave("vector", w1_raw3, grouped_tile("w1_grouped3", behind="w1_raw1"))
         (w1_q2,) = quantize(interleave("scalar", w1_raw2, grouped_tile("w1_grouped2", behind="w1_grouped0")), "w1_q2")
         (w1_q3,) = quantize(w1_grouped3, "w1_q3")
-        centres(0, w1_q0, c_rows0, 0, V, "c_bank0")
+        centres(0, w1_q0, c_rows0, 0, HALF, "c_bank0")
+        centres(0, w1_q0, c_rows0, HALF, V, "r_bank0")
         part0 = place([P, S], F32, "part0", first=True)
         look_up_add(c_rows0, part0[:], 0, S)
+        w2_grouped3 = interleave("scalar", w2_raw3, grouped_tile("w2_grouped3", behind="w1_raw2"))
         c_rows1 = place([P, V], F32, "c_rows1")
         centres(1, w1_q1, c_rows1, 0, V, "c_bank1")
-        w2_grouped3 = interleave("scalar", w2_raw3, grouped_tile("w2_grouped3", ahead="qn_first"))
         c_rows2 = place([P, V], F32, "c_rows2")
         centres(2, w1_q2, c_rows2, 0, V, "c_bank2")
-        w2_grouped0 = interleave("scalar", w2_raw0, grouped_tile("w2_grouped0", behind="qn_first"))
+        w2_grouped0 = interleave("scalar", w2_raw0, grouped_tile("w2_grouped0", ahead="qn_second"), 0, P // 2)
         part2a = place([P, HALF], F32, "part2a")
         look_up(c_rows2, part2a[:], 0, HALF)
         (w2_q3,) = quantize(w2_grouped3, "w2_q3")
-        w2_grouped12 = interleave("vector", w2_raw12, grouped_tile("w2_grouped12", 2, behind="qn_third"))
+        interleave("vector", w2_raw0, w2_grouped0, P // 2, P)
+        w2_grouped12 = interleave("vector", w2_raw12, grouped_tile("w2_grouped12", 2, behind="qn_second"))
         (w2_q0,) = quantize(w2_grouped0, "w2_q0", first=True)
         w2_q1, w2_q2 = quantize(w2_grouped12, "w2_q12")
-        part1a = place([P, HALF], F32, "part1a", behind="w2_grouped0")
+        part1a = place([P, HALF], F32, "part1a", ahead="w2_grouped0")
         look_up_add(c_rows1, part1a[:], 0, HALF)
         turned_bank = psum.tile([P, S], F32, name="turned_bank", tag="r_bank3")
         for jt in range(M_TILES):
@@ -246,7 +246,7 @@ def tile_picked_ivfpq_none_p_kernel(tc, x_words, x_scales, w1, w2, dn, qn, offs,
             sum_bank = psum.tile([P, HALF], F32, name=f"sum_bank{half}", tag=f"c_bank{half}")
             for i in range(2):
                 jt = 2 * half + i
-                dn_spread = late_cols[:, M_TILES - 1 + jt : M_TILES + jt].to_broadcast([P, P])
+                dn_spread = norm_cols[:, M_TILES + jt : M_TILES + jt + 1].to_broadcast([P, P])
                 nc.tensor.matmul(sum_bank[:, i * P : (i + 1) * P], dn_spread, identity[:], start=i == 0, stop=False, is_transpose=True)
             for i in range(2):
                 jt = 2 * half + i
@@ -266,12 +266,12 @@ def tile_picked_ivfpq_none_p_kernel(tc, x_words, x_scales, w1, w2, dn, qn, offs,
             nc.vector.tensor_tensor(result3[:], sum_banks[half][:], part[:], ADD)
             store(3, half * HALF, (half + 1) * HALF, result3[:])
 
-        sum2a = add_dn(part2a, 0, "sum2a", behind="w2_grouped12")
-        store(0, 0, S, finish(r_banks[0][:], part0[:], "result0", ahead="w2_grouped12")[:])
+        sum2a = add_dn(part2a, 0, "sum2a", inside="w2_grouped12")
+        store(0, 0, S, finish(r_banks[0][:], part0[:], "result0", behind="w2_grouped12")[:])
         finish_half(1, 0, part1a)
         part1b = place([P, HALF], F32, "part1b", behind="part0")
         look_up_add(c_rows1, part1b[:], HALF, S)
-        sum2b = add_dn(part2b, HALF, "sum2b", behind="part1a")
+        sum2b = add_dn(part2b, HALF, "sum2b", ahead="part1a")
         finish_half(1, 1, part1b)
         finish_half(2, 0, sum2a)
         finish_last(0, part3a)

@@ -220,11 +220,13 @@ def tile_picked_ivfpq_none_p_kernel(tc, x_words, x_scales, w1, w2, dn, qn, offs,
         centres(1, w1_q1, c_rows1, 0, V, "c_bank1")
         c_rows2 = place([P, V], F32, "c_rows2")
         centres(2, w1_q2, c_rows2, 0, V, "c_bank2")
-        w2_grouped0 = interleave("scalar", w2_raw0, grouped_tile("w2_grouped0", ahead="qn_second"), 0, P // 2)
+        w2_grouped0 = interleave("scalar", w2_raw0, grouped_tile("w2_grouped0", ahead="qn_second"), 0, P - P // 4)
         part2a = place([P, HALF], F32, "part2a")
         look_up(c_rows2, part2a[:], 0, HALF)
+        c_rows3 = place([P, V], F32, "c_rows3")
+        centres(3, w1_q3, c_rows3, 0, V, "c_bank3")
         (w2_q3,) = quantize(w2_grouped3, "w2_q3")
-        interleave("vector", w2_raw0, w2_grouped0, P // 2, P)
+        interleave("vector", w2_raw0, w2_grouped0, P - P // 4, P)
         w2_grouped12 = interleave("vector", w2_raw12, grouped_tile("w2_grouped12", 2, behind="qn_second"))
         (w2_q0,) = quantize(w2_grouped0, "w2_q0", first=True)
         w2_q1, w2_q2 = quantize(w2_grouped12, "w2_q12")
@@ -237,8 +239,6 @@ def tile_picked_ivfpq_none_p_kernel(tc, x_words, x_scales, w1, w2, dn, qn, offs,
         r_banks = [rests(t, quantized) for t, quantized in enumerate((w2_q0, w2_q1, w2_q2))]
         turned = place([P, S], F32, "turned")
         nc.scalar.activation(turned[:], turned_bank[:], IDENTITY, scale=-2.0)
-        c_rows3 = place([P, V], F32, "c_rows3", behind="w2_q0_codes")
-        centres(3, w1_q3, c_rows3, 0, V, "c_bank3")
         part2b = place([P, HALF], F32, "part2b", ahead="w2_q0_codes")
         look_up(c_rows2, part2b[:], HALF, S)
         sum_banks = []
@@ -252,18 +252,17 @@ def tile_picked_ivfpq_none_p_kernel(tc, x_words, x_scales, w1, w2, dn, qn, offs,
                 jt = 2 * half + i
                 nc.tensor.matmul(sum_bank[:, i * P : (i + 1) * P], turned[:, jt * P : (jt + 1) * P], identity[:], start=False, stop=i == 1, is_transpose=True)
             sum_banks.append(sum_bank)
-        part3a = place([P, HALF], F32, "part3a")
-        look_up(c_rows3, part3a[:], 0, HALF)
-        part3b = place([P, HALF], F32, "part3b")
-        look_up(c_rows3, part3b[:], HALF, S)
+        part3 = place([P, S], F32, "part3", behind="w2_q0_codes")
+        for j0 in (0, HALF):
+            look_up(c_rows3, part3[:, j0 : j0 + HALF], j0, j0 + HALF)
 
         def finish_half(t, half, added):
             columns = slice(half * HALF, (half + 1) * HALF)
             store(t, columns.start, columns.stop, finish(r_banks[t][:, columns], added[:], f"result{t}_{half}")[:])
 
-        def finish_last(half, part):
+        def finish_last(half):
             result3 = place([P, HALF], F32, f"result3_{half}")
-            nc.vector.tensor_tensor(result3[:], sum_banks[half][:], part[:], ADD)
+            nc.vector.tensor_tensor(result3[:], sum_banks[half][:], part3[:, half * HALF : (half + 1) * HALF], ADD)
             store(3, half * HALF, (half + 1) * HALF, result3[:])
 
         sum2a = add_dn(part2a, 0, "sum2a", inside="w2_grouped12")
@@ -274,6 +273,6 @@ def tile_picked_ivfpq_none_p_kernel(tc, x_words, x_scales, w1, w2, dn, qn, offs,
         sum2b = add_dn(part2b, HALF, "sum2b", ahead="part1a")
         finish_half(1, 1, part1b)
         finish_half(2, 0, sum2a)
-        finish_last(0, part3a)
+        finish_last(0)
         finish_half(2, 1, sum2b)
-        finish_last(1, part3b)
+        finish_last(1)

@@ -143,8 +143,8 @@ def tile_picked_ivfpq_none_p_kernel(tc, x_words, x_scales, w1, w2, dn, qn, offs,
         nc.scalar.copy(norm_cols[:], qn_bank[:, : 2 * M_TILES])
         qn_cols = [norm_cols[:, :1], qn_second[:, :1], norm_cols[:, 2:3], norm_cols[:, 3:4]]
 
-        def move_rows(plane, gathered):
-            nc.vector.memset(plane[:].bitcast(I32), 0)
+        def move_rows(plane, gathered, clearing_engine):
+            clearing_engine.memset(plane[:].bitcast(I32), 0)
             for i in range(4):
                 nc.sync.dma_start(
                     out=plane[:].bitcast(I32)[i:P:QUADRANT, :],
@@ -157,7 +157,7 @@ def tile_picked_ivfpq_none_p_kernel(tc, x_words, x_scales, w1, w2, dn, qn, offs,
         cent_bytes = place([P, V], U8, "cent_bytes")
         nc.vector.tensor_copy(cent_bytes[:], scale_table[:].indirect(cent_list[:]))
         cent_plane = place([P, V], U8, "cent_plane")
-        move_rows(cent_plane, cent_bytes)
+        move_rows(cent_plane, cent_bytes, nc.vector)
         offs_bytes = place([P, S], U8, "offs_bytes")
         nc.vector.tensor_copy(offs_bytes[:], scale_table[:].indirect(offs_list[:]))
 
@@ -166,7 +166,7 @@ def tile_picked_ivfpq_none_p_kernel(tc, x_words, x_scales, w1, w2, dn, qn, offs,
         w2_raw0 = load_weight(w2, 0, 1, "w2_raw0", behind="dn_col0")
         w2_raw12 = load_weight(w2, 1, 2, "w2_raw12", ahead="dn_col0")
         offs_plane = place([P, S], U8, "offs_plane", behind="dn_col1")
-        move_rows(offs_plane, offs_bytes)
+        move_rows(offs_plane, offs_bytes, nc.gpsimd)
 
         def gather_words(index_list, j0, j1, name, **where):
             words = place([P, j1 - j0], U32, name, **where)
@@ -178,10 +178,11 @@ def tile_picked_ivfpq_none_p_kernel(tc, x_words, x_scales, w1, w2, dn, qn, offs,
             multiply(bank[:], quantized, cent_words[:, v0:v1], cent_plane[:, v0:v1])
             nc.scalar.activation(c_rows[:, v0:v1], bank[:], IDENTITY, bias=qn_cols[t], scale=-2.0)
 
-        def rests(t, quantized):
-            bank = psum.tile([P, S], F32, name=f"r_bank{t}", tag=f"r_bank{t}")
-            for words, j0 in ((offs_words_a, 0), (offs_words_b, HALF)):
-                multiply(bank[:, j0 : j0 + HALF], quantized, words[:], offs_plane[:, j0 : j0 + HALF])
+        def rests(name, slot, passes):
+            bank = psum.tile([P, S], F32, name=name, tag=slot)
+            for i, (quantized, half) in enumerate(passes):
+                plane = offs_plane[:, half * HALF : (half + 1) * HALF]
+                multiply(bank[:, i * HALF : (i + 1) * HALF], quantized, (offs_words_a, offs_words_b)[half][:], plane)
             return bank
 
         def look_up_add(c_rows, part, j0, j1):
@@ -213,30 +214,31 @@ def tile_picked_ivfpq_none_p_kernel(tc, x_words, x_scales, w1, w2, dn, qn, offs,
         (w1_q3,) = quantize(w1_grouped3, "w1_q3")
         centres(0, w1_q0, c_rows0, 0, HALF, "c_bank0")
         centres(0, w1_q0, c_rows0, HALF, V, "r_bank0")
-        part0 = place([P, S], F32, "part0", first=True)
+        part0 = place([P, S], F32, "part0")
         look_up_add(c_rows0, part0[:], 0, S)
         w2_grouped3 = interleave("scalar", w2_raw3, grouped_tile("w2_grouped3", behind="w1_raw2"))
         c_rows1 = place([P, V], F32, "c_rows1")
         centres(1, w1_q1, c_rows1, 0, V, "c_bank1")
         c_rows2 = place([P, V], F32, "c_rows2")
         centres(2, w1_q2, c_rows2, 0, V, "c_bank2")
-        w2_grouped0 = interleave("scalar", w2_raw0, grouped_tile("w2_grouped0", ahead="qn_second"), 0, P - P // 4)
+        w2_grouped0 = interleave("scalar", w2_raw0, grouped_tile("w2_grouped0", behind="qn_second"), 0, P // 2)
         part2a = place([P, HALF], F32, "part2a")
         look_up(c_rows2, part2a[:], 0, HALF)
         c_rows3 = place([P, V], F32, "c_rows3")
         centres(3, w1_q3, c_rows3, 0, V, "c_bank3")
         (w2_q3,) = quantize(w2_grouped3, "w2_q3")
-        interleave("vector", w2_raw0, w2_grouped0, P - P // 4, P)
-        w2_grouped12 = interleave("vector", w2_raw12, grouped_tile("w2_grouped12", 2, behind="qn_second"))
+        interleave("vector", w2_raw0, w2_grouped0, P // 2, P)
+        w2_grouped12 = interleave("vector", w2_raw12, grouped_tile("w2_grouped12", 2, ahead="qn_second"))
         (w2_q0,) = quantize(w2_grouped0, "w2_q0", first=True)
         w2_q1, w2_q2 = quantize(w2_grouped12, "w2_q12")
-        part1a = place([P, HALF], F32, "part1a", ahead="w2_grouped0")
+        part1a = place([P, HALF], F32, "part1a", behind="w2_grouped0")
         look_up_add(c_rows1, part1a[:], 0, HALF)
         turned_bank = psum.tile([P, S], F32, name="turned_bank", tag="r_bank3")
         for jt in range(M_TILES):
             words = (offs_words_a, offs_words_b)[jt // 2][:, jt % 2 * P : (jt % 2 + 1) * P]
             multiply(turned_bank[:, jt * P : (jt + 1) * P], (words, offs_plane[:, jt * P : (jt + 1) * P]), *w2_q3)
-        r_banks = [rests(t, quantized) for t, quantized in enumerate((w2_q0, w2_q1, w2_q2))]
+        r_bank0 = rests("r_bank0", "r_bank0", ((w2_q0, 0), (w2_q0, 1)))
+        r_halves = [rests(f"r_half{half}", f"r_bank{1 + half}", ((w2_q1, half), (w2_q2, half))) for half in range(2)]
         turned = place([P, S], F32, "turned")
         nc.scalar.activation(turned[:], turned_bank[:], IDENTITY, scale=-2.0)
         part2b = place([P, HALF], F32, "part2b", ahead="w2_q0_codes")
@@ -252,27 +254,34 @@ def tile_picked_ivfpq_none_p_kernel(tc, x_words, x_scales, w1, w2, dn, qn, offs,
                 jt = 2 * half + i
                 nc.tensor.matmul(sum_bank[:, i * P : (i + 1) * P], turned[:, jt * P : (jt + 1) * P], identity[:], start=False, stop=i == 1, is_transpose=True)
             sum_banks.append(sum_bank)
-        part3 = place([P, S], F32, "part3", behind="w2_q0_codes")
-        for j0 in (0, HALF):
-            look_up(c_rows3, part3[:, j0 : j0 + HALF], j0, j0 + HALF)
+        part3a = place([P, HALF], F32, "part3a", behind="w2_q0_codes")
+        look_up(c_rows3, part3a[:], 0, HALF)
 
         def finish_half(t, half, added):
-            columns = slice(half * HALF, (half + 1) * HALF)
-            store(t, columns.start, columns.stop, finish(r_banks[t][:, columns], added[:], f"result{t}_{half}")[:])
+            r_part = r_halves[half][:, (t - 1) * HALF : t * HALF]
+            store(t, half * HALF, (half + 1) * HALF, finish(r_part, added[:], f"result{t}_{half}")[:])
 
-        def finish_last(half):
+        def finish_last(half, part):
             result3 = place([P, HALF], F32, f"result3_{half}")
-            nc.vector.tensor_tensor(result3[:], sum_banks[half][:], part3[:, half * HALF : (half + 1) * HALF], ADD)
+            nc.vector.tensor_tensor(result3[:], sum_banks[half][:], part[:], ADD)
             store(3, half * HALF, (half + 1) * HALF, result3[:])
 
-        sum2a = add_dn(part2a, 0, "sum2a", inside="w2_grouped12")
-        store(0, 0, S, finish(r_banks[0][:], part0[:], "result0", behind="w2_grouped12")[:])
+        sum2a = add_dn(part2a, 0, "sum2a", ahead="w2_grouped12")
+        result0 = place([P, S], F32, "result0", inside="w2_raw12")
+        for j0 in (0, HALF):
+            columns = slice(j0, j0 + HALF)
+            nc.vector.scalar_tensor_tensor(result0[:, columns], r_bank0[:, columns], -2.0, part0[:, columns], MULT, ADD)
+            store(0, j0, j0 + HALF, result0[:, columns])
         finish_half(1, 0, part1a)
-        part1b = place([P, HALF], F32, "part1b", behind="part0")
-        look_up_add(c_rows1, part1b[:], HALF, S)
-        sum2b = add_dn(part2b, HALF, "sum2b", ahead="part1a")
-        finish_half(1, 1, part1b)
         finish_half(2, 0, sum2a)
-        finish_last(0)
-        finish_half(2, 1, sum2b)
-        finish_last(1)
+        part1b = place([P, HALF], F32, "part1b", behind="part1a")
+        look_up_add(c_rows1, part1b[:], HALF, S)
+        sum2b = add_dn(part2b, HALF, "sum2b", behind="sum2a")
+        part3b = place([P, HALF], F32, "part3b", ahead="part1a")
+        look_up(c_rows3, part3b[:], HALF, S)
+        finish_last(0, part3a)
+        finish_half(1, 1, part1b)
+        finish_last(1, part3b)
+        for j0 in (0, QUARTER):
+            r_part = r_halves[1][:, HALF + j0 : HALF + j0 + QUARTER]
+            store(2, HALF + j0, HALF + j0 + QUARTER, finish(r_part, sum2b[:, j0 : j0 + QUARTER], f"result2_{HALF + j0}")[:])

from contextlib import ExitStack

import concourse.mybir as mybir
from concourse.masks import make_identity

K, T, S, V, N = 512, 2048, 512, 512, 512
FLOPS = 2 * K * N * (V + S)

F32 = mybir.dt.float32
BF16 = mybir.dt.bfloat16
I32 = mybir.dt.int32
U32 = mybir.dt.uint32
U16 = mybir.dt.uint16
U8 = mybir.dt.uint8
FP8X4 = mybir.dt.float8_e4m3fn_x4
ADD = mybir.AluOpType.add
MULT = mybir.AluOpType.mult
IDENTITY = mybir.ActivationFunctionType.Identity
COPY = mybir.ActivationFunctionType.Copy

P = 128
PACK = 4
GROUP = 16
BLOCK = 8
QUADRANT = 32
LINE = 4
PAD = 16
M_TILES = N // P
SPARE = 16
HALF = S // 2
QUARTER = S // 4
OVERLAP = 64
LEAD = 4096
CHAIN = 10240
BYTES_OF = {F32: 4, BF16: 2, U32: 4, U8: 1, I32: 4}


def tile_picked_ivfpq_none_p_kernel(tc, x_words, x_scales, w1, w2, dn, qn, offs, cent, own, out):
    nc = tc.nc
    with ExitStack() as ctx:
        keep = ctx.enter_context(tc.tile_pool(name="keep", bufs=1))
        shared = ctx.enter_context(tc.tile_pool(name="shared", bufs=1))
        psum = ctx.enter_context(tc.psum_pool(name="psum", bufs=1))
        spans = {}
        chains = []

        def place(shape, dtype, name, behind=None, ahead=None, inside=None, first=False):
            size = BYTES_OF[dtype]
            for extent in shape[1:]:
                size = size * extent
            if first:
                offset = len(chains) * CHAIN + LEAD
                chains.append(name)
            elif behind:
                offset = spans[behind][1] - OVERLAP
            elif inside:
                offset = spans[inside][0] + OVERLAP
            elif ahead:
                offset = spans[ahead][0] + OVERLAP - size
            else:
                return keep.tile(shape, dtype, name=name, align_bytes=64)
            spans[name] = (offset, offset + size)
            return shared.tile(shape, dtype, name=name, offset=offset, align_bytes=64)

        def load_weight(w, t, tiles, name, **where):
            raw = place([P, PACK, tiles * P], F32, name, **where)
            nc.sync.dma_start(out=raw[:], in_=w[:, t * P : (t + tiles) * P].rearrange("(p j) m -> p j m", j=PACK))
            return raw

        def grouped_tile(name, tiles=1, **where):
            return place([P, tiles * P * PACK], BF16, name, **where)

        def interleave(engine, raw, grouped, m0=0, m1=None):
            m1 = m1 or raw.shape[2]
            target = grouped[:, m0 * PACK : m1 * PACK].rearrange("p (c i j) -> p c j i", i=LINE, j=PACK)
            source = raw[:, :, m0:m1].rearrange("p j (c i) -> p c j i", i=LINE)
            if engine == "vector":
                nc.vector.tensor_copy(target, source)
            else:
                nc.scalar.activation(target, source, COPY)
            return grouped

        def quantize(grouped, name, **where):
            columns = grouped.shape[1] // PACK
            codes = place([P, columns], U32, name + "_codes", **where)
            scales = place([P, columns], U8, name + "_scales")
            nc.vector.quantize_mx(out=codes[:].bitcast(FP8X4), scales=scales[:], in_=grouped[:])
            return [(codes[:, c : c + P], scales[:, c : c + P]) for c in range(0, columns, P)]

        def multiply(bank, quantized, words, plane):
            codes, scales = quantized
            nc.tensor.matmul_mx(
                out=bank,
                lhsT=codes.bitcast(FP8X4),
                lhsT_scale=scales,
                rhs=words.bitcast(FP8X4),
                rhs_scale=plane,
                start=True,
                stop=True,
            )

        def offsets(tile, j0, j1):
            return tile[:, j0 // GROUP : j1 // GROUP]

        cent_list = keep.tile([P, V // GROUP], U16, name="cent_list")
        offs_list = keep.tile([P, S // GROUP], U16, name="offs_list")
        own_list = keep.tile([P, S // GROUP], U16, name="own_list")
        scale_table = place([P, T], U8, "scale_table")
        nc.sync.dma_start(
            out=scale_table[:].bitcast(I32),
            in_=x_scales[0].bitcast(I32).unsqueeze(1).to_broadcast([K // 32, BLOCK, T // 4]),
        )
        nc.sync.dma_start(cent_list[:], cent)
        nc.sync.dma_start(offs_list[:], offs)
        nc.sync.dma_start(own_list[:], own)
        norm_rows = place([P, P], F32, "norm_rows", first=True)
        nc.gpsimd.memset(norm_rows[:], 0.0)
        nc.sync.dma_start(out=norm_rows[:M_TILES, :], in_=qn.rearrange("(t p) o -> t (p o)", p=P))
        nc.sync.dma_start(out=norm_rows[M_TILES : 2 * M_TILES, :], in_=dn[0].rearrange("(t p) -> t p", p=P))
        word_table = place([P, T], I32, "word_table")
        nc.sync.dma_start(out=word_table[:], in_=x_words[0].rearrange("p n t -> p (n t)").bitcast(I32))
        w1_raw0 = load_weight(w1, 0, 1, "w1_raw0", first=True)
        w1_raw1 = load_weight(w1, 1, 1, "w1_raw1", first=True)
        w1_raw2 = load_weight(w1, 2, 1, "w1_raw2", first=True)

        identity = place([P, P], F32, "identity")
        nc.vector.memset(identity[:], 0.0)
        make_identity(nc, identity[:], nomemset=True)
        qn_bank = psum.tile([P, P], F32, name="qn_bank", tag="r_bank3")
        nc.tensor.transpose(qn_bank[:], norm_rows[:], identity[:])
        dn_rows = place([P, S], F32, "dn_rows")
        for half, bank_slot in enumerate(("r_bank1", "r_bank2")):
            dn_bank = psum.tile([P, HALF], F32, name=f"dn_bank{half}", tag=bank_slot)
            for i in range(2):
                jt = 2 * half + i
                dn_col = place([P, 2 * PAD], F32, f"dn_col{jt}", first=jt != 2)
                nc.scalar.copy(dn_col[:, :1], qn_bank[:, M_TILES + jt : M_TILES + jt + 1])
                nc.tensor.transpose(dn_bank[:, i * P : (i + 1) * P], dn_col[:, :1].to_broadcast([P, P]), identity[:])
            nc.scalar.copy(dn_rows[:, half * HALF : (half + 1) * HALF], dn_bank[:])
        qn_second = place([P, 2 * PAD], F32, "qn_second", first=True)
        nc.scalar.copy(qn_second[:, :1], qn_bank[:, 1:2])
        norm_cols = place([P, 2 * M_TILES], F32, "norm_cols")
        nc.scalar.copy(norm_cols[:], qn_bank[:, : 2 * M_TILES])
        qn_cols = [norm_cols[:, :1], qn_second[:, :1], norm_cols[:, 2:3], norm_cols[:, 3:4]]

        def move_rows(plane, gathered, clearing_engine):
            clearing_engine.memset(plane[:].bitcast(I32), 0)
            for i in range(4):
                nc.sync.dma_start(
                    out=plane[:].bitcast(I32)[i:P:QUADRANT, :],
                    in_=gathered[:].bitcast(I32)[BLOCK * i : P : QUADRANT, :],
                )

        c_rows0 = place([P, V + SPARE], F32, "c_rows0")
        nc.vector.memset(c_rows0[:, V:], 0.0)

        cent_bytes = place([P, V], U8, "cent_bytes")
        nc.vector.tensor_copy(cent_bytes[:], scale_table[:].indirect(cent_list[:]))
        cent_plane = place([P, V], U8, "cent_plane")
        move_rows(cent_plane, cent_bytes, nc.vector)
        offs_bytes = place([P, S], U8, "offs_bytes")
        nc.vector.tensor_copy(offs_bytes[:], scale_table[:].indirect(offs_list[:]))

        w1_raw3 = load_weight(w1, 3, 1, "w1_raw3", ahead="norm_rows")
        w2_raw3 = load_weight(w2, 3, 1, "w2_raw3", behind="norm_rows")
        w2_raw0 = load_weight(w2, 0, 1, "w2_raw0", behind="dn_col0")
        w2_raw12 = load_weight(w2, 1, 2, "w2_raw12", ahead="dn_col0")
        offs_plane = place([P, S], U8, "offs_plane", behind="dn_col1")
        move_rows(offs_plane, offs_bytes, nc.gpsimd)

        def gather_words(index_list, j0, j1, name, **where):
            words = place([P, j1 - j0], U32, name, **where)
            nc.vector.tensor_copy(words[:], word_table[:].bitcast(U32).indirect(offsets(index_list, j0, j1)))
            return words

        def centres(t, quantized, c_rows, v0, v1, bank_slot):
            bank = psum.tile([P, v1 - v0], F32, name=f"c_bank{t}_{v0}", tag=bank_slot)
            multiply(bank[:], quantized, cent_words[:, v0:v1], cent_plane[:, v0:v1])
            nc.scalar.activation(c_rows[:, v0:v1], bank[:], IDENTITY, bias=qn_cols[t], scale=-2.0)

        def rests(name, slot, passes):
            bank = psum.tile([P, S], F32, name=name, tag=slot)
            for i, (quantized, half) in enumerate(passes):
                plane = offs_plane[:, half * HALF : (half + 1) * HALF]
                multiply(bank[:, i * HALF : (i + 1) * HALF], quantized, (offs_words_a, offs_words_b)[half][:], plane)
            return bank

        def look_up_add(c_rows, part, j0, j1):
            nc.vector.tensor_tensor(part, c_rows[:].indirect(offsets(own_list, j0, j1)), dn_rows[:, j0:j1], ADD)

        def look_up(c_rows, part, j0, j1):
            nc.scalar.activation(part, c_rows[:].indirect(offsets(own_list, j0, j1)), COPY)

        def add_dn(part, j0, name, **where):
            total = place([P, HALF], F32, name, **where)
            nc.gpsimd.tensor_tensor(total[:], part[:], dn_rows[:, j0 : j0 + HALF], ADD)
            return total

        def finish(r_part, added, name, **where):
            result = place([P, added.shape[1]], F32, name, **where)
            nc.vector.scalar_tensor_tensor(result[:], r_part, -2.0, added, MULT, ADD)
            return result

        def store(t, j0, j1, result):
            nc.sync.dma_start(out=out[t * P : (t + 1) * P, j0:j1], in_=result)

        cent_words = gather_words(cent_list, 0, V, "cent_words")
        (w1_q0,) = quantize(interleave("scalar", w1_raw0, grouped_tile("w1_grouped0", behind="dn_col3")), "w1_q0")
        offs_words_a = gather_words(offs_list, 0, HALF, "offs_words_a", ahead="w1_raw0")
        (w1_q1,) = quantize(interleave("scalar", w1_raw1, grouped_tile("w1_grouped1", ahead="dn_col3")), "w1_q1")
        offs_words_b = gather_words(offs_list, HALF, S, "offs_words_b", ahead="w1_raw1")
        w1_grouped3 = interleave("vector", w1_raw3, grouped_tile("w1_grouped3", behind="w1_raw1"))
        (w1_q2,) = quantize(interleave("scalar", w1_raw2, grouped_tile("w1_grouped2", behind="w1_grouped0")), "w1_q2")
        (w1_q3,) = quantize(w1_grouped3, "w1_q3")
        centres(0, w1_q0, c_rows0, 0, HALF, "c_bank0")
        centres(0, w1_q0, c_rows0, HALF, V, "r_bank0")
        part0 = place([P, S], F32, "part0")
        look_up_add(c_rows0, part0[:], 0, S)
        w2_grouped3 = interleave("scalar", w2_raw3, grouped_tile("w2_grouped3", behind="w1_raw2"))
        c_rows1 = place([P, V], F32, "c_rows1")
        centres(1, w1_q1, c_rows1, 0, V, "c_bank1")
        c_rows2 = place([P, V], F32, "c_rows2")
        centres(2, w1_q2, c_rows2, 0, V, "c_bank2")
        w2_grouped0 = interleave("scalar", w2_raw0, grouped_tile("w2_grouped0", behind="qn_second"), 0, P // 2)
        part2a = place([P, HALF], F32, "part2a")
        look_up(c_rows2, part2a[:], 0, HALF)
        c_rows3 = place([P, V], F32, "c_rows3")
        centres(3, w1_q3, c_rows3, 0, V, "c_bank3")
        (w2_q3,) = quantize(w2_grouped3, "w2_q3")
        interleave("vector", w2_raw0, w2_grouped0, P // 2, P)
        w2_grouped12 = interleave("vector", w2_raw12, grouped_tile("w2_grouped12", 2, ahead="qn_second"))
        (w2_q0,) = quantize(w2_grouped0, "w2_q0", first=True)
        w2_q1, w2_q2 = quantize(w2_grouped12, "w2_q12")
        part1a = place([P, HALF], F32, "part1a", behind="w2_grouped0")
        look_up_add(c_rows1, part1a[:], 0, HALF)
        turned_bank = psum.tile([P, S], F32, name="turned_bank", tag="r_bank3")
        for jt in range(M_TILES):
            words = (offs_words_a, offs_words_b)[jt // 2][:, jt % 2 * P : (jt % 2 + 1) * P]
            multiply(turned_bank[:, jt * P : (jt + 1) * P], (words, offs_plane[:, jt * P : (jt + 1) * P]), *w2_q3)
        r_bank0 = rests("r_bank0", "r_bank0", ((w2_q0, 0), (w2_q0, 1)))
        r_halves = [rests(f"r_half{half}", f"r_bank{1 + half}", ((w2_q1, half), (w2_q2, half))) for half in range(2)]
        turned = place([P, S], F32, "turned")
        nc.scalar.activation(turned[:], turned_bank[:], IDENTITY, scale=-2.0)
        part2b = place([P, HALF], F32, "part2b", ahead="w2_q0_codes")
        look_up(c_rows2, part2b[:], HALF, S)
        sum_banks = []
        for half in range(2):
            sum_bank = psum.tile([P, HALF], F32, name=f"sum_bank{half}", tag=f"c_bank{half}")
            for i in range(2):
                jt = 2 * half + i
                dn_spread = norm_cols[:, M_TILES + jt : M_TILES + jt + 1].to_broadcast([P, P])
                nc.tensor.matmul(sum_bank[:, i * P : (i + 1) * P], dn_spread, identity[:], start=i == 0, stop=False, is_transpose=True)
            for i in range(2):
                jt = 2 * half + i
                nc.tensor.matmul(sum_bank[:, i * P : (i + 1) * P], turned[:, jt * P : (jt + 1) * P], identity[:], start=False, stop=i == 1, is_transpose=True)
            sum_banks.append(sum_bank)
        part3a = place([P, HALF], F32, "part3a", behind="w2_q0_codes")
        look_up(c_rows3, part3a[:], 0, HALF)

        def finish_half(t, half, added):
            r_part = r_halves[half][:, (t - 1) * HALF : t * HALF]
            store(t, half * HALF, (half + 1) * HALF, finish(r_part, added[:], f"result{t}_{half}")[:])

        def finish_last(half, part):
            result3 = place([P, HALF], F32, f"result3_{half}")
            nc.vector.tensor_tensor(result3[:], sum_banks[half][:], part[:], ADD)
            store(3, half * HALF, (half + 1) * HALF, result3[:])

        sum2a = add_dn(part2a, 0, "sum2a", ahead="w2_grouped12")
        result0 = place([P, S], F32, "result0", inside="w2_raw12")
        for j0 in (0, HALF):
            columns = slice(j0, j0 + HALF)
            nc.vector.scalar_tensor_tensor(result0[:, columns], r_bank0[:, columns], -2.0, part0[:, columns], MULT, ADD)
            store(0, j0, j0 + HALF, result0[:, columns])
        finish_half(1, 0, part1a)
        finish_half(2, 0, sum2a)
        part1b = place([P, HALF], F32, "part1b", behind="part1a")
        look_up_add(c_rows1, part1b[:], HALF, S)
        sum2b = add_dn(part2b, HALF, "sum2b", behind="sum2a")
        part3b = place([P, HALF], F32, "part3b", ahead="part1a")
        look_up(c_rows3, part3b[:], HALF, S)
        finish_last(0, part3a)
        finish_half(1, 1, part1b)
        finish_last(1, part3b)
        for j0 in (0, QUARTER):
            r_part = r_halves[1][:, HALF + j0 : HALF + j0 + QUARTER]
            store(2, HALF + j0, HALF + j0 + QUARTER, finish(r_part, sum2b[:, j0 : j0 + QUARTER], f"result2_{HALF + j0}")[:])
